import numpy as np
import ml_dtypes


def mxq(x, axis, fmt="e4m3"):
    dtype, down = {"e4m3": (ml_dtypes.float8_e4m3fn, 7), "e5m2": (ml_dtypes.float8_e5m2, 14)}[fmt]
    v = np.moveaxis(np.asarray(x, np.float32).astype(ml_dtypes.bfloat16).astype(np.float64), axis, -1)
    blocks = v.reshape(v.shape[:-1] + (-1, 32))
    amax = np.abs(blocks).max(-1, keepdims=True)
    byte = np.maximum(np.where(amax > 0, np.frexp(amax)[1] - 1 + 127, 0) - down, 1)
    scale = np.exp2(byte - 127.0)
    codes = (blocks / scale).astype(np.float32).astype(dtype).astype(np.float64)
    return np.moveaxis((codes * scale).reshape(v.shape), -1, axis)


WIDE = False


def mx_kscale(k):
    if not WIDE:
        return np.ones(k)
    levels = np.array([10, -10, 5, -5, 0])
    if k % 512:
        return np.exp2(np.random.permutation(np.resize(levels, k // 32))).repeat(32)
    a = np.empty((k // 512, 16))
    for p in range(k // 512):
        a[p, :8] = np.random.permutation(np.resize(levels, 8))
        for g in range(8):
            far = levels[np.abs(levels - a[p, g]) >= 10]
            a[p, g + 8] = far[np.random.randint(len(far))]
    return np.exp2(a.ravel()).repeat(32)


def f64(x):
    return np.asarray(x).astype(np.float64)


def striped(idx):
    return np.tile(idx.reshape(-1, 16).T, (8, 1)).astype(np.uint16)


def unstriped(offs):
    return offs[:16].T.reshape(-1).astype(np.int64)


E2M1 = np.array([0.0, 0.5, 1.0, 1.5, 2.0, 3.0, 4.0, 6.0, -0.0, -0.5, -1.0, -1.5, -2.0, -3.0, -4.0, -6.0])


def pack_weight(w, fmt):
    k, n = w.shape
    w = f64(np.asarray(w, np.float32).astype(ml_dtypes.bfloat16)).reshape(k // 32, 32, n)
    amax = np.abs(w).max(1)
    if fmt == "e4m3":
        byte = np.frexp(amax)[1] - 1 + 127 - 7
    else:
        mant, ex = np.frexp(amax / 6.0)
        byte = np.where(mant > 0.5, ex, ex - 1) + 127
    byte = np.clip(np.where(amax > 0, byte, 1), 1, 254)
    scaled = (w * np.exp2(127.0 - byte)[:, None, :]).reshape(k, n).astype(np.float32)
    by_word = np.ascontiguousarray(scaled.reshape(k // 512, 128, 4, n).transpose(0, 1, 3, 2))
    if fmt == "e4m3":
        words = by_word.astype(ml_dtypes.float8_e4m3fn).view(np.uint8)
    else:
        c = by_word.astype(ml_dtypes.float4_e2m1fn).view(np.uint8) & 0xF
        words = (c[..., 0::2] | (c[..., 1::2] << 4)).reshape(k // 512, 128, 2 * n)
    return np.ascontiguousarray(words), np.ascontiguousarray(byte.astype(np.uint8).reshape(k // 512, 16, n))


def unpack_weight(words, scales, fmt):
    g, _, n = scales.shape
    words = np.ascontiguousarray(words).reshape(g, 128, n, -1)
    if fmt == "e4m3":
        vals = words.view(ml_dtypes.float8_e4m3fn).astype(np.float64)
    else:
        nib = np.empty((g, 128, n, 4), np.uint8)
        nib[..., 0::2] = words & 0xF
        nib[..., 1::2] = words >> 4
        vals = E2M1[nib]
    vals = vals * np.repeat(np.exp2(scales.astype(np.float64) - 127.0), 8, axis=1)[..., None]
    return vals.transpose(0, 1, 3, 2).reshape(g * 512, n)


def gelu(v):
    return 0.5 * v * (1.0 + np.tanh(np.sqrt(2.0 / np.pi) * (v + 0.044715 * v**3)))


def striped8(idx):
    return np.concatenate([v.reshape(-1, 16).T for v in idx]).astype(np.uint16)


def unstriped8(offs):
    return np.stack([offs[16 * g:16 * g + 16].T.reshape(-1) for g in range(8)]).astype(np.int64)


def put_heads(h, wgs, idx8, t2):
    r = np.arange(h.shape[0])
    page = np.zeros((h.shape[0], t2))
    page[r[:, None], idx8[r % 512 // 64]] = wgs[r // 4 % 128] * h
    return page


K, T, S, H, T2, N = 512, 2048, 1024, 1024, 2048, 384

def setup_inputs():
    n = np.random.standard_normal
    s = mx_kscale(K)[:, None]
    u = mx_kscale(H)[:, None]
    tab_words, tab_scales = pack_weight(n((K, T)) * s, "e4m3")
    w4_words, w4_scales = pack_weight(n((K, H)) / np.sqrt(K) / s, "e2m1")
    w8_words, w8_scales = pack_weight(n((H, N)) / np.sqrt(H) / u, "e4m3")
    return {
        "tab_words": tab_words, "tab_scales": tab_scales,
        "offs": striped(np.random.permutation(T)[:S]),
        "w1": (n((K, H)) / np.sqrt(K) / s).astype(np.float32),
        "w4_words": w4_words, "w4_scales": w4_scales,
        "bg": (0.5 * n(H)).astype(np.float32),
        "wgs": np.repeat(np.random.uniform(0.5, 2.0, (8, S)), 16, axis=0).astype(np.float32),
        "offs2": striped8(np.stack([np.random.permutation(T2)[:S] for _ in range(8)])),
        "amb": (0.5 * n(H)).astype(np.float32),
        "expo": (np.exp(0.3 * n((H, T2))) * u).astype(np.float32),
        "w8_words": w8_words, "w8_scales": w8_scales,
    }

def reference(tab_words, tab_scales, offs, w1, w4_words, w4_scales, bg, wgs, offs2, amb, expo, w8_words, w8_scales):
    v = unpack_weight(tab_words, tab_scales, "e4m3")[:, unstriped(offs)]
    w4 = unpack_weight(w4_words, w4_scales, "e2m1")
    w8 = unpack_weight(w8_words, w8_scales, "e4m3")
    a = mxq(f64(w1), 0, "e4m3").T @ v
    b = w4.T @ v
    h = a / (1.0 + np.exp(-(b + f64(bg)[:, None])))
    page = put_heads(h, f64(wgs), unstriped8(offs2), T2)
    z = (page + f64(amb)[:, None]) * f64(expo)
    out = w8.T @ mxq(z, 0, "e4m3")
    return out

@@ -1,0 +1,255 @@
+from contextlib import ExitStack
+
+import concourse.mybir as mybir
+
+K, T, S, H, T2, N = 512, 2048, 1024, 1024, 2048, 384
+FLOPS = 2 * K * H * S * 2 + 2 * H * N * T2
+
+F32 = mybir.dt.float32
+BF16 = mybir.dt.bfloat16
+I32 = mybir.dt.int32
+U32 = mybir.dt.uint32
+U16 = mybir.dt.uint16
+U8 = mybir.dt.uint8
+FP8X4 = mybir.dt.float8_e4m3fn_x4
+FP4X4 = mybir.dt.float4_e2m1fn_x4
+ACT = mybir.ActivationFunctionType
+MULT = mybir.AluOpType.mult
+
+P = 128
+BANK = 512
+PLANES = 8
+CHUNKS = T2 // BANK
+GP = 256
+
+
+def tile_list_reefer_yard_alarm_kernel(
+    tc, tab_words, tab_scales, offs, w1, w4_words, w4_scales, bg, wgs, offs2, amb, expo, w8_words, w8_scales, out
+):
+    nc = tc.nc
+    with ExitStack() as ctx:
+        keep = ctx.enter_context(tc.tile_pool(name="keep", bufs=1))
+        ring = ctx.enter_context(tc.tile_pool(name="ring", bufs=2))
+        psum = ctx.enter_context(tc.psum_pool(name="psum", bufs=4))
+
+        offs_t = keep.tile([P, S // 16], U16, name="offs_t")
+        offs2_t = keep.tile([P, S // 16], U16, name="offs2_t")
+        tabw = keep.tile([P, T], I32, name="tabw", tag="tab_then_page")
+        tabs = ring.tile([P, T], U8, name="tabs", tag="expo")
+        w4w_raw = ring.tile([P, 2 * H], U8, name="w4w_raw", tag="raw8", align_bytes=64)
+        w4s_raw = ring.tile([P, H], U8, name="w4s_raw", tag="expo")
+        w4w = keep.tile([P, 2 * H], U8, name="w4w", align_bytes=64)
+        w4s = keep.tile([P, H], U8, name="w4s", align_bytes=64)
+        bg_t = keep.tile([P, 2, 4], F32, name="bg_t")
+        amb_t = keep.tile([P, 2, 4], F32, name="amb_t")
+        warm = ring.tile([P, 8], F32, name="warm", tag="raw8", align_bytes=64)
+        warm2 = keep.tile([P, 8], F32, name="warm2", tag="wgs")
+        page0 = keep.tile([P, T2], F32, name="page0")
+
+        nc.vector.memset(tabs[:].bitcast(I32), 0)
+        nc.vector.memset(w4s_raw[:].bitcast(I32), 0)
+        nc.vector.memset(warm[:], 0.0)
+        nc.scalar.activation(warm2[:], warm[:], ACT.Sigmoid)
+        nc.vector.memset(page0[:, 0:1023], 0.0)
+        nc.vector.memset(page0[:, 1023:T2], 0.0)
+
+        nc.sync.dma_start(offs_t[:], offs)
+        nc.sync.dma_start(w4w_raw[:].bitcast(I32), w4_words[0].bitcast(I32))
+        nc.sync.dma_start(tabw[:], tab_words[0].rearrange("p t i -> p (t i)").bitcast(I32))
+        for r in range(4):
+            nc.sync.dma_start(tabs[r:P:32, :].bitcast(I32), tab_scales[0, r:16:4, :].bitcast(I32))
+        for r in range(4):
+            nc.sync.dma_start(w4s_raw[r:P:32, :].bitcast(I32), w4_scales[0, r:16:4, :].bitcast(I32))
+        nc.gpsimd.dma_start(bg_t[:], bg.rearrange("(b p t) -> p b t", b=2, t=4))
+        nc.gpsimd.dma_start(amb_t[:], amb.rearrange("(b p t) -> p b t", b=2, t=4))
+        nc.sync.dma_start(offs2_t[:], offs2)
+        w1raw = {}
+
+        def load_w1(b):
+            w1raw[b] = ring.tile([P, 4, 512], F32, name=f"w1raw{b}", tag="raw8", align_bytes=64)
+            nc.sync.dma_start(w1raw[b][:], w1[:, 512 * b : 512 * (b + 1)].rearrange("(p j) c -> p j c", j=4))
+
+        expo_t = {}
+
+        def load_expo(j):
+            b, u = divmod(j, 2)
+            expo_t[j] = ring.tile([P, 2, T2], F32, name=f"expo{j}", tag="expo")
+            rows = expo[512 * b : 512 * (b + 1), :].rearrange("(p t) m -> p t m", t=4)
+            nc.sync.dma_start(expo_t[j][:], rows[:, 2 * u : 2 * u + 2, :])
+
+        load_w1(0)
+        wgs_t = keep.tile([P, S], F32, name="wgs_t", tag="wgs")
+        nc.sync.dma_start(wgs_t[:], wgs)
+
+        gw = [keep.tile([P, BANK], U32, name=f"gw{h}", align_bytes=64) for h in range(2)]
+        gs = [keep.tile([P, BANK], U8, name=f"gs{h}", align_bytes=64) for h in range(2)]
+
+        def gather(h):
+            lst = offs_t[:, 32 * h : 32 * (h + 1)]
+            nc.vector.tensor_copy(gw[h][:], tabw[:].bitcast(U32).indirect(lst))
+            nc.vector.tensor_copy(gs[h][:], tabs[:].indirect(lst))
+
+        nc.vector.tensor_copy(
+            w4w[:].bitcast(U16).rearrange("p (b t m) -> p b t m", b=2, t=4),
+            w4w_raw[:].bitcast(U16).rearrange("p (b m t) -> p b t m", b=2, t=4),
+        )
+        gather(0)
+        for b in range(2):
+            nc.vector.tensor_copy(
+                w4s[:, 512 * b : 512 * (b + 1)].rearrange("p (t m) -> p t m", t=4),
+                w4s_raw[:, 512 * b : 512 * (b + 1)].rearrange("p (m t) -> p t m", t=4),
+            )
+
+        groups = [(0, 1), (1, 2), (2, 4), (4, 8)]
+        w1q, w1s = {}, {}
+
+        def prepare_w1(k0, k1):
+            b, t0 = divmod(k0, 4)
+            nt = k1 - k0
+            bf = keep.tile([P, nt * 512], BF16, name=f"w1bf{k0}", tag=f"w1bf{k0}", align_bytes=64)
+            q = keep.tile([P, nt * P], U32, name=f"w1q{k0}", align_bytes=64)
+            s = keep.tile([P, nt * P], U8, name=f"w1s{k0}", align_bytes=64)
+            src = w1raw[b][:].rearrange("p j (m t) -> p m t j", t=4)[:, :, t0 : t0 + nt, :]
+            nc.scalar.copy(bf[:].rearrange("p (t m j) -> p m t j", t=nt, j=4), src)
+            nc.vector.quantize_mx(out=q[:].bitcast(FP8X4), scales=s[:], in_=bf[:])
+            for k in range(k0, k1):
+                w1q[k] = q[:, (k - k0) * P : (k - k0 + 1) * P]
+                w1s[k] = s[:, (k - k0) * P : (k - k0 + 1) * P]
+
+        sig = {}
+
+        def gate(k, h):
+            b, t = divmod(k, 4)
+            if h == 0:
+                sig[k] = ring.tile([P, S], F32, name=f"sig{k}", tag="q4", bufs=8, align_bytes=64)
+            acc = psum.tile([P, BANK], F32, name="acc_b", tag="pb")
+            nc.tensor.matmul_mx(
+                out=acc[:],
+                lhsT=w4w[:, 256 * k : 256 * (k + 1)].bitcast(FP4X4),
+                lhsT_scale=w4s[:, P * k : P * (k + 1)],
+                rhs=gw[h][:].bitcast(FP8X4),
+                rhs_scale=gs[h][:],
+                start=True,
+                stop=True,
+            )
+            cols = slice(BANK * h, BANK * (h + 1))
+            nc.scalar.activation(sig[k][:, cols], acc[:], ACT.Sigmoid, bias=bg_t[:, b, t : t + 1])
+            nc.gpsimd.tensor_tensor(sig[k][:, cols], sig[k][:, cols], wgs_t[:, cols], MULT)
+
+        gate(0, 0)
+        prepare_w1(*groups[0])
+        gather(1)
+        load_w1(1)
+        load_expo(0)
+        load_expo(1)
+        gate(0, 1)
+        page1 = keep.tile([P, T2], F32, name="page1", tag="tab_then_page")
+        nc.gpsimd.memset(page1[:], 0.0)
+        pages = [page0, page1]
+        gate(1, 0)
+        gate(1, 1)
+        prepare_w1(*groups[1])
+        prepare_w1(*groups[2])
+        for k in range(2, PLANES):
+            gate(k, 0)
+            gate(k, 1)
+        prepare_w1(*groups[3])
+        w8w = keep.tile([P, 2, N], I32, name="w8w", tag="w1bf2", align_bytes=64)
+        w8s = keep.tile([P, 2, N], U8, name="w8s", tag="w1bf1", align_bytes=64)
+        nc.gpsimd.memset(w8s[:].rearrange("p a c -> p (a c)").bitcast(I32), 0)
+        nc.sync.dma_start(w8w[:], w8_words.rearrange("a p c i -> p a (c i)").bitcast(I32))
+        for r in range(4):
+            nc.sync.dma_start(w8s[r:P:32, :, :].bitcast(I32), w8_scales[:, r:16:4, :].rearrange("a q c -> q a c").bitcast(I32))
+
+        def place(k):
+            hw = ring.tile([P, S], F32, name="hw", tag="hw")
+            for h in range(2):
+                acc = psum.tile([P, BANK], F32, name="acc_a", tag="pa")
+                nc.tensor.matmul_mx(
+                    out=acc[:],
+                    lhsT=w1q[k].bitcast(FP8X4),
+                    lhsT_scale=w1s[k],
+                    rhs=gw[h][:].bitcast(FP8X4),
+                    rhs_scale=gs[h][:],
+                    start=True,
+                    stop=True,
+                )
+                cols = slice(BANK * h, BANK * (h + 1))
+                nc.vector.tensor_tensor(hw[:, cols], acc[:], sig[k][:, cols], MULT)
+                if k == 0:
+                    nc.vector.tensor_copy(pages[0][:].indirect(offs2_t[:, 32 * h : 32 * (h + 1)]), hw[:, cols])
+            if k > 0:
+                nc.vector.tensor_copy(pages[k % 2][:].indirect(offs2_t[:]), hw[:])
+
+        def level(k, dst, cols):
+            b, t = divmod(k, 4)
+            nc.scalar.activation(dst, pages[k % 2][:, cols], ACT.Identity, bias=amb_t[:, b, t : t + 1])
+
+        def expose(eng, dst_words, lev, ex):
+            eng.tensor_tensor(
+                dst_words.bitcast(BF16).rearrange("p (c i t) -> p c t i", i=4, t=2),
+                lev.rearrange("p t (c i) -> p c t i", i=4),
+                ex.rearrange("p t (c i) -> p c t i", i=4),
+                MULT,
+            )
+
+        zq = [keep.tile([P, T2], U32, name=f"zq{b}", align_bytes=64) for b in range(2)]
+        zs = [keep.tile([P, T2], U8, name=f"zs{b}", align_bytes=64) for b in range(2)]
+        zw0 = keep.tile([P, 2, T2], F32, name="zw0")
+        zw1 = []
+        for j in range(3):
+            lev = ring.tile([P, 2, T2], F32, name="lev", tag="lev")
+            for u in range(2):
+                place(2 * j + u)
+                level(2 * j + u, lev[:, u, :], slice(0, T2))
+            for g in range(T2 // GP):
+                cols = slice(GP * g, GP * (g + 1))
+                if j < 2:
+                    dst = zw0[:, j, cols]
+                else:
+                    c, o = divmod(GP * g, BANK)
+                    if o == 0:
+                        zw1.append(ring.tile([P, 2, BANK], F32, name=f"zw1_{c}", tag="q4", bufs=8, align_bytes=64))
+                    dst = zw1[c][:, 0, o : o + GP]
+                expose(nc.gpsimd, dst, lev[:, :, cols], expo_t[j][:, :, cols])
+            if j < 2:
+                load_expo(j + 2)
+            if j == 1:
+                for half in range(2):
+                    cols = slice(1024 * half, 1024 * (half + 1))
+                    zb = ring.tile([P, 1024, 2], F32, name="zb0", tag="raw8", align_bytes=64)
+                    nc.scalar.copy(zb[:], zw0[:, :, cols].rearrange("p u m -> p m u"))
+                    nc.vector.quantize_mx(
+                        out=zq[0][:, cols].bitcast(FP8X4), scales=zs[0][:, cols], in_=zb[:].rearrange("p m u -> p (m u)").bitcast(BF16)
+                    )
+
+        place(6)
+        levs = [ring.tile([P, 2, BANK], F32, name=f"lev3_{c}", tag="q4", bufs=8, align_bytes=64) for c in range(CHUNKS)]
+        for c in range(CHUNKS):
+            level(6, levs[c][:, 0, :], slice(BANK * c, BANK * (c + 1)))
+        place(7)
+        for c in range(CHUNKS):
+            level(7, levs[c][:, 1, :], slice(BANK * c, BANK * (c + 1)))
+        for c in range(CHUNKS):
+            cols = slice(BANK * c, BANK * (c + 1))
+            expose(nc.vector, zw1[c][:, 1, :], levs[c][:], expo_t[3][:, :, cols])
+            zb = ring.tile([P, BANK, 2], F32, name="zb1", tag="zb1", align_bytes=64)
+            nc.vector.tensor_copy(zb[:], zw1[c][:].rearrange("p u m -> p m u"))
+            nc.vector.quantize_mx(
+                out=zq[1][:, cols].bitcast(FP8X4), scales=zs[1][:, cols], in_=zb[:].rearrange("p m u -> p (m u)").bitcast(BF16)
+            )
+            for nb in range(N // P):
+                acc = psum.tile([P, BANK], F32, name="acc_o", tag=("pa", "pb")[(3 * c + nb) % 2])
+                for b in range(2):
+                    nc.tensor.matmul_mx(
+                        out=acc[:],
+                        lhsT=w8w[:, b, P * nb : P * (nb + 1)].bitcast(FP8X4),
+                        lhsT_scale=w8s[:, b, P * nb : P * (nb + 1)],
+                        rhs=zq[b][:, cols].bitcast(FP8X4),
+                        rhs_scale=zs[b][:, cols],
+                        start=(b == 0),
+                        stop=(b == 1),
+                    )
+                res = ring.tile([P, BANK], F32, name="res", tag="res", bufs=6)
+                nc.scalar.copy(res[:], acc[:])
+                nc.sync.dma_start(out[P * nb : P * (nb + 1), cols], res[:])

@@ -18,9 +18,7 @@ MULT = mybir.AluOpType.mult
 
 P = 128
 BANK = 512
-PLANES = 8
 CHUNKS = T2 // BANK
-GP = 256
 
 
 def tile_list_reefer_yard_alarm_kernel(
@@ -34,39 +32,38 @@ def tile_list_reefer_yard_alarm_kernel(
 
         offs_t = keep.tile([P, S // 16], U16, name="offs_t")
         offs2_t = keep.tile([P, S // 16], U16, name="offs2_t")
-        tabw = keep.tile([P, T], I32, name="tabw", tag="tab_then_page")
-        tabs = ring.tile([P, T], U8, name="tabs", tag="expo")
-        w4w_raw = ring.tile([P, 2 * H], U8, name="w4w_raw", tag="raw8", align_bytes=64)
+        warm = ring.tile([P, 8], F32, name="warm", tag="raw8")
+        tabs = ring.tile([P, T], U8, name="tabs", tag="raw8")
         w4s_raw = ring.tile([P, H], U8, name="w4s_raw", tag="expo")
+        tabw = ring.tile([P, T], I32, name="tabw", tag="expo")
+        w4w_raw = keep.tile([P, 2 * H], U8, name="w4w_raw", tag="page1")
         w4w = keep.tile([P, 2 * H], U8, name="w4w", align_bytes=64)
         w4s = keep.tile([P, H], U8, name="w4s", align_bytes=64)
         bg_t = keep.tile([P, 2, 4], F32, name="bg_t")
         amb_t = keep.tile([P, 2, 4], F32, name="amb_t")
-        warm = ring.tile([P, 8], F32, name="warm", tag="raw8", align_bytes=64)
         warm2 = keep.tile([P, 8], F32, name="warm2", tag="wgs")
         page0 = keep.tile([P, T2], F32, name="page0")
 
         nc.vector.memset(tabs[:].bitcast(I32), 0)
         nc.vector.memset(w4s_raw[:].bitcast(I32), 0)
         nc.vector.memset(warm[:], 0.0)
-        nc.scalar.activation(warm2[:], warm[:], ACT.Sigmoid)
-        nc.vector.memset(page0[:, 0:1023], 0.0)
-        nc.vector.memset(page0[:, 1023:T2], 0.0)
+        nc.vector.memset(page0[:], 0.0)
 
         nc.sync.dma_start(offs_t[:], offs)
         nc.sync.dma_start(w4w_raw[:].bitcast(I32), w4_words[0].bitcast(I32))
         nc.sync.dma_start(tabw[:], tab_words[0].rearrange("p t i -> p (t i)").bitcast(I32))
+        nc.sync.dma_start(offs2_t[:], offs2)
         for r in range(4):
-            nc.sync.dma_start(tabs[r:P:32, :].bitcast(I32), tab_scales[0, r:16:4, :].bitcast(I32))
+            nc.scalar.dma_start(tabs[r:P:32, :].bitcast(I32), tab_scales[0, r:16:4, :].bitcast(I32))
         for r in range(4):
             nc.sync.dma_start(w4s_raw[r:P:32, :].bitcast(I32), w4_scales[0, r:16:4, :].bitcast(I32))
+        nc.scalar.activation(warm2[:], warm[:], ACT.Sigmoid)
         nc.gpsimd.dma_start(bg_t[:], bg.rearrange("(b p t) -> p b t", b=2, t=4))
         nc.gpsimd.dma_start(amb_t[:], amb.rearrange("(b p t) -> p b t", b=2, t=4))
-        nc.sync.dma_start(offs2_t[:], offs2)
         w1raw = {}
 
         def load_w1(b):
-            w1raw[b] = ring.tile([P, 4, 512], F32, name=f"w1raw{b}", tag="raw8", align_bytes=64)
+            w1raw[b] = ring.tile([P, 4, 512], F32, name=f"w1raw{b}", tag="raw8")
             nc.sync.dma_start(w1raw[b][:], w1[:, 512 * b : 512 * (b + 1)].rearrange("(p j) c -> p j c", j=4))
 
         expo_t = {}
@@ -83,45 +80,49 @@ def tile_list_reefer_yard_alarm_kernel(
 
         gw = [keep.tile([P, BANK], U32, name=f"gw{h}", align_bytes=64) for h in range(2)]
         gs = [keep.tile([P, BANK], U8, name=f"gs{h}", align_bytes=64) for h in range(2)]
-
-        def gather(h):
-            lst = offs_t[:, 32 * h : 32 * (h + 1)]
-            nc.vector.tensor_copy(gw[h][:], tabw[:].bitcast(U32).indirect(lst))
-            nc.vector.tensor_copy(gs[h][:], tabs[:].indirect(lst))
+        halves = [slice(BANK * h, BANK * (h + 1)) for h in range(2)]
+        lists = [offs_t[:, 32 * h : 32 * (h + 1)] for h in range(2)]
 
         nc.vector.tensor_copy(
             w4w[:].bitcast(U16).rearrange("p (b t m) -> p b t m", b=2, t=4),
             w4w_raw[:].bitcast(U16).rearrange("p (b m t) -> p b t m", b=2, t=4),
         )
-        gather(0)
-        for b in range(2):
-            nc.vector.tensor_copy(
-                w4s[:, 512 * b : 512 * (b + 1)].rearrange("p (t m) -> p t m", t=4),
-                w4s_raw[:, 512 * b : 512 * (b + 1)].rearrange("p (m t) -> p t m", t=4),
-            )
+        page1 = keep.tile([P, T2], F32, name="page1", tag="page1")
+        nc.gpsimd.memset(page1[:], 0.0)
+        pages = [page0, page1]
+        nc.vector.tensor_copy(gs[0][:], tabs[:].indirect(lists[0]))
+        nc.vector.tensor_copy(gw[0][:], tabw[:].bitcast(U32).indirect(lists[0]))
+        nc.vector.tensor_copy(
+            w4s[:].rearrange("p (b t m) -> p b t m", b=2, t=4),
+            w4s_raw[:].rearrange("p (b m t) -> p b t m", b=2, t=4),
+        )
+        nc.vector.tensor_copy(gs[1][:], tabs[:].indirect(lists[1]))
+        nc.vector.tensor_copy(gw[1][:], tabw[:].bitcast(U32).indirect(lists[1]))
+        load_w1(1)
+        load_expo(0)
+        load_expo(1)
 
-        groups = [(0, 1), (1, 2), (2, 4), (4, 8)]
         w1q, w1s = {}, {}
 
-        def prepare_w1(k0, k1):
+        def prepare_w1(k0, k1, cast):
             b, t0 = divmod(k0, 4)
             nt = k1 - k0
             bf = keep.tile([P, nt * 512], BF16, name=f"w1bf{k0}", tag=f"w1bf{k0}", align_bytes=64)
             q = keep.tile([P, nt * P], U32, name=f"w1q{k0}", align_bytes=64)
             s = keep.tile([P, nt * P], U8, name=f"w1s{k0}", align_bytes=64)
             src = w1raw[b][:].rearrange("p j (m t) -> p m t j", t=4)[:, :, t0 : t0 + nt, :]
-            nc.scalar.copy(bf[:].rearrange("p (t m j) -> p m t j", t=nt, j=4), src)
+            cast(bf[:].rearrange("p (t m j) -> p m t j", t=nt, j=4), src)
             nc.vector.quantize_mx(out=q[:].bitcast(FP8X4), scales=s[:], in_=bf[:])
             for k in range(k0, k1):
                 w1q[k] = q[:, (k - k0) * P : (k - k0 + 1) * P]
                 w1s[k] = s[:, (k - k0) * P : (k - k0 + 1) * P]
 
-        sig = {}
+        val = {}
 
-        def gate(k, h):
+        def trust(k, h):
             b, t = divmod(k, 4)
             if h == 0:
-                sig[k] = ring.tile([P, S], F32, name=f"sig{k}", tag="q4", bufs=8, align_bytes=64)
+                val[k] = ring.tile([P, S], F32, name=f"val{k}", tag="q4", bufs=9, align_bytes=64)
             acc = psum.tile([P, BANK], F32, name="acc_b", tag="pb")
             nc.tensor.matmul_mx(
                 out=acc[:],
@@ -132,54 +133,40 @@ def tile_list_reefer_yard_alarm_kernel(
                 start=True,
                 stop=True,
             )
-            cols = slice(BANK * h, BANK * (h + 1))
-            nc.scalar.activation(sig[k][:, cols], acc[:], ACT.Sigmoid, bias=bg_t[:, b, t : t + 1])
-            nc.gpsimd.tensor_tensor(sig[k][:, cols], sig[k][:, cols], wgs_t[:, cols], MULT)
+            nc.scalar.activation(val[k][:, halves[h]], acc[:], ACT.Sigmoid, bias=bg_t[:, b, t : t + 1])
 
-        gate(0, 0)
-        prepare_w1(*groups[0])
-        gather(1)
-        load_w1(1)
-        load_expo(0)
-        load_expo(1)
-        gate(0, 1)
-        page1 = keep.tile([P, T2], F32, name="page1", tag="tab_then_page")
-        nc.gpsimd.memset(page1[:], 0.0)
-        pages = [page0, page1]
-        gate(1, 0)
-        gate(1, 1)
-        prepare_w1(*groups[1])
-        prepare_w1(*groups[2])
-        for k in range(2, PLANES):
-            gate(k, 0)
-            gate(k, 1)
-        prepare_w1(*groups[3])
-        w8w = keep.tile([P, 2, N], I32, name="w8w", tag="w1bf2", align_bytes=64)
-        w8s = keep.tile([P, 2, N], U8, name="w8s", tag="w1bf1", align_bytes=64)
-        nc.gpsimd.memset(w8s[:].rearrange("p a c -> p (a c)").bitcast(I32), 0)
-        nc.sync.dma_start(w8w[:], w8_words.rearrange("a p c i -> p a (c i)").bitcast(I32))
-        for r in range(4):
-            nc.sync.dma_start(w8s[r:P:32, :, :].bitcast(I32), w8_scales[:, r:16:4, :].rearrange("a q c -> q a c").bitcast(I32))
+        def deviation(k, h):
+            acc = psum.tile([P, BANK], F32, name="acc_a", tag="pa")
+            nc.tensor.matmul_mx(
+                out=acc[:],
+                lhsT=w1q[k].bitcast(FP8X4),
+                lhsT_scale=w1s[k],
+                rhs=gw[h][:].bitcast(FP8X4),
+                rhs_scale=gs[h][:],
+                start=True,
+                stop=True,
+            )
+            return acc
+
+        def weigh(eng, k, cols):
+            eng.tensor_tensor(val[k][:, cols], val[k][:, cols], wgs_t[:, cols], MULT)
+
+        def gate(k):
+            trust(k, 0)
+            trust(k, 1)
+            weigh(nc.gpsimd, k, slice(0, S))
+
+        def times_a_on_vector(k, h):
+            nc.vector.tensor_tensor(val[k][:, halves[h]], deviation(k, h)[:], val[k][:, halves[h]], MULT)
+
+        def times_a_on_gpsimd(k):
+            a_sb = ring.tile([P, S], F32, name="a_sb", tag="a_sb", bufs=3)
+            for h in range(2):
+                nc.scalar.copy(a_sb[:, halves[h]], deviation(k, h)[:])
+            nc.gpsimd.tensor_tensor(val[k][:], val[k][:], a_sb[:], MULT)
 
         def place(k):
-            hw = ring.tile([P, S], F32, name="hw", tag="hw")
-            for h in range(2):
-                acc = psum.tile([P, BANK], F32, name="acc_a", tag="pa")
-                nc.tensor.matmul_mx(
-                    out=acc[:],
-                    lhsT=w1q[k].bitcast(FP8X4),
-                    lhsT_scale=w1s[k],
-                    rhs=gw[h][:].bitcast(FP8X4),
-                    rhs_scale=gs[h][:],
-                    start=True,
-                    stop=True,
-                )
-                cols = slice(BANK * h, BANK * (h + 1))
-                nc.vector.tensor_tensor(hw[:, cols], acc[:], sig[k][:, cols], MULT)
-                if k == 0:
-                    nc.vector.tensor_copy(pages[0][:].indirect(offs2_t[:, 32 * h : 32 * (h + 1)]), hw[:, cols])
-            if k > 0:
-                nc.vector.tensor_copy(pages[k % 2][:].indirect(offs2_t[:]), hw[:])
+            nc.vector.tensor_copy(pages[k % 2][:].indirect(offs2_t[:]), val[k][:])
 
         def level(k, dst, cols):
             b, t = divmod(k, 4)
@@ -197,52 +184,105 @@ def tile_list_reefer_yard_alarm_kernel(
         zs = [keep.tile([P, T2], U8, name=f"zs{b}", align_bytes=64) for b in range(2)]
         zw0 = keep.tile([P, 2, T2], F32, name="zw0")
         zw1 = []
-        for j in range(3):
-            lev = ring.tile([P, 2, T2], F32, name="lev", tag="lev")
-            for u in range(2):
-                place(2 * j + u)
-                level(2 * j + u, lev[:, u, :], slice(0, T2))
-            for g in range(T2 // GP):
-                cols = slice(GP * g, GP * (g + 1))
+        lev = {}
+
+        def level_whole(k):
+            j, u = divmod(k, 2)
+            if u == 0:
+                lev[j] = ring.tile([P, 2, T2], F32, name=f"lev{j}", tag="lev", align_bytes=64)
+            level(k, lev[j][:, u, :], slice(0, T2))
+
+        def expose_pair(j):
+            for c in range(CHUNKS):
+                cols = slice(BANK * c, BANK * (c + 1))
                 if j < 2:
                     dst = zw0[:, j, cols]
                 else:
-                    c, o = divmod(GP * g, BANK)
-                    if o == 0:
-                        zw1.append(ring.tile([P, 2, BANK], F32, name=f"zw1_{c}", tag="q4", bufs=8, align_bytes=64))
-                    dst = zw1[c][:, 0, o : o + GP]
-                expose(nc.gpsimd, dst, lev[:, :, cols], expo_t[j][:, :, cols])
+                    zw1.append(ring.tile([P, 2, BANK], F32, name=f"zw1_{c}", tag="q4", bufs=9, align_bytes=64))
+                    dst = zw1[c][:, 0, :]
+                expose(nc.gpsimd, dst, lev[j][:, :, cols], expo_t[j][:, :, cols])
             if j < 2:
                 load_expo(j + 2)
-            if j == 1:
-                for half in range(2):
-                    cols = slice(1024 * half, 1024 * (half + 1))
-                    zb = ring.tile([P, 1024, 2], F32, name="zb0", tag="raw8", align_bytes=64)
-                    nc.scalar.copy(zb[:], zw0[:, :, cols].rearrange("p u m -> p m u"))
-                    nc.vector.quantize_mx(
-                        out=zq[0][:, cols].bitcast(FP8X4), scales=zs[0][:, cols], in_=zb[:].rearrange("p m u -> p (m u)").bitcast(BF16)
-                    )
 
-        place(6)
-        levs = [ring.tile([P, 2, BANK], F32, name=f"lev3_{c}", tag="q4", bufs=8, align_bytes=64) for c in range(CHUNKS)]
-        for c in range(CHUNKS):
-            level(6, levs[c][:, 0, :], slice(BANK * c, BANK * (c + 1)))
-        place(7)
-        for c in range(CHUNKS):
-            level(7, levs[c][:, 1, :], slice(BANK * c, BANK * (c + 1)))
+        trust(0, 0)
+        prepare_w1(0, 2, nc.vector.tensor_copy)
+        prepare_w1(2, 4, nc.scalar.copy)
+        trust(0, 1)
+        for h in range(2):
+            weigh((nc.vector, nc.gpsimd)[h], 0, halves[h])
+            times_a_on_vector(0, h)
+            nc.vector.tensor_copy(page0[:].indirect(offs2_t[:, 32 * h : 32 * (h + 1)]), val[0][:, halves[h]])
+        gate(1)
+        gate(2)
+        times_a_on_gpsimd(2)
+        prepare_w1(4, 8, nc.scalar.copy)
+        w8w = keep.tile([P, 2, N], I32, name="w8w", tag="w1bf4", align_bytes=64)
+        w8s = keep.tile([P, 2, N], U8, name="w8s", tag="w1bf0", align_bytes=64)
+        nc.vector.memset(w8s[:].rearrange("p a c -> p (a c)").bitcast(I32), 0)
+        for r in range(4):
+            nc.sync.dma_start(w8s[r:P:32, :, :].bitcast(I32), w8_scales[:, r:16:4, :].rearrange("a q c -> q a c").bitcast(I32))
+        nc.sync.dma_start(w8w[:], w8_words.rearrange("a p c i -> p a (c i)").bitcast(I32))
+        gate(3)
+        times_a_on_gpsimd(3)
+        level_whole(0)
+        for h in range(2):
+            times_a_on_vector(1, h)
+        place(1)
+        gate(4)
+        gate(5)
+        times_a_on_gpsimd(4)
+        level_whole(1)
+        place(2)
+        expose_pair(0)
+        times_a_on_gpsimd(5)
+        gate(6)
+        trust(7, 0)
+        trust(7, 1)
+        level_whole(2)
+        place(3)
+        level_whole(3)
+        place(4)
+        expose_pair(1)
+        weigh(nc.gpsimd, 7, slice(0, S))
+        level_whole(4)
+        place(5)
+        level_whole(5)
+        expose_pair(2)
+        zb0 = ring.tile([P, T2, 2], F32, name="zb0", tag="lev", align_bytes=64)
         for c in range(CHUNKS):
             cols = slice(BANK * c, BANK * (c + 1))
-            expose(nc.vector, zw1[c][:, 1, :], levs[c][:], expo_t[3][:, :, cols])
-            zb = ring.tile([P, BANK, 2], F32, name="zb1", tag="zb1", align_bytes=64)
-            nc.vector.tensor_copy(zb[:], zw1[c][:].rearrange("p u m -> p m u"))
+            nc.scalar.copy(zb0[:, cols, :], zw0[:, :, cols].rearrange("p u m -> p m u"))
+
+        levs = []
+        for k in (6, 7):
+            for h in range(2):
+                times_a_on_vector(k, h)
+            place(k)
+            for c in range(CHUNKS):
+                if k == 6:
+                    levs.append(ring.tile([P, 2, BANK], F32, name=f"lev3_{c}", tag="q4", bufs=9, align_bytes=64))
+                level(k, levs[c][:, k - 6, :], slice(BANK * c, BANK * (c + 1)))
+
+        def quantise(b, cols, words):
             nc.vector.quantize_mx(
-                out=zq[1][:, cols].bitcast(FP8X4), scales=zs[1][:, cols], in_=zb[:].rearrange("p m u -> p (m u)").bitcast(BF16)
+                out=zq[b][:, cols].bitcast(FP8X4), scales=zs[b][:, cols], in_=words.rearrange("p m u -> p (m u)").bitcast(BF16)
             )
-            for nb in range(N // P):
-                acc = psum.tile([P, BANK], F32, name="acc_o", tag=("pa", "pb")[(3 * c + nb) % 2])
-                for b in range(2):
+
+        pieces = [(0, 512), (512, 512), (1024, 512), (1536, 256), (1792, 256)]
+        for i, (m0, width) in enumerate(pieces):
+            cols = slice(m0, m0 + width)
+            c, o = divmod(m0, BANK)
+            part = slice(o, o + width)
+            quantise(0, cols, zb0[:, cols, :])
+            expose(nc.vector, zw1[c][:, 1, part], levs[c][:, :, part], expo_t[3][:, :, cols])
+            zb = ring.tile([P, width, 2], F32, name="zb1", tag="zb1", align_bytes=64)
+            nc.vector.tensor_copy(zb[:], zw1[c][:, :, part].rearrange("p u m -> p m u"))
+            quantise(1, cols, zb[:])
+            accs = [psum.tile([P, width], F32, name="acc_o", tag=("pa", "pb")[(3 * i + nb) % 2]) for nb in range(N // P)]
+            for b in range(2):
+                for nb in range(N // P):
                     nc.tensor.matmul_mx(
-                        out=acc[:],
+                        out=accs[nb][:],
                         lhsT=w8w[:, b, P * nb : P * (nb + 1)].bitcast(FP8X4),
                         lhsT_scale=w8s[:, b, P * nb : P * (nb + 1)],
                         rhs=zq[b][:, cols].bitcast(FP8X4),
@@ -250,6 +290,10 @@ def tile_list_reefer_yard_alarm_kernel(
                         start=(b == 0),
                         stop=(b == 1),
                     )
-                res = ring.tile([P, BANK], F32, name="res", tag="res", bufs=6)
-                nc.scalar.copy(res[:], acc[:])
+            for nb in range(N // P):
+                res = ring.tile([P, width], F32, name="res", tag="res", bufs=6)
+                if i == len(pieces) - 1 and nb == 1:
+                    nc.vector.tensor_copy(res[:], accs[nb][:])
+                else:
+                    nc.scalar.copy(res[:], accs[nb][:])
                 nc.sync.dma_start(out[P * nb : P * (nb + 1), cols], res[:])

@@ -18,6 +18,7 @@ MULT = mybir.AluOpType.mult
 
 P = 128
 BANK = 512
+SW = (0, 1)
 CHUNKS = T2 // BANK
 
 
@@ -28,102 +29,108 @@ def tile_list_reefer_yard_alarm_kernel(
     with ExitStack() as ctx:
         keep = ctx.enter_context(tc.tile_pool(name="keep", bufs=1))
         ring = ctx.enter_context(tc.tile_pool(name="ring", bufs=2))
-        psum = ctx.enter_context(tc.psum_pool(name="psum", bufs=4))
+        psum = ctx.enter_context(tc.psum_pool(name="psum", bufs=5))
 
         offs_t = keep.tile([P, S // 16], U16, name="offs_t")
         offs2_t = keep.tile([P, S // 16], U16, name="offs2_t")
-        warm = ring.tile([P, 8], F32, name="warm", tag="raw8")
-        tabs = ring.tile([P, T], U8, name="tabs", tag="raw8")
-        w4s_raw = ring.tile([P, H], U8, name="w4s_raw", tag="expo")
-        tabw = ring.tile([P, T], I32, name="tabw", tag="expo")
-        w4w_raw = keep.tile([P, 2 * H], U8, name="w4w_raw", tag="page1")
+        warm = keep.tile([P, 8], F32, name="warm")
+        tabs = keep.tile([P, T], U8, name="tabs", tag="raw1", align_bytes=64)
+        w4s_raw = keep.tile([P, H], U8, name="w4s_raw", tag="page1")
+        tabw = keep.tile([P, T], I32, name="tabw", tag="expo0")
+        w4w_raw = [keep.tile([P, H], U8, name=f"w4w_raw{b}", tag=("raw0", "wgs")[b], align_bytes=64) for b in range(2)]
         w4w = keep.tile([P, 2 * H], U8, name="w4w", align_bytes=64)
         w4s = keep.tile([P, H], U8, name="w4s", align_bytes=64)
         bg_t = keep.tile([P, 2, 4], F32, name="bg_t")
         amb_t = keep.tile([P, 2, 4], F32, name="amb_t")
-        warm2 = keep.tile([P, 8], F32, name="warm2", tag="wgs")
+        warm2 = keep.tile([P, 8], F32, name="warm2")
         page0 = keep.tile([P, T2], F32, name="page0")
 
         nc.vector.memset(tabs[:].bitcast(I32), 0)
         nc.vector.memset(w4s_raw[:].bitcast(I32), 0)
         nc.vector.memset(warm[:], 0.0)
         nc.vector.memset(page0[:], 0.0)
+        w8s = keep.tile([P, 2, N], U8, name="w8s", align_bytes=64)
+        nc.vector.memset(w8s[:].rearrange("p a c -> p (a c)").bitcast(I32), 0)
 
         nc.sync.dma_start(offs_t[:], offs)
-        nc.sync.dma_start(w4w_raw[:].bitcast(I32), w4_words[0].bitcast(I32))
+        for b in range(2):
+            nc.sync.dma_start(w4w_raw[b][:].bitcast(I32), w4_words[0, :, H * b : H * (b + 1)].bitcast(I32))
         nc.sync.dma_start(tabw[:], tab_words[0].rearrange("p t i -> p (t i)").bitcast(I32))
         nc.sync.dma_start(offs2_t[:], offs2)
         for r in range(4):
             nc.scalar.dma_start(tabs[r:P:32, :].bitcast(I32), tab_scales[0, r:16:4, :].bitcast(I32))
         for r in range(4):
-            nc.sync.dma_start(w4s_raw[r:P:32, :].bitcast(I32), w4_scales[0, r:16:4, :].bitcast(I32))
+            nc.scalar.dma_start(w4s_raw[r:P:32, :].bitcast(I32), w4_scales[0, r:16:4, :].bitcast(I32))
         nc.scalar.activation(warm2[:], warm[:], ACT.Sigmoid)
         nc.gpsimd.dma_start(bg_t[:], bg.rearrange("(b p t) -> p b t", b=2, t=4))
         nc.gpsimd.dma_start(amb_t[:], amb.rearrange("(b p t) -> p b t", b=2, t=4))
+        for r in range(4):
+            nc.gpsimd.dma_start(w8s[r:P:32, :, :].bitcast(I32), w8_scales[:, r:16:4, :].rearrange("a q c -> q a c").bitcast(I32))
         w1raw = {}
 
         def load_w1(b):
-            w1raw[b] = ring.tile([P, 4, 512], F32, name=f"w1raw{b}", tag="raw8")
+            w1raw[b] = keep.tile([P, 4, 512], F32, name=f"w1raw{b}", tag=f"raw{b}", align_bytes=64)
             nc.sync.dma_start(w1raw[b][:], w1[:, 512 * b : 512 * (b + 1)].rearrange("(p j) c -> p j c", j=4))
 
         expo_t = {}
 
         def load_expo(j):
             b, u = divmod(j, 2)
-            expo_t[j] = ring.tile([P, 2, T2], F32, name=f"expo{j}", tag="expo")
+            expo_t[j] = keep.tile([P, 2, T2], F32, name=f"expo{j}", tag=("expo0", "raw0")[j % 2], align_bytes=(None, 64)[j % 2])
             rows = expo[512 * b : 512 * (b + 1), :].rearrange("(p t) m -> p t m", t=4)
             nc.sync.dma_start(expo_t[j][:], rows[:, 2 * u : 2 * u + 2, :])
 
-        load_w1(0)
-        wgs_t = keep.tile([P, S], F32, name="wgs_t", tag="wgs")
-        nc.sync.dma_start(wgs_t[:], wgs)
 
         gw = [keep.tile([P, BANK], U32, name=f"gw{h}", align_bytes=64) for h in range(2)]
-        gs = [keep.tile([P, BANK], U8, name=f"gs{h}", align_bytes=64) for h in range(2)]
+        gs = [keep.tile([P, BANK], U8, name="gs0", align_bytes=64)]
         halves = [slice(BANK * h, BANK * (h + 1)) for h in range(2)]
         lists = [offs_t[:, 32 * h : 32 * (h + 1)] for h in range(2)]
 
-        nc.vector.tensor_copy(
-            w4w[:].bitcast(U16).rearrange("p (b t m) -> p b t m", b=2, t=4),
-            w4w_raw[:].bitcast(U16).rearrange("p (b m t) -> p b t m", b=2, t=4),
-        )
-        page1 = keep.tile([P, T2], F32, name="page1", tag="page1")
-        nc.gpsimd.memset(page1[:], 0.0)
-        pages = [page0, page1]
+        for b in range(2):
+            nc.vector.tensor_copy(
+                w4w[:, H * b : H * (b + 1)].bitcast(U16).rearrange("p (t m) -> p t m", t=4),
+                w4w_raw[b][:].bitcast(U16).rearrange("p (m t) -> p t m", t=4),
+            )
+        load_w1(0)
+        wgs_t = keep.tile([P, S], F32, name="wgs_t", tag="wgs", align_bytes=64)
+        nc.sync.dma_start(wgs_t[:], wgs)
         nc.vector.tensor_copy(gs[0][:], tabs[:].indirect(lists[0]))
         nc.vector.tensor_copy(gw[0][:], tabw[:].bitcast(U32).indirect(lists[0]))
         nc.vector.tensor_copy(
             w4s[:].rearrange("p (b t m) -> p b t m", b=2, t=4),
             w4s_raw[:].rearrange("p (b m t) -> p b t m", b=2, t=4),
         )
+        gs.append(keep.tile([P, BANK], U8, name="gs1", align_bytes=64))
         nc.vector.tensor_copy(gs[1][:], tabs[:].indirect(lists[1]))
         nc.vector.tensor_copy(gw[1][:], tabw[:].bitcast(U32).indirect(lists[1]))
         load_w1(1)
-        load_expo(0)
-        load_expo(1)
+        page1 = keep.tile([P, T2], F32, name="page1", tag="page1")
+        nc.gpsimd.memset(page1[:], 0.0)
+        pages = [page0, page1]
 
         w1q, w1s = {}, {}
 
-        def prepare_w1(k0, k1, cast):
-            b, t0 = divmod(k0, 4)
-            nt = k1 - k0
-            bf = keep.tile([P, nt * 512], BF16, name=f"w1bf{k0}", tag=f"w1bf{k0}", align_bytes=64)
-            q = keep.tile([P, nt * P], U32, name=f"w1q{k0}", align_bytes=64)
-            s = keep.tile([P, nt * P], U8, name=f"w1s{k0}", align_bytes=64)
-            src = w1raw[b][:].rearrange("p j (m t) -> p m t j", t=4)[:, :, t0 : t0 + nt, :]
-            cast(bf[:].rearrange("p (t m j) -> p m t j", t=nt, j=4), src)
-            nc.vector.quantize_mx(out=q[:].bitcast(FP8X4), scales=s[:], in_=bf[:])
-            for k in range(k0, k1):
-                w1q[k] = q[:, (k - k0) * P : (k - k0 + 1) * P]
-                w1s[k] = s[:, (k - k0) * P : (k - k0 + 1) * P]
+        def prepare_w1(b, casts):
+            bf = keep.tile([P, 4, P, 4], BF16, name=f"w1bf{b}", tag=f"w1bf{b}", align_bytes=64)
+            q = keep.tile([P, 4 * P], U32, name=f"w1q{b}", align_bytes=64)
+            s = keep.tile([P, 4 * P], U8, name=f"w1s{b}", align_bytes=64)
+            src = w1raw[b][:].rearrange("p j (m t) -> p m t j", t=4)
+            for cast, t0, t1 in casts:
+                cast(bf[:, t0:t1, :, :].rearrange("p t m j -> p m t j"), src[:, :, t0:t1, :])
+            nc.vector.quantize_mx(out=q[:].bitcast(FP8X4), scales=s[:], in_=bf[:].rearrange("p t m j -> p (t m j)"))
+            for t in range(4):
+                w1q[4 * b + t] = q[:, t * P : (t + 1) * P]
+                w1s[4 * b + t] = s[:, t * P : (t + 1) * P]
 
         val = {}
 
         def trust(k, h):
             b, t = divmod(k, 4)
-            if h == 0:
-                val[k] = ring.tile([P, S], F32, name=f"val{k}", tag="q4", bufs=9, align_bytes=64)
-            acc = psum.tile([P, BANK], F32, name="acc_b", tag="pb")
+            if h == 0 and k in (0, 1, 3, 7):
+                val[k] = keep.tile([P, S], F32, name=f"val{k}", tag={0: "raw0", 1: "w1bf0", 3: "raw1", 7: "zq0"}[k], align_bytes=64)
+            elif h == 0:
+                val[k] = ring.tile([P, S], F32, name=f"val{k}", tag="q4", bufs=4, align_bytes=64)
+            acc = psum.tile([P, BANK], F32, name="acc_b", tag="pb", bufs=3)
             nc.tensor.matmul_mx(
                 out=acc[:],
                 lhsT=w4w[:, 256 * k : 256 * (k + 1)].bitcast(FP4X4),
@@ -157,7 +164,7 @@ def tile_list_reefer_yard_alarm_kernel(
             weigh(nc.gpsimd, k, slice(0, S))
 
         def times_a_on_vector(k, h):
-            nc.vector.tensor_tensor(val[k][:, halves[h]], deviation(k, h)[:], val[k][:, halves[h]], MULT)
+            nc.vector.tensor_tensor(val[k][:, halves[h]], val[k][:, halves[h]], deviation(k, h)[:], MULT)
 
         def times_a_on_gpsimd(k):
             a_sb = ring.tile([P, S], F32, name="a_sb", tag="a_sb", bufs=3)
@@ -180,10 +187,8 @@ def tile_list_reefer_yard_alarm_kernel(
                 MULT,
             )
 
-        zq = [keep.tile([P, T2], U32, name=f"zq{b}", align_bytes=64) for b in range(2)]
-        zs = [keep.tile([P, T2], U8, name=f"zs{b}", align_bytes=64) for b in range(2)]
         zw0 = keep.tile([P, 2, T2], F32, name="zw0")
-        zw1 = []
+        zw1 = keep.tile([P, CHUNKS + 2, BANK], F32, name="zw1")
         lev = {}
 
         def level_whole(k):
@@ -193,42 +198,35 @@ def tile_list_reefer_yard_alarm_kernel(
             level(k, lev[j][:, u, :], slice(0, T2))
 
         def expose_pair(j):
-            for c in range(CHUNKS):
-                cols = slice(BANK * c, BANK * (c + 1))
-                if j < 2:
-                    dst = zw0[:, j, cols]
-                else:
-                    zw1.append(ring.tile([P, 2, BANK], F32, name=f"zw1_{c}", tag="q4", bufs=9, align_bytes=64))
-                    dst = zw1[c][:, 0, :]
-                expose(nc.gpsimd, dst, lev[j][:, :, cols], expo_t[j][:, :, cols])
+            if j < 2:
+                expose(nc.gpsimd, zw0[:, j, :], lev[j][:], expo_t[j][:])
+            else:
+                for c in range(CHUNKS):
+                    cols = slice(BANK * c, BANK * (c + 1))
+                    expose(nc.gpsimd, zw1[:, c, :], lev[j][:, :, cols], expo_t[j][:, :, cols])
             if j < 2:
                 load_expo(j + 2)
 
+        prepare_w1(0, [(nc.scalar.copy, 0, 4)])
+        load_expo(0)
         trust(0, 0)
-        prepare_w1(0, 2, nc.vector.tensor_copy)
-        prepare_w1(2, 4, nc.scalar.copy)
         trust(0, 1)
         for h in range(2):
             weigh((nc.vector, nc.gpsimd)[h], 0, halves[h])
             times_a_on_vector(0, h)
             nc.vector.tensor_copy(page0[:].indirect(offs2_t[:, 32 * h : 32 * (h + 1)]), val[0][:, halves[h]])
+        load_expo(1)
         gate(1)
-        gate(2)
-        times_a_on_gpsimd(2)
-        prepare_w1(4, 8, nc.scalar.copy)
-        w8w = keep.tile([P, 2, N], I32, name="w8w", tag="w1bf4", align_bytes=64)
-        w8s = keep.tile([P, 2, N], U8, name="w8s", tag="w1bf0", align_bytes=64)
-        nc.vector.memset(w8s[:].rearrange("p a c -> p (a c)").bitcast(I32), 0)
-        for r in range(4):
-            nc.sync.dma_start(w8s[r:P:32, :, :].bitcast(I32), w8_scales[:, r:16:4, :].rearrange("a q c -> q a c").bitcast(I32))
-        nc.sync.dma_start(w8w[:], w8_words.rearrange("a p c i -> p a (c i)").bitcast(I32))
-        gate(3)
-        times_a_on_gpsimd(3)
-        level_whole(0)
         for h in range(2):
             times_a_on_vector(1, h)
         place(1)
+        gate(2)
+        times_a_on_gpsimd(2)
+        prepare_w1(1, [(nc.scalar.copy, 0, 4)])
+        gate(3)
+        times_a_on_gpsimd(3)
         gate(4)
+        level_whole(0)
         gate(5)
         times_a_on_gpsimd(4)
         level_whole(1)
@@ -240,6 +238,8 @@ def tile_list_reefer_yard_alarm_kernel(
         trust(7, 1)
         level_whole(2)
         place(3)
+        w8w = keep.tile([P, 2, N], I32, name="w8w", tag="raw1", align_bytes=64)
+        nc.sync.dma_start(w8w[:], w8_words.rearrange("a p c i -> p a (c i)").bitcast(I32))
         level_whole(3)
         place(4)
         expose_pair(1)
@@ -260,33 +260,37 @@ def tile_list_reefer_yard_alarm_kernel(
             place(k)
             for c in range(CHUNKS):
                 if k == 6:
-                    levs.append(ring.tile([P, 2, BANK], F32, name=f"lev3_{c}", tag="q4", bufs=9, align_bytes=64))
+                    levs.append(ring.tile([P, 2, BANK], F32, name=f"lev3_{c}", tag="q4", bufs=4, align_bytes=64))
                 level(k, levs[c][:, k - 6, :], slice(BANK * c, BANK * (c + 1)))
 
+        zq = [keep.tile([P, T2], U32, name=f"zq{b}", tag=f"zq{b}", align_bytes=64) for b in range(2)]
+        zs = [keep.tile([P, T2], U8, name=f"zs{b}", align_bytes=64) for b in range(2)]
+
         def quantise(b, cols, words):
-            nc.vector.quantize_mx(
-                out=zq[b][:, cols].bitcast(FP8X4), scales=zs[b][:, cols], in_=words.rearrange("p m u -> p (m u)").bitcast(BF16)
-            )
+            q, s = zq[b][:, cols], zs[b][:, cols]
+            nc.vector.quantize_mx(out=q.bitcast(FP8X4), scales=s, in_=words.rearrange("p m u -> p (m u)").bitcast(BF16))
+            return q, s
 
         pieces = [(0, 512), (512, 512), (1024, 512), (1536, 256), (1792, 256)]
         for i, (m0, width) in enumerate(pieces):
             cols = slice(m0, m0 + width)
             c, o = divmod(m0, BANK)
             part = slice(o, o + width)
-            quantise(0, cols, zb0[:, cols, :])
-            expose(nc.vector, zw1[c][:, 1, part], levs[c][:, :, part], expo_t[3][:, :, cols])
+            row = CHUNKS + i % 2
+            z = [quantise(0, cols, zb0[:, cols, :])]
+            expose(nc.vector, zw1[:, row, part], levs[c][:, :, part], expo_t[3][:, :, cols])
             zb = ring.tile([P, width, 2], F32, name="zb1", tag="zb1", align_bytes=64)
-            nc.vector.tensor_copy(zb[:], zw1[c][:, :, part].rearrange("p u m -> p m u"))
-            quantise(1, cols, zb[:])
-            accs = [psum.tile([P, width], F32, name="acc_o", tag=("pa", "pb")[(3 * i + nb) % 2]) for nb in range(N // P)]
+            (nc.scalar.copy if i in SW else nc.vector.tensor_copy)(zb[:], zw1[:, c : row + 1 : row - c, part].rearrange("p u m -> p m u"))
+            z.append(quantise(1, cols, zb[:]))
+            accs = [psum.tile([P, width], F32, name="acc_o", tag=("pa", "pb", "pa")[nb], bufs=(5, 3, 5)[nb]) for nb in range(N // P)]
             for b in range(2):
                 for nb in range(N // P):
                     nc.tensor.matmul_mx(
                         out=accs[nb][:],
                         lhsT=w8w[:, b, P * nb : P * (nb + 1)].bitcast(FP8X4),
                         lhsT_scale=w8s[:, b, P * nb : P * (nb + 1)],
-                        rhs=zq[b][:, cols].bitcast(FP8X4),
-                        rhs_scale=zs[b][:, cols],
+                        rhs=z[b][0].bitcast(FP8X4),
+                        rhs_scale=z[b][1],
                         start=(b == 0),
                         stop=(b == 1),
                     )

@@ -1,6 +1,7 @@
 from contextlib import ExitStack
 
 import concourse.mybir as mybir
+from concourse.masks import make_identity
 
 K, T, S, H, T2, N = 512, 2048, 1024, 1024, 2048, 384
 FLOPS = 2 * K * H * S * 2 + 2 * H * N * T2
@@ -18,7 +19,7 @@ MULT = mybir.AluOpType.mult
 
 P = 128
 BANK = 512
-SW = (0, 1)
+SW = (1, 2)
 CHUNKS = T2 // BANK
 
 
@@ -36,7 +37,7 @@ def tile_list_reefer_yard_alarm_kernel(
         warm = keep.tile([P, 8], F32, name="warm")
         tabs = keep.tile([P, T], U8, name="tabs", tag="raw1", align_bytes=64)
         w4s_raw = keep.tile([P, H], U8, name="w4s_raw", tag="page1")
-        tabw = keep.tile([P, T], I32, name="tabw", tag="expo0")
+        tabw = keep.tile([P, T], I32, name="tabw", tag="expo0", align_bytes=64)
         w4w_raw = [keep.tile([P, H], U8, name=f"w4w_raw{b}", tag=("raw0", "wgs")[b], align_bytes=64) for b in range(2)]
         w4w = keep.tile([P, 2 * H], U8, name="w4w", align_bytes=64)
         w4s = keep.tile([P, H], U8, name="w4s", align_bytes=64)
@@ -76,7 +77,7 @@ def tile_list_reefer_yard_alarm_kernel(
 
         def load_expo(j):
             b, u = divmod(j, 2)
-            expo_t[j] = keep.tile([P, 2, T2], F32, name=f"expo{j}", tag=("expo0", "raw0")[j % 2], align_bytes=(None, 64)[j % 2])
+            expo_t[j] = keep.tile([P, 2, T2], F32, name=f"expo{j}", tag=("expo0", "raw0")[j % 2], align_bytes=64)
             rows = expo[512 * b : 512 * (b + 1), :].rearrange("(p t) m -> p t m", t=4)
             nc.sync.dma_start(expo_t[j][:], rows[:, 2 * u : 2 * u + 2, :])
 
@@ -108,7 +109,19 @@ def tile_list_reefer_yard_alarm_kernel(
         nc.gpsimd.memset(page1[:], 0.0)
         pages = [page0, page1]
 
+        ident = keep.tile([P, P], F32, name="ident")
+        make_identity(nc, ident[:])
+        wgs_col = keep.tile([P, 8, 8], F32, name="wgs_col")
+
+        def turn_wgs():
+            for h in range(2):
+                bank = psum.tile([P, 4, P], F32, name="wgs_bank", tag="pa")
+                for q in range(4):
+                    nc.tensor.transpose(bank[:, q, :], wgs_t[:, BANK * h + P * q : BANK * h + P * (q + 1)], ident[:])
+                nc.scalar.copy(wgs_col[:, 4 * h : 4 * h + 4, :], bank[:, :, 0:P:16])
+
         w1q, w1s = {}, {}
+        w1_whole = {}
 
         def prepare_w1(b, casts):
             bf = keep.tile([P, 4, P, 4], BF16, name=f"w1bf{b}", tag=f"w1bf{b}", align_bytes=64)
@@ -118,6 +131,7 @@ def tile_list_reefer_yard_alarm_kernel(
             for cast, t0, t1 in casts:
                 cast(bf[:, t0:t1, :, :].rearrange("p t m j -> p m t j"), src[:, :, t0:t1, :])
             nc.vector.quantize_mx(out=q[:].bitcast(FP8X4), scales=s[:], in_=bf[:].rearrange("p t m j -> p (t m j)"))
+            w1_whole[b] = (q, s)
             for t in range(4):
                 w1q[4 * b + t] = q[:, t * P : (t + 1) * P]
                 w1s[4 * b + t] = s[:, t * P : (t + 1) * P]
@@ -155,6 +169,33 @@ def tile_list_reefer_yard_alarm_kernel(
             )
             return acc
 
+        aw = [keep.tile([P, 4, P], F32, name=f"aw{jt}", tag=f"aw{jt}") for jt in range(8)]
+
+        def weighted_rows(jt):
+            h, q = divmod(jt, 4)
+            acc = psum.tile([P, 4, P], F32, name="acc_t", tag="pa")
+            nc.tensor.matmul_mx(
+                out=acc[:].rearrange("p t m -> p (t m)"),
+                lhsT=gw[h][:, P * q : P * (q + 1)].bitcast(FP8X4),
+                lhsT_scale=gs[h][:, P * q : P * (q + 1)],
+                rhs=w1_whole[1][0][:].bitcast(FP8X4),
+                rhs_scale=w1_whole[1][1][:],
+                start=True,
+                stop=True,
+            )
+            for g in range(8):
+                run = slice(16 * g, 16 * (g + 1))
+                nc.scalar.activation(aw[jt][:, :, run], acc[:, :, run], ACT.Copy, scale=wgs_col[:, jt, g : g + 1])
+
+        def turned_back(k, h):
+            acc = psum.tile([P, BANK], F32, name="acc_r", tag="pa")
+            for q in range(4):
+                nc.tensor.transpose(acc[:, P * q : P * (q + 1)], aw[4 * h + q][:, k - 4, :], ident[:])
+            return acc
+
+        def factor(k, h):
+            return deviation(k, h) if k < 4 else turned_back(k, h)
+
         def weigh(eng, k, cols):
             eng.tensor_tensor(val[k][:, cols], val[k][:, cols], wgs_t[:, cols], MULT)
 
@@ -164,12 +205,12 @@ def tile_list_reefer_yard_alarm_kernel(
             weigh(nc.gpsimd, k, slice(0, S))
 
         def times_a_on_vector(k, h):
-            nc.vector.tensor_tensor(val[k][:, halves[h]], val[k][:, halves[h]], deviation(k, h)[:], MULT)
+            nc.vector.tensor_tensor(val[k][:, halves[h]], val[k][:, halves[h]], factor(k, h)[:], MULT)
 
         def times_a_on_gpsimd(k):
-            a_sb = ring.tile([P, S], F32, name="a_sb", tag="a_sb", bufs=3)
+            a_sb = ring.tile([P, S], F32, name="a_sb", tag="a_sb", bufs=3, align_bytes=64)
             for h in range(2):
-                nc.scalar.copy(a_sb[:, halves[h]], deviation(k, h)[:])
+                nc.scalar.copy(a_sb[:, halves[h]], factor(k, h)[:])
             nc.gpsimd.tensor_tensor(val[k][:], val[k][:], a_sb[:], MULT)
 
         def place(k):
@@ -187,24 +228,31 @@ def tile_list_reefer_yard_alarm_kernel(
                 MULT,
             )
 
-        zw0 = keep.tile([P, 2, T2], F32, name="zw0")
-        zw1 = keep.tile([P, CHUNKS + 2, BANK], F32, name="zw1")
-        lev = {}
+        zw = [keep.tile([P, 2 * T2], F32, name=f"zw{b}") for b in range(2)]
+        late = keep.tile([P, 3 * T2], F32, name="late")
+        lev = {
+            2: late[:, T2 : 3 * T2].rearrange("p (t m) -> p t m", t=2),
+            3: late[:, 0 : 2 * T2].rearrange("p (t m) -> p t m", t=2),
+        }
+
+        def pair_words(j, cols):
+            return zw[j // 2][:, T2 * (j % 2) + cols.start : T2 * (j % 2) + cols.stop]
+
+        def both_pairs(b, cols):
+            return zw[b][:].rearrange("p (u m) -> p m u", u=2)[:, cols, :]
 
         def level_whole(k):
             j, u = divmod(k, 2)
-            if u == 0:
-                lev[j] = ring.tile([P, 2, T2], F32, name=f"lev{j}", tag="lev", align_bytes=64)
+            if j not in lev:
+                lev[j] = ring.tile([P, 2, T2], F32, name=f"lev{j}", tag="lev", align_bytes=64)[:]
             level(k, lev[j][:, u, :], slice(0, T2))
 
-        def expose_pair(j):
-            if j < 2:
-                expose(nc.gpsimd, zw0[:, j, :], lev[j][:], expo_t[j][:])
-            else:
-                for c in range(CHUNKS):
-                    cols = slice(BANK * c, BANK * (c + 1))
-                    expose(nc.gpsimd, zw1[:, c, :], lev[j][:, :, cols], expo_t[j][:, :, cols])
-            if j < 2:
+        def expose_cols(eng, j, cols):
+            expose(eng, pair_words(j, cols), lev[j][:, :, cols], expo_t[j][:, :, cols])
+
+        def expose_half(j, half):
+            expose_cols(nc.gpsimd, j, slice(2 * BANK * half, 2 * BANK * (half + 1)))
+            if half == 1:
                 load_expo(j + 2)
 
         prepare_w1(0, [(nc.scalar.copy, 0, 4)])
@@ -217,70 +265,73 @@ def tile_list_reefer_yard_alarm_kernel(
             nc.vector.tensor_copy(page0[:].indirect(offs2_t[:, 32 * h : 32 * (h + 1)]), val[0][:, halves[h]])
         load_expo(1)
         gate(1)
-        for h in range(2):
-            times_a_on_vector(1, h)
-        place(1)
+        times_a_on_gpsimd(1)
+        turn_wgs()
         gate(2)
         times_a_on_gpsimd(2)
         prepare_w1(1, [(nc.scalar.copy, 0, 4)])
+        place(1)
         gate(3)
         times_a_on_gpsimd(3)
-        gate(4)
         level_whole(0)
-        gate(5)
-        times_a_on_gpsimd(4)
-        level_whole(1)
         place(2)
-        expose_pair(0)
-        times_a_on_gpsimd(5)
-        gate(6)
-        trust(7, 0)
-        trust(7, 1)
-        level_whole(2)
+        for jt in range(4):
+            weighted_rows(jt)
+        level_whole(1)
+        expose_half(0, 0)
+        for jt in range(4, 8):
+            weighted_rows(jt)
         place(3)
         w8w = keep.tile([P, 2, N], I32, name="w8w", tag="raw1", align_bytes=64)
         nc.sync.dma_start(w8w[:], w8_words.rearrange("a p c i -> p a (c i)").bitcast(I32))
-        level_whole(3)
+
+        def gated(k):
+            trust(k, 0)
+            trust(k, 1)
+            times_a_on_gpsimd(k)
+
+        gated(4)
+        expose_half(0, 1)
+        level_whole(2)
         place(4)
-        expose_pair(1)
-        weigh(nc.gpsimd, 7, slice(0, S))
-        level_whole(4)
+        gated(5)
+        level_whole(3)
+        expose_half(1, 0)
         place(5)
+        gated(6)
+        expose_half(1, 1)
+        trust(7, 0)
+        trust(7, 1)
+        level_whole(4)
+        place(6)
         level_whole(5)
-        expose_pair(2)
+        expose_cols(nc.gpsimd, 2, slice(0, T2))
         zb0 = ring.tile([P, T2, 2], F32, name="zb0", tag="lev", align_bytes=64)
         for c in range(CHUNKS):
             cols = slice(BANK * c, BANK * (c + 1))
-            nc.scalar.copy(zb0[:, cols, :], zw0[:, :, cols].rearrange("p u m -> p m u"))
+            nc.scalar.copy(zb0[:, cols, :], both_pairs(0, cols))
 
-        levs = []
-        for k in (6, 7):
-            for h in range(2):
-                times_a_on_vector(k, h)
-            place(k)
-            for c in range(CHUNKS):
-                if k == 6:
-                    levs.append(ring.tile([P, 2, BANK], F32, name=f"lev3_{c}", tag="q4", bufs=4, align_bytes=64))
-                level(k, levs[c][:, k - 6, :], slice(BANK * c, BANK * (c + 1)))
+        level_whole(6)
+        for h in range(2):
+            times_a_on_vector(7, h)
+        place(7)
 
         zq = [keep.tile([P, T2], U32, name=f"zq{b}", tag=f"zq{b}", align_bytes=64) for b in range(2)]
-        zs = [keep.tile([P, T2], U8, name=f"zs{b}", align_bytes=64) for b in range(2)]
+        zs = [keep.tile([P, T2], U8, name=f"zs{b}", tag=("expo0", "zs1")[b], align_bytes=64) for b in range(2)]
 
         def quantise(b, cols, words):
             q, s = zq[b][:, cols], zs[b][:, cols]
             nc.vector.quantize_mx(out=q.bitcast(FP8X4), scales=s, in_=words.rearrange("p m u -> p (m u)").bitcast(BF16))
             return q, s
 
-        pieces = [(0, 512), (512, 512), (1024, 512), (1536, 256), (1792, 256)]
+        pieces = [(0, 256), (256, 512), (768, 512), (1280, 512), (1792, 256)]
         for i, (m0, width) in enumerate(pieces):
             cols = slice(m0, m0 + width)
-            c, o = divmod(m0, BANK)
-            part = slice(o, o + width)
-            row = CHUNKS + i % 2
+            level(7, lev[3][:, 1, cols], cols)
             z = [quantise(0, cols, zb0[:, cols, :])]
-            expose(nc.vector, zw1[:, row, part], levs[c][:, :, part], expo_t[3][:, :, cols])
-            zb = ring.tile([P, width, 2], F32, name="zb1", tag="zb1", align_bytes=64)
-            (nc.scalar.copy if i in SW else nc.vector.tensor_copy)(zb[:], zw1[:, c : row + 1 : row - c, part].rearrange("p u m -> p m u"))
+            expose_cols(nc.vector, 3, cols)
+            zb = ring.tile([P, width, 2], F32, name="zb1", tag="a_sb", bufs=3, align_bytes=64)
+            (nc.scalar.copy if i in SW else nc.vector.tensor_copy)(zb[:], both_pairs(1, cols))
             z.append(quantise(1, cols, zb[:]))
             accs = [psum.tile([P, width], F32, name="acc_o", tag=("pa", "pb", "pa")[nb], bufs=(5, 3, 5)[nb]) for nb in range(N // P)]
             for b in range(2):
@@ -295,7 +346,7 @@ def tile_list_reefer_yard_alarm_kernel(
                         stop=(b == 1),
                     )
             for nb in range(N // P):
-                res = ring.tile([P, width], F32, name="res", tag="res", bufs=6)
+                res = keep.tile([P, width], F32, name="res", tag=f"aw{(3 * i + nb) % 8}")
                 if i == len(pieces) - 1 and nb == 1:
                     nc.vector.tensor_copy(res[:], accs[nb][:])
                 else:

@@ -16,6 +16,7 @@ FP8X4 = mybir.dt.float8_e4m3fn_x4
 FP4X4 = mybir.dt.float4_e2m1fn_x4
 ACT = mybir.ActivationFunctionType
 MULT = mybir.AluOpType.mult
+ADD = mybir.AluOpType.add
 
 P = 128
 BANK = 512
@@ -36,42 +37,41 @@ def tile_list_reefer_yard_alarm_kernel(
         offs2_t = keep.tile([P, S // 16], U16, name="offs2_t")
         warm = keep.tile([P, 8], F32, name="warm")
         tabs = keep.tile([P, T], U8, name="tabs", tag="raw1", align_bytes=64)
-        w4s_raw = keep.tile([P, H], U8, name="w4s_raw", tag="page1")
+        w4s_raw = keep.tile([P, H], U8, name="w4s_raw")
         tabw = keep.tile([P, T], I32, name="tabw", tag="expo0", align_bytes=64)
-        w4w_raw = [keep.tile([P, H], U8, name=f"w4w_raw{b}", tag=("raw0", "wgs")[b], align_bytes=64) for b in range(2)]
+        w4w_raw = keep.tile([P, 2 * H], U8, name="w4w_raw", tag="wgs", align_bytes=64)
         w4w = keep.tile([P, 2 * H], U8, name="w4w", align_bytes=64)
         w4s = keep.tile([P, H], U8, name="w4s", align_bytes=64)
         bg_t = keep.tile([P, 2, 4], F32, name="bg_t")
         amb_t = keep.tile([P, 2, 4], F32, name="amb_t")
         warm2 = keep.tile([P, 8], F32, name="warm2")
         page0 = keep.tile([P, T2], F32, name="page0")
+        page1 = keep.tile([P, T2], F32, name="page1")
 
         nc.vector.memset(tabs[:].bitcast(I32), 0)
         nc.vector.memset(w4s_raw[:].bitcast(I32), 0)
         nc.vector.memset(warm[:], 0.0)
         nc.vector.memset(page0[:], 0.0)
-        w8s = keep.tile([P, 2, N], U8, name="w8s", align_bytes=64)
-        nc.vector.memset(w8s[:].rearrange("p a c -> p (a c)").bitcast(I32), 0)
+        nc.vector.memset(page1[:], 0.0)
 
-        nc.sync.dma_start(offs_t[:], offs)
-        for b in range(2):
-            nc.sync.dma_start(w4w_raw[b][:].bitcast(I32), w4_words[0, :, H * b : H * (b + 1)].bitcast(I32))
-        nc.sync.dma_start(tabw[:], tab_words[0].rearrange("p t i -> p (t i)").bitcast(I32))
-        nc.sync.dma_start(offs2_t[:], offs2)
-        for r in range(4):
-            nc.scalar.dma_start(tabs[r:P:32, :].bitcast(I32), tab_scales[0, r:16:4, :].bitcast(I32))
-        for r in range(4):
-            nc.scalar.dma_start(w4s_raw[r:P:32, :].bitcast(I32), w4_scales[0, r:16:4, :].bitcast(I32))
-        nc.scalar.activation(warm2[:], warm[:], ACT.Sigmoid)
-        nc.gpsimd.dma_start(bg_t[:], bg.rearrange("(b p t) -> p b t", b=2, t=4))
-        nc.gpsimd.dma_start(amb_t[:], amb.rearrange("(b p t) -> p b t", b=2, t=4))
-        for r in range(4):
-            nc.gpsimd.dma_start(w8s[r:P:32, :, :].bitcast(I32), w8_scales[:, r:16:4, :].rearrange("a q c -> q a c").bitcast(I32))
         w1raw = {}
 
         def load_w1(b):
             w1raw[b] = keep.tile([P, 4, 512], F32, name=f"w1raw{b}", tag=f"raw{b}", align_bytes=64)
             nc.sync.dma_start(w1raw[b][:], w1[:, 512 * b : 512 * (b + 1)].rearrange("(p j) c -> p j c", j=4))
+
+        nc.sync.dma_start(offs_t[:], offs)
+        nc.sync.dma_start(offs2_t[:], offs2)
+        nc.sync.dma_start(w4w_raw[:].bitcast(I32), w4_words[0].bitcast(I32))
+        nc.sync.dma_start(tabw[:], tab_words[0].rearrange("p t i -> p (t i)").bitcast(I32))
+        load_w1(0)
+        for r in range(4):
+            nc.scalar.dma_start(tabs[r:P:32, :].bitcast(I32), tab_scales[0, r:16:4, :].bitcast(I32))
+        nc.gpsimd.dma_start(bg_t[:], bg.rearrange("(b p t) -> p b t", b=2, t=4))
+        for r in range(4):
+            (nc.scalar, nc.gpsimd)[r // 2].dma_start(w4s_raw[r:P:32, :].bitcast(I32), w4_scales[0, r:16:4, :].bitcast(I32))
+        nc.scalar.activation(warm2[:], warm[:], ACT.Sigmoid)
+        nc.gpsimd.dma_start(amb_t[:], amb.rearrange("(b p t) -> p b t", b=2, t=4))
 
         expo_t = {}
 
@@ -87,12 +87,10 @@ def tile_list_reefer_yard_alarm_kernel(
         halves = [slice(BANK * h, BANK * (h + 1)) for h in range(2)]
         lists = [offs_t[:, 32 * h : 32 * (h + 1)] for h in range(2)]
 
-        for b in range(2):
-            nc.vector.tensor_copy(
-                w4w[:, H * b : H * (b + 1)].bitcast(U16).rearrange("p (t m) -> p t m", t=4),
-                w4w_raw[b][:].bitcast(U16).rearrange("p (m t) -> p t m", t=4),
-            )
-        load_w1(0)
+        nc.vector.tensor_copy(
+            w4w[:].bitcast(U16).rearrange("p (b t m) -> p b t m", b=2, t=4),
+            w4w_raw[:].bitcast(U16).rearrange("p (b m t) -> p b t m", b=2, t=4),
+        )
         wgs_t = keep.tile([P, S], F32, name="wgs_t", tag="wgs", align_bytes=64)
         nc.sync.dma_start(wgs_t[:], wgs)
         nc.vector.tensor_copy(gs[0][:], tabs[:].indirect(lists[0]))
@@ -105,8 +103,6 @@ def tile_list_reefer_yard_alarm_kernel(
         nc.vector.tensor_copy(gs[1][:], tabs[:].indirect(lists[1]))
         nc.vector.tensor_copy(gw[1][:], tabw[:].bitcast(U32).indirect(lists[1]))
         load_w1(1)
-        page1 = keep.tile([P, T2], F32, name="page1", tag="page1")
-        nc.gpsimd.memset(page1[:], 0.0)
         pages = [page0, page1]
 
         ident = keep.tile([P, P], F32, name="ident")
@@ -228,7 +224,7 @@ def tile_list_reefer_yard_alarm_kernel(
                 MULT,
             )
 
-        zw = [keep.tile([P, 2 * T2], F32, name=f"zw{b}") for b in range(2)]
+        zw = [keep.tile([P, 2 * T2], F32, name=f"zw{b}", tag=f"zw{b}") for b in range(2)]
         late = keep.tile([P, 3 * T2], F32, name="late")
         lev = {
             2: late[:, T2 : 3 * T2].rearrange("p (t m) -> p t m", t=2),
@@ -255,22 +251,25 @@ def tile_list_reefer_yard_alarm_kernel(
             if half == 1:
                 load_expo(j + 2)
 
-        prepare_w1(0, [(nc.scalar.copy, 0, 4)])
+        def cast_on_gpsimd(dst, src):
+            nc.gpsimd.tensor_scalar(dst, src, 1.0, 0.0, MULT, ADD)
+
+        prepare_w1(0, [(nc.scalar.copy, 0, 2), (cast_on_gpsimd, 2, 4)])
         load_expo(0)
         trust(0, 0)
         trust(0, 1)
         for h in range(2):
-            weigh((nc.vector, nc.gpsimd)[h], 0, halves[h])
+            weigh(nc.gpsimd, 0, halves[h])
             times_a_on_vector(0, h)
             nc.vector.tensor_copy(page0[:].indirect(offs2_t[:, 32 * h : 32 * (h + 1)]), val[0][:, halves[h]])
         load_expo(1)
         gate(1)
         times_a_on_gpsimd(1)
-        turn_wgs()
+        prepare_w1(1, [(nc.scalar.copy, 0, 4)])
         gate(2)
         times_a_on_gpsimd(2)
-        prepare_w1(1, [(nc.scalar.copy, 0, 4)])
         place(1)
+        turn_wgs()
         gate(3)
         times_a_on_gpsimd(3)
         level_whole(0)
@@ -284,6 +283,12 @@ def tile_list_reefer_yard_alarm_kernel(
         place(3)
         w8w = keep.tile([P, 2, N], I32, name="w8w", tag="raw1", align_bytes=64)
         nc.sync.dma_start(w8w[:], w8_words.rearrange("a p c i -> p a (c i)").bitcast(I32))
+        w8s = w1_whole[0][1]
+        for quad in range(4):
+            nc.sync.dma_start(
+                w8s[32 * quad + 4 : 32 * quad + 12, 0:N].bitcast(I32),
+                w8_scales[:, 4 * quad : 4 * quad + 4, :].bitcast(I32),
+            )
 
         def gated(k):
             trust(k, 0)
@@ -324,7 +329,9 @@ def tile_list_reefer_yard_alarm_kernel(
             nc.vector.quantize_mx(out=q.bitcast(FP8X4), scales=s, in_=words.rearrange("p m u -> p (m u)").bitcast(BF16))
             return q, s
 
-        pieces = [(0, 256), (256, 512), (768, 512), (1280, 512), (1792, 256)]
+        pieces = [(0, 256), (256, 512), (768, 512), (1280, 256), (1536, 256), (1792, 256)]
+        spare = keep.tile([P, 2 * T2], F32, name="spare", tag="zw0")
+        used = 0
         for i, (m0, width) in enumerate(pieces):
             cols = slice(m0, m0 + width)
             level(7, lev[3][:, 1, cols], cols)
@@ -339,15 +346,19 @@ def tile_list_reefer_yard_alarm_kernel(
                     nc.tensor.matmul_mx(
                         out=accs[nb][:],
                         lhsT=w8w[:, b, P * nb : P * (nb + 1)].bitcast(FP8X4),
-                        lhsT_scale=w8s[:, b, P * nb : P * (nb + 1)],
+                        lhsT_scale=w8s[4 * (b + 1) : P, P * nb : P * (nb + 1)],
                         rhs=z[b][0].bitcast(FP8X4),
                         rhs_scale=z[b][1],
                         start=(b == 0),
                         stop=(b == 1),
                     )
             for nb in range(N // P):
-                res = keep.tile([P, width], F32, name="res", tag=f"aw{(3 * i + nb) % 8}")
-                if i == len(pieces) - 1 and nb == 1:
+                if 3 * i + nb < 8:
+                    res = keep.tile([P, width], F32, name="res", tag=f"aw{3 * i + nb}")
+                else:
+                    res = spare[:, used : used + width]
+                    used = used + width
+                if i == len(pieces) - 1 and nb > 0:
                     nc.vector.tensor_copy(res[:], accs[nb][:])
                 else:
                     nc.scalar.copy(res[:], accs[nb][:])

@@ -16,12 +16,12 @@ FP8X4 = mybir.dt.float8_e4m3fn_x4
 FP4X4 = mybir.dt.float4_e2m1fn_x4
 ACT = mybir.ActivationFunctionType
 MULT = mybir.AluOpType.mult
-ADD = mybir.AluOpType.add
 
 P = 128
 BANK = 512
 SW = (1, 2)
 CHUNKS = T2 // BANK
+A_AT = {3: 0, 4: 1536, 5: 2560, 6: 3072}
 
 
 def tile_list_reefer_yard_alarm_kernel(
@@ -35,22 +35,21 @@ def tile_list_reefer_yard_alarm_kernel(
 
         offs_t = keep.tile([P, S // 16], U16, name="offs_t")
         offs2_t = keep.tile([P, S // 16], U16, name="offs2_t")
-        warm = keep.tile([P, 8], F32, name="warm")
+        warm = keep.tile([P, 8], F32, name="warm", tag="expo0", align_bytes=64)
         tabs = keep.tile([P, T], U8, name="tabs", tag="raw1", align_bytes=64)
         w4s_raw = keep.tile([P, H], U8, name="w4s_raw")
-        tabw = keep.tile([P, T], I32, name="tabw", tag="expo0", align_bytes=64)
         w4w_raw = keep.tile([P, 2 * H], U8, name="w4w_raw", tag="wgs", align_bytes=64)
         w4w = keep.tile([P, 2 * H], U8, name="w4w", align_bytes=64)
         w4s = keep.tile([P, H], U8, name="w4s", align_bytes=64)
         bg_t = keep.tile([P, 2, 4], F32, name="bg_t")
         amb_t = keep.tile([P, 2, 4], F32, name="amb_t")
-        warm2 = keep.tile([P, 8], F32, name="warm2")
+        warm2 = keep.tile([P, 8], F32, name="warm2", tag="raw0", align_bytes=64)
         page0 = keep.tile([P, T2], F32, name="page0")
         page1 = keep.tile([P, T2], F32, name="page1")
 
+        nc.vector.memset(warm[:], 0.0)
         nc.vector.memset(tabs[:].bitcast(I32), 0)
         nc.vector.memset(w4s_raw[:].bitcast(I32), 0)
-        nc.vector.memset(warm[:], 0.0)
         nc.vector.memset(page0[:], 0.0)
         nc.vector.memset(page1[:], 0.0)
 
@@ -63,15 +62,16 @@ def tile_list_reefer_yard_alarm_kernel(
         nc.sync.dma_start(offs_t[:], offs)
         nc.sync.dma_start(offs2_t[:], offs2)
         nc.sync.dma_start(w4w_raw[:].bitcast(I32), w4_words[0].bitcast(I32))
+        for r in range(4):
+            nc.sync.dma_start(tabs[r:P:32, :].bitcast(I32), tab_scales[0, r:16:4, :].bitcast(I32))
+        for r in range(4):
+            nc.sync.dma_start(w4s_raw[r:P:32, :].bitcast(I32), w4_scales[0, r:16:4, :].bitcast(I32))
+        nc.scalar.activation(warm2[:], warm[:], ACT.Sigmoid)
+        nc.gpsimd.dma_start(bg_t[:], bg.rearrange("(b p t) -> p b t", b=2, t=4))
+        nc.gpsimd.dma_start(amb_t[:], amb.rearrange("(b p t) -> p b t", b=2, t=4))
+        tabw = keep.tile([P, T], I32, name="tabw", tag="expo0", align_bytes=64)
         nc.sync.dma_start(tabw[:], tab_words[0].rearrange("p t i -> p (t i)").bitcast(I32))
         load_w1(0)
-        for r in range(4):
-            nc.scalar.dma_start(tabs[r:P:32, :].bitcast(I32), tab_scales[0, r:16:4, :].bitcast(I32))
-        nc.gpsimd.dma_start(bg_t[:], bg.rearrange("(b p t) -> p b t", b=2, t=4))
-        for r in range(4):
-            (nc.scalar, nc.gpsimd)[r // 2].dma_start(w4s_raw[r:P:32, :].bitcast(I32), w4_scales[0, r:16:4, :].bitcast(I32))
-        nc.scalar.activation(warm2[:], warm[:], ACT.Sigmoid)
-        nc.gpsimd.dma_start(amb_t[:], amb.rearrange("(b p t) -> p b t", b=2, t=4))
 
         expo_t = {}
 
@@ -92,29 +92,32 @@ def tile_list_reefer_yard_alarm_kernel(
             w4w_raw[:].bitcast(U16).rearrange("p (b m t) -> p b t m", b=2, t=4),
         )
         wgs_t = keep.tile([P, S], F32, name="wgs_t", tag="wgs", align_bytes=64)
-        nc.sync.dma_start(wgs_t[:], wgs)
-        nc.vector.tensor_copy(gs[0][:], tabs[:].indirect(lists[0]))
-        nc.vector.tensor_copy(gw[0][:], tabw[:].bitcast(U32).indirect(lists[0]))
+        for half in halves:
+            nc.sync.dma_start(wgs_t[:, half], wgs[:, half])
+        gs.append(keep.tile([P, BANK], U8, name="gs1", align_bytes=64))
+        for h in range(2):
+            nc.vector.tensor_copy(gs[h][:], tabs[:].indirect(lists[h]))
         nc.vector.tensor_copy(
             w4s[:].rearrange("p (b t m) -> p b t m", b=2, t=4),
             w4s_raw[:].rearrange("p (b m t) -> p b t m", b=2, t=4),
         )
-        gs.append(keep.tile([P, BANK], U8, name="gs1", align_bytes=64))
-        nc.vector.tensor_copy(gs[1][:], tabs[:].indirect(lists[1]))
-        nc.vector.tensor_copy(gw[1][:], tabw[:].bitcast(U32).indirect(lists[1]))
+        for h in range(2):
+            nc.vector.tensor_copy(gw[h][:], tabw[:].bitcast(U32).indirect(lists[h]))
         load_w1(1)
         pages = [page0, page1]
 
         ident = keep.tile([P, P], F32, name="ident")
         make_identity(nc, ident[:])
-        wgs_col = keep.tile([P, 8, 8], F32, name="wgs_col")
+        lev0 = ring.tile([P, 2, T2], F32, name="lev0", tag="lev", align_bytes=64)
+        wgs_late = keep.tile([P, 32], F32, name="wgs_late")
+        wgs_col = [lev0[:, 1, 0:32], wgs_late[:]]
 
         def turn_wgs():
             for h in range(2):
                 bank = psum.tile([P, 4, P], F32, name="wgs_bank", tag="pa")
                 for q in range(4):
                     nc.tensor.transpose(bank[:, q, :], wgs_t[:, BANK * h + P * q : BANK * h + P * (q + 1)], ident[:])
-                nc.scalar.copy(wgs_col[:, 4 * h : 4 * h + 4, :], bank[:, :, 0:P:16])
+                nc.scalar.copy(wgs_col[h].rearrange("p (q g) -> p q g", g=8), bank[:, :, 0:P:16])
 
         w1q, w1s = {}, {}
         w1_whole = {}
@@ -137,7 +140,7 @@ def tile_list_reefer_yard_alarm_kernel(
         def trust(k, h):
             b, t = divmod(k, 4)
             if h == 0 and k in (0, 1, 3, 7):
-                val[k] = keep.tile([P, S], F32, name=f"val{k}", tag={0: "raw0", 1: "w1bf0", 3: "raw1", 7: "zq0"}[k], align_bytes=64)
+                val[k] = keep.tile([P, S], F32, name=f"val{k}", tag={0: "raw0", 1: "w1bf0", 3: "w1bf1", 7: "zq0"}[k], align_bytes=64)
             elif h == 0:
                 val[k] = ring.tile([P, S], F32, name=f"val{k}", tag="q4", bufs=4, align_bytes=64)
             acc = psum.tile([P, BANK], F32, name="acc_b", tag="pb", bufs=3)
@@ -181,7 +184,7 @@ def tile_list_reefer_yard_alarm_kernel(
             )
             for g in range(8):
                 run = slice(16 * g, 16 * (g + 1))
-                nc.scalar.activation(aw[jt][:, :, run], acc[:, :, run], ACT.Copy, scale=wgs_col[:, jt, g : g + 1])
+                nc.scalar.activation(aw[jt][:, :, run], acc[:, :, run], ACT.Copy, scale=wgs_col[h][:, 8 * q + g : 8 * q + g + 1])
 
         def turned_back(k, h):
             acc = psum.tile([P, BANK], F32, name="acc_r", tag="pa")
@@ -204,10 +207,16 @@ def tile_list_reefer_yard_alarm_kernel(
             nc.vector.tensor_tensor(val[k][:, halves[h]], val[k][:, halves[h]], factor(k, h)[:], MULT)
 
         def times_a_on_gpsimd(k):
-            a_sb = ring.tile([P, S], F32, name="a_sb", tag="a_sb", bufs=3, align_bytes=64)
+            if k < 3:
+                a_sb = ring.tile([P, S], F32, name="a_sb", tag="a_sb", bufs=3, align_bytes=64)[:]
+            else:
+                a_sb = zw[0][:, A_AT[k] : A_AT[k] + S]
             for h in range(2):
                 nc.scalar.copy(a_sb[:, halves[h]], factor(k, h)[:])
-            nc.gpsimd.tensor_tensor(val[k][:], val[k][:], a_sb[:], MULT)
+            gated_rows = val[k]
+            if k == 1:
+                val[k] = keep.tile([P, S], F32, name="val1_done", tag="raw1", align_bytes=64)
+            nc.gpsimd.tensor_tensor(val[k][:], gated_rows[:], a_sb, MULT)
 
         def place(k):
             nc.vector.tensor_copy(pages[k % 2][:].indirect(offs2_t[:]), val[k][:])
@@ -227,6 +236,7 @@ def tile_list_reefer_yard_alarm_kernel(
         zw = [keep.tile([P, 2 * T2], F32, name=f"zw{b}", tag=f"zw{b}") for b in range(2)]
         late = keep.tile([P, 3 * T2], F32, name="late")
         lev = {
+            0: lev0[:],
             2: late[:, T2 : 3 * T2].rearrange("p (t m) -> p t m", t=2),
             3: late[:, 0 : 2 * T2].rearrange("p (t m) -> p t m", t=2),
         }
@@ -247,26 +257,23 @@ def tile_list_reefer_yard_alarm_kernel(
             expose(eng, pair_words(j, cols), lev[j][:, :, cols], expo_t[j][:, :, cols])
 
         def expose_half(j, half):
-            expose_cols(nc.gpsimd, j, slice(2 * BANK * half, 2 * BANK * (half + 1)))
+            expose_cols(nc.gpsimd, j, slice((0, (1536, 1024)[j], T2)[half], (0, (1536, 1024)[j], T2)[half + 1]))
             if half == 1:
                 load_expo(j + 2)
 
-        def cast_on_gpsimd(dst, src):
-            nc.gpsimd.tensor_scalar(dst, src, 1.0, 0.0, MULT, ADD)
-
-        prepare_w1(0, [(nc.scalar.copy, 0, 2), (cast_on_gpsimd, 2, 4)])
+        prepare_w1(0, [(nc.scalar.copy, 0, 2), (nc.vector.tensor_copy, 2, 4)])
         load_expo(0)
         trust(0, 0)
         trust(0, 1)
         for h in range(2):
-            weigh(nc.gpsimd, 0, halves[h])
+            weigh((nc.vector, nc.gpsimd)[h], 0, halves[h])
             times_a_on_vector(0, h)
             nc.vector.tensor_copy(page0[:].indirect(offs2_t[:, 32 * h : 32 * (h + 1)]), val[0][:, halves[h]])
         load_expo(1)
         gate(1)
-        times_a_on_gpsimd(1)
-        prepare_w1(1, [(nc.scalar.copy, 0, 4)])
         gate(2)
+        prepare_w1(1, [(nc.scalar.copy, 0, 4)])
+        times_a_on_gpsimd(1)
         times_a_on_gpsimd(2)
         place(1)
         turn_wgs()

@@ -19,9 +19,25 @@ MULT = mybir.AluOpType.mult
 
 P = 128
 BANK = 512
-SW = (1, 2)
-CHUNKS = T2 // BANK
-A_AT = {3: 0, 4: 1536, 5: 2560, 6: 3072}
+GROUP = 16
+BANKS_A, BANKS_B = 5, 3
+KIB = 1024
+
+LAID_AT = {
+    "w1_first": 8 * KIB,
+    "plane2": 24 * KIB,
+    "plane3": 28 * KIB,
+    "plane1_gate": 33 * KIB,
+    "wgs": 37 * KIB,
+    "w1_second": 41 * KIB,
+}
+W4_RAW_AT = 7 * KIB
+W1_ROUNDED_AT = (32 * KIB, 26 * KIB)
+TAB_SCALES_AT = 40 * KIB
+W4_SCALES_LATE_AT = 32 * KIB
+
+PIECES = [(0, 256), (256, 512), (768, 512), (1280, 256), (1536, 256), (1792, 256)]
+SCALAR_WEAVES = (1, 2)
 
 
 def tile_list_reefer_yard_alarm_kernel(
@@ -30,80 +46,83 @@ def tile_list_reefer_yard_alarm_kernel(
     nc = tc.nc
     with ExitStack() as ctx:
         keep = ctx.enter_context(tc.tile_pool(name="keep", bufs=1))
+        laid = ctx.enter_context(tc.tile_pool(name="laid", bufs=1))
         ring = ctx.enter_context(tc.tile_pool(name="ring", bufs=2))
-        psum = ctx.enter_context(tc.psum_pool(name="psum", bufs=5))
+        psum = ctx.enter_context(tc.psum_pool(name="psum", bufs=BANKS_A))
 
-        offs_t = keep.tile([P, S // 16], U16, name="offs_t")
-        offs2_t = keep.tile([P, S // 16], U16, name="offs2_t")
-        warm = keep.tile([P, 8], F32, name="warm", tag="expo0", align_bytes=64)
-        tabs = keep.tile([P, T], U8, name="tabs", tag="raw1", align_bytes=64)
-        w4s_raw = keep.tile([P, H], U8, name="w4s_raw")
-        w4w_raw = keep.tile([P, 2 * H], U8, name="w4w_raw", tag="wgs", align_bytes=64)
+        def shared(shape, name, tag):
+            if tag in LAID_AT:
+                return laid.tile(shape, F32, name=name, tag=tag, align_bytes=64, offset=LAID_AT[tag])
+            return keep.tile(shape, F32, name=name, tag=tag, align_bytes=64)
+
+        offs_t = keep.tile([P, S // GROUP], U16, name="offs_t")
+        offs2_t = keep.tile([P, S // GROUP], U16, name="offs2_t")
+        warm_in = keep.tile([P, 8], F32, name="warm_in", tag="table", align_bytes=64)
+        tab_sc = laid.tile([P, T], U8, name="tab_sc", align_bytes=64, offset=TAB_SCALES_AT)
+        w4s_raw = keep.tile([P, H], U8, name="w4s_raw", align_bytes=64)
+        w4w_raw = laid.tile([P, 2 * H], U8, name="w4w_raw", align_bytes=64, offset=W4_RAW_AT)
         w4w = keep.tile([P, 2 * H], U8, name="w4w", align_bytes=64)
-        w4s = keep.tile([P, H], U8, name="w4s", align_bytes=64)
+        w4s_first = keep.tile([P, P], U8, name="w4s_first", align_bytes=64)
         bg_t = keep.tile([P, 2, 4], F32, name="bg_t")
         amb_t = keep.tile([P, 2, 4], F32, name="amb_t")
-        warm2 = keep.tile([P, 8], F32, name="warm2", tag="raw0", align_bytes=64)
+        warm_out = keep.tile([P, 8], F32, name="warm_out")
         page0 = keep.tile([P, T2], F32, name="page0")
-        page1 = keep.tile([P, T2], F32, name="page1")
 
-        nc.vector.memset(warm[:], 0.0)
-        nc.vector.memset(tabs[:].bitcast(I32), 0)
-        nc.vector.memset(w4s_raw[:].bitcast(I32), 0)
+        nc.vector.memset(warm_in[:], 0.0)
+        nc.vector.memset(tab_sc[:].bitcast(I32), 0)
         nc.vector.memset(page0[:], 0.0)
-        nc.vector.memset(page1[:], 0.0)
+        nc.vector.memset(w4s_raw[:].bitcast(I32), 0)
 
-        w1raw = {}
+        w1_raw = {}
 
         def load_w1(b):
-            w1raw[b] = keep.tile([P, 4, 512], F32, name=f"w1raw{b}", tag=f"raw{b}", align_bytes=64)
-            nc.sync.dma_start(w1raw[b][:], w1[:, 512 * b : 512 * (b + 1)].rearrange("(p j) c -> p j c", j=4))
+            w1_raw[b] = shared([P, 4, 512], f"w1_raw{b}", ("w1_first", "w1_second")[b])
+            nc.sync.dma_start(w1_raw[b][:], w1[:, 512 * b : 512 * (b + 1)].rearrange("(p j) c -> p j c", j=4))
 
         nc.sync.dma_start(offs_t[:], offs)
         nc.sync.dma_start(offs2_t[:], offs2)
         nc.sync.dma_start(w4w_raw[:].bitcast(I32), w4_words[0].bitcast(I32))
         for r in range(4):
-            nc.sync.dma_start(tabs[r:P:32, :].bitcast(I32), tab_scales[0, r:16:4, :].bitcast(I32))
-        for r in range(4):
-            nc.sync.dma_start(w4s_raw[r:P:32, :].bitcast(I32), w4_scales[0, r:16:4, :].bitcast(I32))
-        nc.scalar.activation(warm2[:], warm[:], ACT.Sigmoid)
+            nc.sync.dma_start(tab_sc[r:P:32, :].bitcast(I32), tab_scales[0, r:16:4, :].bitcast(I32))
+        nc.scalar.activation(warm_out[:], warm_in[:], ACT.Sigmoid)
         nc.gpsimd.dma_start(bg_t[:], bg.rearrange("(b p t) -> p b t", b=2, t=4))
         nc.gpsimd.dma_start(amb_t[:], amb.rearrange("(b p t) -> p b t", b=2, t=4))
-        tabw = keep.tile([P, T], I32, name="tabw", tag="expo0", align_bytes=64)
-        nc.sync.dma_start(tabw[:], tab_words[0].rearrange("p t i -> p (t i)").bitcast(I32))
-        load_w1(0)
+        tab_w = keep.tile([P, T], I32, name="tab_w", tag="table", align_bytes=64)
+        nc.sync.dma_start(tab_w[:], tab_words[0].rearrange("p t i -> p (t i)").bitcast(I32))
+        halves = [slice(BANK * h, BANK * (h + 1)) for h in range(2)]
+        for r in range(4):
+            nc.sync.dma_start(w4s_raw[r:P:32, :].bitcast(I32), w4_scales[0, r:16:4, :].bitcast(I32))
 
         expo_t = {}
 
         def load_expo(j):
             b, u = divmod(j, 2)
-            expo_t[j] = keep.tile([P, 2, T2], F32, name=f"expo{j}", tag=("expo0", "raw0")[j % 2], align_bytes=64)
+            expo_t[j] = shared([P, 2, T2], f"expo{j}", ("table", "w1_first")[u])
             rows = expo[512 * b : 512 * (b + 1), :].rearrange("(p t) m -> p t m", t=4)
             nc.sync.dma_start(expo_t[j][:], rows[:, 2 * u : 2 * u + 2, :])
 
-
-        gw = [keep.tile([P, BANK], U32, name=f"gw{h}", align_bytes=64) for h in range(2)]
-        gs = [keep.tile([P, BANK], U8, name="gs0", align_bytes=64)]
-        halves = [slice(BANK * h, BANK * (h + 1)) for h in range(2)]
-        lists = [offs_t[:, 32 * h : 32 * (h + 1)] for h in range(2)]
+        got_w = [keep.tile([P, BANK], U32, name=f"got_w{h}", align_bytes=64) for h in range(2)]
+        got_s = [keep.tile([P, BANK], U8, name=f"got_s{h}", align_bytes=64) for h in range(2)]
+        list_cols = [slice(BANK // GROUP * h, BANK // GROUP * (h + 1)) for h in range(2)]
 
         nc.vector.tensor_copy(
             w4w[:].bitcast(U16).rearrange("p (b t m) -> p b t m", b=2, t=4),
             w4w_raw[:].bitcast(U16).rearrange("p (b m t) -> p b t m", b=2, t=4),
         )
-        wgs_t = keep.tile([P, S], F32, name="wgs_t", tag="wgs", align_bytes=64)
+        load_w1(0)
+        page1 = laid.tile([P, T2], F32, name="page1", align_bytes=64, offset=0)
+        nc.gpsimd.memset(page1[:], 0.0)
+        for h in range(2):
+            nc.vector.tensor_copy(got_s[h][:], tab_sc[:].indirect(offs_t[:, list_cols[h]]))
+        wgs_t = shared([P, S], "wgs_t", "wgs")
         for half in halves:
             nc.sync.dma_start(wgs_t[:, half], wgs[:, half])
-        gs.append(keep.tile([P, BANK], U8, name="gs1", align_bytes=64))
-        for h in range(2):
-            nc.vector.tensor_copy(gs[h][:], tabs[:].indirect(lists[h]))
-        nc.vector.tensor_copy(
-            w4s[:].rearrange("p (b t m) -> p b t m", b=2, t=4),
-            w4s_raw[:].rearrange("p (b m t) -> p b t m", b=2, t=4),
-        )
-        for h in range(2):
-            nc.vector.tensor_copy(gw[h][:], tabw[:].bitcast(U32).indirect(lists[h]))
         load_w1(1)
+        w4s_dealt = w4s_raw[:].rearrange("p (b m t) -> p b t m", b=2, t=4)
+        nc.vector.tensor_copy(w4s_first[:], w4s_dealt[:, 0, 0, :])
+        w4s = {0: w4s_first[:]}
+        for h in range(2):
+            nc.vector.tensor_copy(got_w[h][:], tab_w[:].bitcast(U32).indirect(offs_t[:, list_cols[h]]))
         pages = [page0, page1]
 
         ident = keep.tile([P, P], F32, name="ident")
@@ -114,240 +133,246 @@ def tile_list_reefer_yard_alarm_kernel(
 
         def turn_wgs():
             for h in range(2):
-                bank = psum.tile([P, 4, P], F32, name="wgs_bank", tag="pa")
+                bank = psum.tile([P, 4, P], F32, name="wgs_bank", tag="banks_a")
                 for q in range(4):
                     nc.tensor.transpose(bank[:, q, :], wgs_t[:, BANK * h + P * q : BANK * h + P * (q + 1)], ident[:])
-                nc.scalar.copy(wgs_col[h].rearrange("p (q g) -> p q g", g=8), bank[:, :, 0:P:16])
+                nc.scalar.copy(wgs_col[h].rearrange("p (q g) -> p q g", g=8), bank[:, :, 0:P:GROUP])
 
-        w1q, w1s = {}, {}
-        w1_whole = {}
+        w1_codes, w1_scales = {}, {}
 
         def prepare_w1(b, casts):
-            bf = keep.tile([P, 4, P, 4], BF16, name=f"w1bf{b}", tag=f"w1bf{b}", align_bytes=64)
-            q = keep.tile([P, 4 * P], U32, name=f"w1q{b}", align_bytes=64)
-            s = keep.tile([P, 4 * P], U8, name=f"w1s{b}", align_bytes=64)
-            src = w1raw[b][:].rearrange("p j (m t) -> p m t j", t=4)
+            rounded = laid.tile([P, 4, P, 4], BF16, name=f"w1_rounded{b}", align_bytes=64, offset=W1_ROUNDED_AT[b])
+            w1_codes[b] = keep.tile([P, 4 * P], U32, name=f"w1_codes{b}", align_bytes=64)
+            w1_scales[b] = keep.tile([P, 4 * P], U8, name=f"w1_scales{b}", align_bytes=64)
+            src = w1_raw[b][:].rearrange("p j (m t) -> p m t j", t=4)
             for cast, t0, t1 in casts:
-                cast(bf[:, t0:t1, :, :].rearrange("p t m j -> p m t j"), src[:, :, t0:t1, :])
-            nc.vector.quantize_mx(out=q[:].bitcast(FP8X4), scales=s[:], in_=bf[:].rearrange("p t m j -> p (t m j)"))
-            w1_whole[b] = (q, s)
-            for t in range(4):
-                w1q[4 * b + t] = q[:, t * P : (t + 1) * P]
-                w1s[4 * b + t] = s[:, t * P : (t + 1) * P]
+                cast(rounded[:, t0:t1, :, :].rearrange("p t m j -> p m t j"), src[:, :, t0:t1, :])
+            nc.vector.quantize_mx(
+                out=w1_codes[b][:].bitcast(FP8X4),
+                scales=w1_scales[b][:],
+                in_=rounded[:].rearrange("p t m j -> p (t m j)"),
+            )
 
         val = {}
+        val_on = {0: "w1_first", 1: "plane1_gate", 7: "z_codes0"}
 
         def trust(k, h):
             b, t = divmod(k, 4)
-            if h == 0 and k in (0, 1, 3, 7):
-                val[k] = keep.tile([P, S], F32, name=f"val{k}", tag={0: "raw0", 1: "w1bf0", 3: "w1bf1", 7: "zq0"}[k], align_bytes=64)
+            if h == 0 and k in val_on:
+                val[k] = shared([P, S], f"val{k}", val_on[k])
             elif h == 0:
-                val[k] = ring.tile([P, S], F32, name=f"val{k}", tag="q4", bufs=4, align_bytes=64)
-            acc = psum.tile([P, BANK], F32, name="acc_b", tag="pb", bufs=3)
+                val[k] = ring.tile([P, S], F32, name=f"val{k}", tag="val", bufs=4, align_bytes=64)
+            acc = psum.tile([P, BANK], F32, name="acc_b", tag="banks_b", bufs=BANKS_B)
             nc.tensor.matmul_mx(
                 out=acc[:],
-                lhsT=w4w[:, 256 * k : 256 * (k + 1)].bitcast(FP4X4),
-                lhsT_scale=w4s[:, P * k : P * (k + 1)],
-                rhs=gw[h][:].bitcast(FP8X4),
-                rhs_scale=gs[h][:],
+                lhsT=w4w[:, 2 * P * k : 2 * P * (k + 1)].bitcast(FP4X4),
+                lhsT_scale=w4s[k],
+                rhs=got_w[h][:].bitcast(FP8X4),
+                rhs_scale=got_s[h][:],
                 start=True,
                 stop=True,
             )
             nc.scalar.activation(val[k][:, halves[h]], acc[:], ACT.Sigmoid, bias=bg_t[:, b, t : t + 1])
 
         def deviation(k, h):
-            acc = psum.tile([P, BANK], F32, name="acc_a", tag="pa")
+            acc = psum.tile([P, BANK], F32, name="acc_a", tag="banks_a")
             nc.tensor.matmul_mx(
                 out=acc[:],
-                lhsT=w1q[k].bitcast(FP8X4),
-                lhsT_scale=w1s[k],
-                rhs=gw[h][:].bitcast(FP8X4),
-                rhs_scale=gs[h][:],
+                lhsT=w1_codes[0][:, P * k : P * (k + 1)].bitcast(FP8X4),
+                lhsT_scale=w1_scales[0][:, P * k : P * (k + 1)],
+                rhs=got_w[h][:].bitcast(FP8X4),
+                rhs_scale=got_s[h][:],
                 start=True,
                 stop=True,
             )
             return acc
 
-        aw = [keep.tile([P, 4, P], F32, name=f"aw{jt}", tag=f"aw{jt}") for jt in range(8)]
+        weighed = [keep.tile([P, 4, P], F32, name=f"weighed{e}", tag=f"weighed{e}") for e in range(S // P)]
 
-        def weighted_rows(jt):
-            h, q = divmod(jt, 4)
-            acc = psum.tile([P, 4, P], F32, name="acc_t", tag="pa")
+        def weigh_transposed(e):
+            h, q = divmod(e, 4)
+            acc = psum.tile([P, 4, P], F32, name="acc_t", tag="banks_a")
             nc.tensor.matmul_mx(
                 out=acc[:].rearrange("p t m -> p (t m)"),
-                lhsT=gw[h][:, P * q : P * (q + 1)].bitcast(FP8X4),
-                lhsT_scale=gs[h][:, P * q : P * (q + 1)],
-                rhs=w1_whole[1][0][:].bitcast(FP8X4),
-                rhs_scale=w1_whole[1][1][:],
+                lhsT=got_w[h][:, P * q : P * (q + 1)].bitcast(FP8X4),
+                lhsT_scale=got_s[h][:, P * q : P * (q + 1)],
+                rhs=w1_codes[1][:].bitcast(FP8X4),
+                rhs_scale=w1_scales[1][:],
                 start=True,
                 stop=True,
             )
             for g in range(8):
-                run = slice(16 * g, 16 * (g + 1))
-                nc.scalar.activation(aw[jt][:, :, run], acc[:, :, run], ACT.Copy, scale=wgs_col[h][:, 8 * q + g : 8 * q + g + 1])
+                run = slice(GROUP * g, GROUP * (g + 1))
+                weight = wgs_col[h][:, 8 * q + g : 8 * q + g + 1]
+                nc.scalar.activation(weighed[e][:, :, run], acc[:, :, run], ACT.Copy, scale=weight)
 
         def turned_back(k, h):
-            acc = psum.tile([P, BANK], F32, name="acc_r", tag="pa")
+            acc = psum.tile([P, BANK], F32, name="acc_r", tag="banks_a")
             for q in range(4):
-                nc.tensor.transpose(acc[:, P * q : P * (q + 1)], aw[4 * h + q][:, k - 4, :], ident[:])
+                nc.tensor.transpose(acc[:, P * q : P * (q + 1)], weighed[4 * h + q][:, k - 4, :], ident[:])
             return acc
 
         def factor(k, h):
             return deviation(k, h) if k < 4 else turned_back(k, h)
 
-        def weigh(eng, k, cols):
-            eng.tensor_tensor(val[k][:, cols], val[k][:, cols], wgs_t[:, cols], MULT)
-
-        def gate(k):
+        def weighed_gate(k):
             trust(k, 0)
             trust(k, 1)
-            weigh(nc.gpsimd, k, slice(0, S))
+            sigmoids = val[k]
+            if k > 1:
+                val[k] = shared([P, S], f"val{k}_weighed", f"plane{k}")
+            nc.gpsimd.tensor_tensor(val[k][:], sigmoids[:], wgs_t[:], MULT)
 
-        def times_a_on_vector(k, h):
+        def times_factor_on_vector(k, h):
             nc.vector.tensor_tensor(val[k][:, halves[h]], val[k][:, halves[h]], factor(k, h)[:], MULT)
 
-        def times_a_on_gpsimd(k):
+        def times_factor_on_gpsimd(k):
             if k < 3:
-                a_sb = ring.tile([P, S], F32, name="a_sb", tag="a_sb", bufs=3, align_bytes=64)[:]
+                copied = ring.tile([P, S], F32, name="copied", tag="stage", bufs=3, align_bytes=64)[:]
             else:
-                a_sb = zw[0][:, A_AT[k] : A_AT[k] + S]
+                copied = words[0][:, S * (k - 3) : S * (k - 2)]
             for h in range(2):
-                nc.scalar.copy(a_sb[:, halves[h]], factor(k, h)[:])
-            gated_rows = val[k]
+                nc.scalar.copy(copied[:, halves[h]], factor(k, h)[:])
+            gate = val[k]
             if k == 1:
-                val[k] = keep.tile([P, S], F32, name="val1_done", tag="raw1", align_bytes=64)
-            nc.gpsimd.tensor_tensor(val[k][:], gated_rows[:], a_sb, MULT)
+                val[k] = shared([P, S], "val1_done", "w1_second")
+            nc.gpsimd.tensor_tensor(val[k][:], gate[:], copied, MULT)
+
+        def gated_on_gpsimd(k):
+            trust(k, 0)
+            trust(k, 1)
+            times_factor_on_gpsimd(k)
 
         def place(k):
             nc.vector.tensor_copy(pages[k % 2][:].indirect(offs2_t[:]), val[k][:])
 
-        def level(k, dst, cols):
-            b, t = divmod(k, 4)
-            nc.scalar.activation(dst, pages[k % 2][:, cols], ACT.Identity, bias=amb_t[:, b, t : t + 1])
-
-        def expose(eng, dst_words, lev, ex):
-            eng.tensor_tensor(
-                dst_words.bitcast(BF16).rearrange("p (c i t) -> p c t i", i=4, t=2),
-                lev.rearrange("p t (c i) -> p c t i", i=4),
-                ex.rearrange("p t (c i) -> p c t i", i=4),
-                MULT,
-            )
-
-        zw = [keep.tile([P, 2 * T2], F32, name=f"zw{b}", tag=f"zw{b}") for b in range(2)]
-        late = keep.tile([P, 3 * T2], F32, name="late")
+        words = [keep.tile([P, 2 * T2], F32, name=f"words{b}", tag=f"words{b}") for b in range(2)]
+        late_lev = keep.tile([P, 3 * T2], F32, name="late_lev")
         lev = {
             0: lev0[:],
-            2: late[:, T2 : 3 * T2].rearrange("p (t m) -> p t m", t=2),
-            3: late[:, 0 : 2 * T2].rearrange("p (t m) -> p t m", t=2),
+            2: late_lev[:, T2 : 3 * T2].rearrange("p (t m) -> p t m", t=2),
+            3: late_lev[:, 0 : 2 * T2].rearrange("p (t m) -> p t m", t=2),
         }
 
-        def pair_words(j, cols):
-            return zw[j // 2][:, T2 * (j % 2) + cols.start : T2 * (j % 2) + cols.stop]
-
-        def both_pairs(b, cols):
-            return zw[b][:].rearrange("p (u m) -> p m u", u=2)[:, cols, :]
-
-        def level_whole(k):
+        def level(k, cols):
+            b, t = divmod(k, 4)
             j, u = divmod(k, 2)
             if j not in lev:
                 lev[j] = ring.tile([P, 2, T2], F32, name=f"lev{j}", tag="lev", align_bytes=64)[:]
-            level(k, lev[j][:, u, :], slice(0, T2))
+            nc.scalar.activation(lev[j][:, u, cols], pages[u][:, cols], ACT.Identity, bias=amb_t[:, b, t : t + 1])
 
-        def expose_cols(eng, j, cols):
-            expose(eng, pair_words(j, cols), lev[j][:, :, cols], expo_t[j][:, :, cols])
+        def expose(eng, j, cols):
+            at = T2 * (j % 2)
+            eng.tensor_tensor(
+                words[j // 2][:, at + cols.start : at + cols.stop].bitcast(BF16).rearrange("p (c i t) -> p c t i", i=4, t=2),
+                lev[j][:, :, cols].rearrange("p t (c i) -> p c t i", i=4),
+                expo_t[j][:, :, cols].rearrange("p t (c i) -> p c t i", i=4),
+                MULT,
+            )
 
         def expose_half(j, half):
-            expose_cols(nc.gpsimd, j, slice((0, (1536, 1024)[j], T2)[half], (0, (1536, 1024)[j], T2)[half + 1]))
+            expose(nc.gpsimd, j, slice(T2 // 2 * half, T2 // 2 * (half + 1)))
             if half == 1:
                 load_expo(j + 2)
 
+        def both_pairs(b, cols):
+            return words[b][:].rearrange("p (u m) -> p m u", u=2)[:, cols, :]
+
+        all_cols = slice(0, T2)
+
         prepare_w1(0, [(nc.scalar.copy, 0, 2), (nc.vector.tensor_copy, 2, 4)])
+        w4s_late = laid.tile([P, 8, P], U8, name="w4s_late", align_bytes=64, offset=W4_SCALES_LATE_AT)
+        nc.vector.tensor_copy(w4s_late[:, 1:4, :], w4s_dealt[:, 0, 1:4, :])
+        nc.vector.tensor_copy(w4s_late[:, 4:8, :], w4s_dealt[:, 1, :, :])
+        for k in range(1, 8):
+            w4s[k] = w4s_late[:, k, :]
         load_expo(0)
         trust(0, 0)
         trust(0, 1)
-        for h in range(2):
-            weigh((nc.vector, nc.gpsimd)[h], 0, halves[h])
-            times_a_on_vector(0, h)
-            nc.vector.tensor_copy(page0[:].indirect(offs2_t[:, 32 * h : 32 * (h + 1)]), val[0][:, halves[h]])
+        for h, eng in enumerate((nc.vector, nc.gpsimd)):
+            eng.tensor_tensor(val[0][:, halves[h]], val[0][:, halves[h]], wgs_t[:, halves[h]], MULT)
+            times_factor_on_vector(0, h)
+            nc.vector.tensor_copy(page0[:].indirect(offs2_t[:, list_cols[h]]), val[0][:, halves[h]])
         load_expo(1)
-        gate(1)
-        gate(2)
+
+        weighed_gate(1)
         prepare_w1(1, [(nc.scalar.copy, 0, 4)])
-        times_a_on_gpsimd(1)
-        times_a_on_gpsimd(2)
+        times_factor_on_gpsimd(1)
+        weighed_gate(2)
+        times_factor_on_gpsimd(2)
         place(1)
         turn_wgs()
-        gate(3)
-        times_a_on_gpsimd(3)
-        level_whole(0)
+        weighed_gate(3)
+        times_factor_on_gpsimd(3)
+        level(0, all_cols)
         place(2)
-        for jt in range(4):
-            weighted_rows(jt)
-        level_whole(1)
+        for e in range(4):
+            weigh_transposed(e)
+        level(1, all_cols)
         expose_half(0, 0)
-        for jt in range(4, 8):
-            weighted_rows(jt)
+        for e in range(4, 8):
+            weigh_transposed(e)
         place(3)
-        w8w = keep.tile([P, 2, N], I32, name="w8w", tag="raw1", align_bytes=64)
+
+        w8w = laid.tile([P, 2, N], I32, name="w8w", tag="w1_second", align_bytes=64, offset=LAID_AT["w1_second"])
         nc.sync.dma_start(w8w[:], w8_words.rearrange("a p c i -> p a (c i)").bitcast(I32))
-        w8s = w1_whole[0][1]
+        w8s = w1_scales[0]
         for quad in range(4):
             nc.sync.dma_start(
                 w8s[32 * quad + 4 : 32 * quad + 12, 0:N].bitcast(I32),
                 w8_scales[:, 4 * quad : 4 * quad + 4, :].bitcast(I32),
             )
 
-        def gated(k):
-            trust(k, 0)
-            trust(k, 1)
-            times_a_on_gpsimd(k)
-
-        gated(4)
+        gated_on_gpsimd(4)
         expose_half(0, 1)
-        level_whole(2)
+        level(2, all_cols)
         place(4)
-        gated(5)
-        level_whole(3)
+        gated_on_gpsimd(5)
+        level(3, all_cols)
         expose_half(1, 0)
         place(5)
-        gated(6)
+        gated_on_gpsimd(6)
         expose_half(1, 1)
         trust(7, 0)
         trust(7, 1)
-        level_whole(4)
+        level(4, all_cols)
         place(6)
-        level_whole(5)
-        expose_cols(nc.gpsimd, 2, slice(0, T2))
-        zb0 = ring.tile([P, T2, 2], F32, name="zb0", tag="lev", align_bytes=64)
-        for c in range(CHUNKS):
+        level(5, all_cols)
+        expose(nc.gpsimd, 2, all_cols)
+        woven0 = ring.tile([P, T2, 2], F32, name="woven0", tag="lev", align_bytes=64)
+        for c in range(T2 // BANK):
             cols = slice(BANK * c, BANK * (c + 1))
-            nc.scalar.copy(zb0[:, cols, :], both_pairs(0, cols))
-
-        level_whole(6)
+            nc.scalar.copy(woven0[:, cols, :], both_pairs(0, cols))
+        level(6, all_cols)
         for h in range(2):
-            times_a_on_vector(7, h)
+            times_factor_on_vector(7, h)
         place(7)
 
-        zq = [keep.tile([P, T2], U32, name=f"zq{b}", tag=f"zq{b}", align_bytes=64) for b in range(2)]
-        zs = [keep.tile([P, T2], U8, name=f"zs{b}", tag=("expo0", "zs1")[b], align_bytes=64) for b in range(2)]
+        z_codes = [keep.tile([P, T2], U32, name=f"z_codes{b}", tag=f"z_codes{b}", align_bytes=64) for b in range(2)]
+        z_scales = [
+            keep.tile([P, T2], U8, name=f"z_scales{b}", tag=("table", "z_scales1")[b], align_bytes=64) for b in range(2)
+        ]
 
-        def quantise(b, cols, words):
-            q, s = zq[b][:, cols], zs[b][:, cols]
-            nc.vector.quantize_mx(out=q.bitcast(FP8X4), scales=s, in_=words.rearrange("p m u -> p (m u)").bitcast(BF16))
-            return q, s
+        def quantise(b, cols, woven):
+            codes, scales = z_codes[b][:, cols], z_scales[b][:, cols]
+            nc.vector.quantize_mx(
+                out=codes.bitcast(FP8X4), scales=scales, in_=woven.rearrange("p m u -> p (m u)").bitcast(BF16)
+            )
+            return codes, scales
 
-        pieces = [(0, 256), (256, 512), (768, 512), (1280, 256), (1536, 256), (1792, 256)]
-        spare = keep.tile([P, 2 * T2], F32, name="spare", tag="zw0")
+        spare = keep.tile([P, 2 * T2], F32, name="spare", tag="words0")
         used = 0
-        for i, (m0, width) in enumerate(pieces):
+        for i, (m0, width) in enumerate(PIECES):
             cols = slice(m0, m0 + width)
-            level(7, lev[3][:, 1, cols], cols)
-            z = [quantise(0, cols, zb0[:, cols, :])]
-            expose_cols(nc.vector, 3, cols)
-            zb = ring.tile([P, width, 2], F32, name="zb1", tag="a_sb", bufs=3, align_bytes=64)
-            (nc.scalar.copy if i in SW else nc.vector.tensor_copy)(zb[:], both_pairs(1, cols))
-            z.append(quantise(1, cols, zb[:]))
-            accs = [psum.tile([P, width], F32, name="acc_o", tag=("pa", "pb", "pa")[nb], bufs=(5, 3, 5)[nb]) for nb in range(N // P)]
+            level(7, cols)
+            z = [quantise(0, cols, woven0[:, cols, :])]
+            expose(nc.vector, 3, cols)
+            woven1 = ring.tile([P, width, 2], F32, name="woven1", tag="stage", bufs=3, align_bytes=64)
+            weave = nc.scalar.copy if i in SCALAR_WEAVES else nc.vector.tensor_copy
+            weave(woven1[:], both_pairs(1, cols))
+            z.append(quantise(1, cols, woven1[:]))
+            bank_sets = [("banks_a", BANKS_A), ("banks_b", BANKS_B), ("banks_a", BANKS_A)]
+            accs = [psum.tile([P, width], F32, name="acc_o", tag=tag, bufs=bufs) for tag, bufs in bank_sets]
             for b in range(2):
                 for nb in range(N // P):
                     nc.tensor.matmul_mx(
@@ -360,13 +385,14 @@ def tile_list_reefer_yard_alarm_kernel(
                         stop=(b == 1),
                     )
             for nb in range(N // P):
-                if 3 * i + nb < 8:
-                    res = keep.tile([P, width], F32, name="res", tag=f"aw{3 * i + nb}")
+                store = i * (N // P) + nb
+                if store < len(weighed):
+                    res = keep.tile([P, width], F32, name="res", tag=f"weighed{store}")[:]
                 else:
                     res = spare[:, used : used + width]
                     used = used + width
-                if i == len(pieces) - 1 and nb > 0:
-                    nc.vector.tensor_copy(res[:], accs[nb][:])
+                if i == len(PIECES) - 1 and nb > 0:
+                    nc.vector.tensor_copy(res, accs[nb][:])
                 else:
-                    nc.scalar.copy(res[:], accs[nb][:])
-                nc.sync.dma_start(out[P * nb : P * (nb + 1), cols], res[:])
+                    nc.scalar.copy(res, accs[nb][:])
+                nc.sync.dma_start(out[P * nb : P * (nb + 1), cols], res)

@@ -24,17 +24,22 @@ BANKS_A, BANKS_B = 5, 3
 KIB = 1024
 
 LAID_AT = {
-    "w1_first": 8 * KIB,
-    "plane2": 24 * KIB,
-    "plane3": 28 * KIB,
-    "plane1_gate": 33 * KIB,
-    "wgs": 37 * KIB,
-    "w1_second": 41 * KIB,
+    "wgs": 8 * KIB,
+    "w1_second": 12 * KIB,
+    "w1_first": 23 * KIB,
+    "plane2": 42 * KIB,
+    "plane3": 46 * KIB,
+    "plane1_gate": 50 * KIB,
 }
-W4_RAW_AT = 7 * KIB
-W1_ROUNDED_AT = (32 * KIB, 26 * KIB)
-TAB_SCALES_AT = 40 * KIB
-W4_SCALES_LATE_AT = 32 * KIB
+W4_DEALT_AT = 20 * KIB
+W4_SCALES_RAW_AT = 22 * KIB
+W1_CODES_AT = 39 * KIB
+GOT_LATE_AT = 41 * KIB
+W4_RAW_AT, W4_RAW_BYTES = 8 * KIB - 64, 64 + 4 * KIB + 64
+W1_ROUNDED_AT = {0: 50 * KIB, 2: 42 * KIB, 4: 44 * KIB}
+WARM_AT = 22 * KIB - 64
+W4_FIRST_AT = 41 * KIB - 64
+SPAN = 64 + KIB + 64
 
 PIECES = [(0, 256), (256, 512), (768, 512), (1280, 256), (1536, 256), (1792, 256)]
 SCALAR_WEAVES = (1, 2)
@@ -57,21 +62,18 @@ def tile_list_reefer_yard_alarm_kernel(
 
         offs_t = keep.tile([P, S // GROUP], U16, name="offs_t")
         offs2_t = keep.tile([P, S // GROUP], U16, name="offs2_t")
-        warm_in = keep.tile([P, 8], F32, name="warm_in", tag="table", align_bytes=64)
-        tab_sc = laid.tile([P, T], U8, name="tab_sc", align_bytes=64, offset=TAB_SCALES_AT)
-        w4s_raw = keep.tile([P, H], U8, name="w4s_raw", align_bytes=64)
-        w4w_raw = laid.tile([P, 2 * H], U8, name="w4w_raw", align_bytes=64, offset=W4_RAW_AT)
-        w4w = keep.tile([P, 2 * H], U8, name="w4w", align_bytes=64)
-        w4s_first = keep.tile([P, P], U8, name="w4s_first", align_bytes=64)
+        warm_in = laid.tile([P, SPAN // 4], F32, name="warm_in", align_bytes=64, offset=WARM_AT)
+        tab_sc = keep.tile([P, T], U8, name="tab_sc", tag="z_scales1", align_bytes=64)
+        w4w_raw = laid.tile([P, W4_RAW_BYTES], U8, name="w4w_raw", align_bytes=64, offset=W4_RAW_AT)
+        w4s_first = laid.tile([P, SPAN], U8, name="w4s_first", align_bytes=64, offset=W4_FIRST_AT)
         bg_t = keep.tile([P, 2, 4], F32, name="bg_t")
         amb_t = keep.tile([P, 2, 4], F32, name="amb_t")
         warm_out = keep.tile([P, 8], F32, name="warm_out")
         page0 = keep.tile([P, T2], F32, name="page0")
 
-        nc.vector.memset(warm_in[:], 0.0)
+        nc.vector.memset(warm_in[:, 0:8], 0.0)
         nc.vector.memset(tab_sc[:].bitcast(I32), 0)
         nc.vector.memset(page0[:], 0.0)
-        nc.vector.memset(w4s_raw[:].bitcast(I32), 0)
 
         w1_raw = {}
 
@@ -81,15 +83,18 @@ def tile_list_reefer_yard_alarm_kernel(
 
         nc.sync.dma_start(offs_t[:], offs)
         nc.sync.dma_start(offs2_t[:], offs2)
-        nc.sync.dma_start(w4w_raw[:].bitcast(I32), w4_words[0].bitcast(I32))
-        for r in range(4):
-            nc.sync.dma_start(tab_sc[r:P:32, :].bitcast(I32), tab_scales[0, r:16:4, :].bitcast(I32))
-        nc.scalar.activation(warm_out[:], warm_in[:], ACT.Sigmoid)
-        nc.gpsimd.dma_start(bg_t[:], bg.rearrange("(b p t) -> p b t", b=2, t=4))
-        nc.gpsimd.dma_start(amb_t[:], amb.rearrange("(b p t) -> p b t", b=2, t=4))
+        nc.sync.dma_start(w4w_raw[:, 0 : 2 * H].bitcast(I32), w4_words[0].bitcast(I32))
         tab_w = keep.tile([P, T], I32, name="tab_w", tag="table", align_bytes=64)
         nc.sync.dma_start(tab_w[:], tab_words[0].rearrange("p t i -> p (t i)").bitcast(I32))
+        for r in range(4):
+            nc.sync.dma_start(tab_sc[r:P:32, :].bitcast(I32), tab_scales[0, r:16:4, :].bitcast(I32))
+        nc.scalar.activation(warm_out[:], warm_in[:, 0:8], ACT.Sigmoid)
+        nc.gpsimd.dma_start(bg_t[:], bg.rearrange("(b p t) -> p b t", b=2, t=4))
+        nc.gpsimd.dma_start(amb_t[:], amb.rearrange("(b p t) -> p b t", b=2, t=4))
+        load_w1(0)
         halves = [slice(BANK * h, BANK * (h + 1)) for h in range(2)]
+        w4s_raw = laid.tile([P, H], U8, name="w4s_raw", align_bytes=64, offset=W4_SCALES_RAW_AT)
+        nc.vector.memset(w4s_raw[:].bitcast(I32), 0)
         for r in range(4):
             nc.sync.dma_start(w4s_raw[r:P:32, :].bitcast(I32), w4_scales[0, r:16:4, :].bitcast(I32))
 
@@ -102,27 +107,28 @@ def tile_list_reefer_yard_alarm_kernel(
             nc.sync.dma_start(expo_t[j][:], rows[:, 2 * u : 2 * u + 2, :])
 
         got_w = [keep.tile([P, BANK], U32, name=f"got_w{h}", align_bytes=64) for h in range(2)]
-        got_s = [keep.tile([P, BANK], U8, name=f"got_s{h}", align_bytes=64) for h in range(2)]
+        got_s = [keep.tile([P, BANK], U8, name="got_s0", align_bytes=64)]
         list_cols = [slice(BANK // GROUP * h, BANK // GROUP * (h + 1)) for h in range(2)]
 
+        w4w = laid.tile([P, 2 * H], U8, name="w4w", align_bytes=64, offset=W4_DEALT_AT)
         nc.vector.tensor_copy(
             w4w[:].bitcast(U16).rearrange("p (b t m) -> p b t m", b=2, t=4),
-            w4w_raw[:].bitcast(U16).rearrange("p (b m t) -> p b t m", b=2, t=4),
+            w4w_raw[:, 0 : 2 * H].bitcast(U16).rearrange("p (b m t) -> p b t m", b=2, t=4),
         )
-        load_w1(0)
-        page1 = laid.tile([P, T2], F32, name="page1", align_bytes=64, offset=0)
-        nc.gpsimd.memset(page1[:], 0.0)
-        for h in range(2):
-            nc.vector.tensor_copy(got_s[h][:], tab_sc[:].indirect(offs_t[:, list_cols[h]]))
         wgs_t = shared([P, S], "wgs_t", "wgs")
         for half in halves:
             nc.sync.dma_start(wgs_t[:, half], wgs[:, half])
+        page1 = laid.tile([P, T2], F32, name="page1", align_bytes=64, offset=0)
+        nc.gpsimd.memset(page1[:], 0.0)
         load_w1(1)
+        nc.vector.tensor_copy(got_w[0][:], tab_w[:].bitcast(U32).indirect(offs_t[:, list_cols[0]]))
+        nc.vector.tensor_copy(got_s[0][:], tab_sc[:].indirect(offs_t[:, list_cols[0]]))
+        nc.vector.tensor_copy(got_w[1][:], tab_w[:].bitcast(U32).indirect(offs_t[:, list_cols[1]]))
         w4s_dealt = w4s_raw[:].rearrange("p (b m t) -> p b t m", b=2, t=4)
-        nc.vector.tensor_copy(w4s_first[:], w4s_dealt[:, 0, 0, :])
-        w4s = {0: w4s_first[:]}
-        for h in range(2):
-            nc.vector.tensor_copy(got_w[h][:], tab_w[:].bitcast(U32).indirect(offs_t[:, list_cols[h]]))
+        nc.vector.tensor_copy(w4s_first[:, 0:P], w4s_dealt[:, 0, 0, :])
+        w4s = {0: w4s_first[:, 0:P]}
+        w4s_late = keep.tile([P, 8, P], U8, name="w4s_late", align_bytes=64)
+        nc.vector.tensor_copy(w4s_late[:].rearrange("p (b t) m -> p b t m", b=2), w4s_dealt)
         pages = [page0, page1]
 
         ident = keep.tile([P, P], F32, name="ident")
@@ -138,23 +144,26 @@ def tile_list_reefer_yard_alarm_kernel(
                     nc.tensor.transpose(bank[:, q, :], wgs_t[:, BANK * h + P * q : BANK * h + P * (q + 1)], ident[:])
                 nc.scalar.copy(wgs_col[h].rearrange("p (q g) -> p q g", g=8), bank[:, :, 0:P:GROUP])
 
-        w1_codes, w1_scales = {}, {}
+        w1_codes = [
+            laid.tile([P, 4 * P], U32, name="w1_codes0", align_bytes=64, offset=W1_CODES_AT),
+            keep.tile([P, 4 * P], U32, name="w1_codes1", align_bytes=64),
+        ]
+        w1_scales = [keep.tile([P, 4 * P], U8, name=f"w1_scales{b}", align_bytes=64) for b in range(2)]
 
-        def prepare_w1(b, casts):
-            rounded = laid.tile([P, 4, P, 4], BF16, name=f"w1_rounded{b}", align_bytes=64, offset=W1_ROUNDED_AT[b])
-            w1_codes[b] = keep.tile([P, 4 * P], U32, name=f"w1_codes{b}", align_bytes=64)
-            w1_scales[b] = keep.tile([P, 4 * P], U8, name=f"w1_scales{b}", align_bytes=64)
+        def prepare_w1(k0, k1):
+            b, t0 = divmod(k0, 4)
+            t1 = t0 + k1 - k0
+            rounded = laid.tile([P, k1 - k0, P, 4], BF16, name=f"w1_rounded{k0}", align_bytes=64, offset=W1_ROUNDED_AT[k0])
             src = w1_raw[b][:].rearrange("p j (m t) -> p m t j", t=4)
-            for cast, t0, t1 in casts:
-                cast(rounded[:, t0:t1, :, :].rearrange("p t m j -> p m t j"), src[:, :, t0:t1, :])
+            nc.scalar.copy(rounded[:].rearrange("p t m j -> p m t j"), src[:, :, t0:t1, :])
             nc.vector.quantize_mx(
-                out=w1_codes[b][:].bitcast(FP8X4),
-                scales=w1_scales[b][:],
+                out=w1_codes[b][:, P * t0 : P * t1].bitcast(FP8X4),
+                scales=w1_scales[b][:, P * t0 : P * t1],
                 in_=rounded[:].rearrange("p t m j -> p (t m j)"),
             )
 
         val = {}
-        val_on = {0: "w1_first", 1: "plane1_gate", 7: "z_codes0"}
+        val_on = {0: "z_codes1", 1: "plane1_gate", 7: "z_codes0"}
 
         def trust(k, h):
             b, t = divmod(k, 4)
@@ -280,23 +289,23 @@ def tile_list_reefer_yard_alarm_kernel(
 
         all_cols = slice(0, T2)
 
-        prepare_w1(0, [(nc.scalar.copy, 0, 2), (nc.vector.tensor_copy, 2, 4)])
-        w4s_late = laid.tile([P, 8, P], U8, name="w4s_late", align_bytes=64, offset=W4_SCALES_LATE_AT)
-        nc.vector.tensor_copy(w4s_late[:, 1:4, :], w4s_dealt[:, 0, 1:4, :])
-        nc.vector.tensor_copy(w4s_late[:, 4:8, :], w4s_dealt[:, 1, :, :])
-        for k in range(1, 8):
+        trust(0, 0)
+        prepare_w1(0, 2)
+        got_s.append(laid.tile([P, BANK], U8, name="got_s1", align_bytes=64, offset=GOT_LATE_AT))
+        nc.vector.tensor_copy(got_s[1][:], tab_sc[:].indirect(offs_t[:, list_cols[1]]))
+        prepare_w1(2, 4)
+        for k in range(8):
             w4s[k] = w4s_late[:, k, :]
         load_expo(0)
-        trust(0, 0)
         trust(0, 1)
-        for h, eng in enumerate((nc.vector, nc.gpsimd)):
-            eng.tensor_tensor(val[0][:, halves[h]], val[0][:, halves[h]], wgs_t[:, halves[h]], MULT)
+        for h in range(2):
+            nc.gpsimd.tensor_tensor(val[0][:, halves[h]], val[0][:, halves[h]], wgs_t[:, halves[h]], MULT)
             times_factor_on_vector(0, h)
             nc.vector.tensor_copy(page0[:].indirect(offs2_t[:, list_cols[h]]), val[0][:, halves[h]])
         load_expo(1)
 
         weighed_gate(1)
-        prepare_w1(1, [(nc.scalar.copy, 0, 4)])
+        prepare_w1(4, 8)
         times_factor_on_gpsimd(1)
         weighed_gate(2)
         times_factor_on_gpsimd(2)
@@ -337,8 +346,10 @@ def tile_list_reefer_yard_alarm_kernel(
         trust(7, 1)
         level(4, all_cols)
         place(6)
-        level(5, all_cols)
-        expose(nc.gpsimd, 2, all_cols)
+        for half in range(2):
+            cols = slice(T2 // 2 * half, T2 // 2 * (half + 1))
+            level(5, cols)
+            expose(nc.gpsimd, 2, cols)
         woven0 = ring.tile([P, T2, 2], F32, name="woven0", tag="lev", align_bytes=64)
         for c in range(T2 // BANK):
             cols = slice(BANK * c, BANK * (c + 1))

@@ -22,6 +22,7 @@ BANK = 512
 GROUP = 16
 BANKS_A, BANKS_B = 5, 3
 KIB = 1024
+WIDE = 1024
 
 LAID_AT = {
     "wgs": 8 * KIB,
@@ -41,7 +42,7 @@ WARM_AT = 22 * KIB - 64
 W4_FIRST_AT = 41 * KIB - 64
 SPAN = 64 + KIB + 64
 
-PIECES = [(0, 256), (256, 512), (768, 512), (1280, 256), (1536, 256), (1792, 256)]
+PIECES = [(0, 256), (256, 512), (768, 512), (1280, 512), (1792, 256)]
 SCALAR_WEAVES = (1, 2)
 
 
@@ -345,6 +346,8 @@ def tile_list_reefer_yard_alarm_kernel(
         trust(7, 0)
         trust(7, 1)
         level(4, all_cols)
+        nc.scalar.copy(words[1][:, halves[0]], factor(7, 0)[:])
+        nc.gpsimd.tensor_tensor(val[7][:, halves[0]], val[7][:, halves[0]], words[1][:, halves[0]], MULT)
         place(6)
         for half in range(2):
             cols = slice(T2 // 2 * half, T2 // 2 * (half + 1))
@@ -355,8 +358,7 @@ def tile_list_reefer_yard_alarm_kernel(
             cols = slice(BANK * c, BANK * (c + 1))
             nc.scalar.copy(woven0[:, cols, :], both_pairs(0, cols))
         level(6, all_cols)
-        for h in range(2):
-            times_factor_on_vector(7, h)
+        times_factor_on_vector(7, 1)
         place(7)
 
         z_codes = [keep.tile([P, T2], U32, name=f"z_codes{b}", tag=f"z_codes{b}", align_bytes=64) for b in range(2)]
@@ -376,7 +378,11 @@ def tile_list_reefer_yard_alarm_kernel(
         for i, (m0, width) in enumerate(PIECES):
             cols = slice(m0, m0 + width)
             level(7, cols)
-            z = [quantise(0, cols, woven0[:, cols, :])]
+            if m0 // WIDE != (m0 + width) // WIDE or m0 == 0:
+                wide = slice(WIDE * ((m0 + width) // WIDE), WIDE * ((m0 + width) // WIDE + 1))
+                if wide.stop <= T2:
+                    quantise(0, wide, woven0[:, wide, :])
+            z = [(z_codes[0][:, cols], z_scales[0][:, cols])]
             expose(nc.vector, 3, cols)
             woven1 = ring.tile([P, width, 2], F32, name="woven1", tag="stage", bufs=3, align_bytes=64)
             weave = nc.scalar.copy if i in SCALAR_WEAVES else nc.vector.tensor_copy

@@ -28,16 +28,20 @@ LAID_AT = {
     "wgs": 8 * KIB,
     "w1_second": 12 * KIB,
     "w1_first": 23 * KIB,
+    "plane1": 12 * KIB,
+    "plane2_gate": 16 * KIB,
     "plane2": 42 * KIB,
-    "plane3": 46 * KIB,
-    "plane1_gate": 50 * KIB,
+    "plane3": 54 * KIB - 64,
+    "plane1_gate": 58 * KIB - 64,
+    "z_codes1": 54 * KIB,
 }
 W4_DEALT_AT = 20 * KIB
 W4_SCALES_RAW_AT = 22 * KIB
 W1_CODES_AT = 39 * KIB
 GOT_LATE_AT = 41 * KIB
 W4_RAW_AT, W4_RAW_BYTES = 8 * KIB - 64, 64 + 4 * KIB + 64
-W1_ROUNDED_AT = {0: 50 * KIB, 2: 42 * KIB, 4: 44 * KIB}
+W1_ROUNDED_AT = {0: 44 * KIB - 64, 2: 42 * KIB, 4: 44 * KIB}
+W1_ROUNDED_BYTES = {0: 64 + 4 * KIB + 64, 2: 2 * KIB, 4: 4 * KIB}
 WARM_AT = 22 * KIB - 64
 W4_FIRST_AT = 41 * KIB - 64
 SPAN = 64 + KIB + 64
@@ -66,14 +70,17 @@ def tile_list_reefer_yard_alarm_kernel(
         warm_in = laid.tile([P, SPAN // 4], F32, name="warm_in", align_bytes=64, offset=WARM_AT)
         tab_sc = keep.tile([P, T], U8, name="tab_sc", tag="z_scales1", align_bytes=64)
         w4w_raw = laid.tile([P, W4_RAW_BYTES], U8, name="w4w_raw", align_bytes=64, offset=W4_RAW_AT)
-        w4s_first = laid.tile([P, SPAN], U8, name="w4s_first", align_bytes=64, offset=W4_FIRST_AT)
         bg_t = keep.tile([P, 2, 4], F32, name="bg_t")
         amb_t = keep.tile([P, 2, 4], F32, name="amb_t")
         warm_out = keep.tile([P, 8], F32, name="warm_out")
         page0 = keep.tile([P, T2], F32, name="page0")
 
+        zeros = keep.tile([P, H // 4], I32, name="zeros", tag="table", align_bytes=64)
+        w4s_raw = keep.tile([P, H], U8, name="w4s_raw", tag="got_w1", align_bytes=64)
+        nc.vector.memset(zeros[:], 0)
         nc.vector.memset(warm_in[:, 0:8], 0.0)
         nc.vector.memset(tab_sc[:].bitcast(I32), 0)
+        nc.vector.tensor_copy(w4s_raw[:].bitcast(I32), zeros[:])
         nc.vector.memset(page0[:], 0.0)
 
         w1_raw = {}
@@ -85,19 +92,17 @@ def tile_list_reefer_yard_alarm_kernel(
         nc.sync.dma_start(offs_t[:], offs)
         nc.sync.dma_start(offs2_t[:], offs2)
         nc.sync.dma_start(w4w_raw[:, 0 : 2 * H].bitcast(I32), w4_words[0].bitcast(I32))
+        for r in range(4):
+            nc.sync.dma_start(tab_sc[r:P:32, :].bitcast(I32), tab_scales[0, r:16:4, :].bitcast(I32))
         tab_w = keep.tile([P, T], I32, name="tab_w", tag="table", align_bytes=64)
         nc.sync.dma_start(tab_w[:], tab_words[0].rearrange("p t i -> p (t i)").bitcast(I32))
         for r in range(4):
-            nc.sync.dma_start(tab_sc[r:P:32, :].bitcast(I32), tab_scales[0, r:16:4, :].bitcast(I32))
+            nc.sync.dma_start(w4s_raw[r:P:32, :].bitcast(I32), w4_scales[0, r:16:4, :].bitcast(I32))
         nc.scalar.activation(warm_out[:], warm_in[:, 0:8], ACT.Sigmoid)
         nc.gpsimd.dma_start(bg_t[:], bg.rearrange("(b p t) -> p b t", b=2, t=4))
         nc.gpsimd.dma_start(amb_t[:], amb.rearrange("(b p t) -> p b t", b=2, t=4))
         load_w1(0)
         halves = [slice(BANK * h, BANK * (h + 1)) for h in range(2)]
-        w4s_raw = laid.tile([P, H], U8, name="w4s_raw", align_bytes=64, offset=W4_SCALES_RAW_AT)
-        nc.vector.memset(w4s_raw[:].bitcast(I32), 0)
-        for r in range(4):
-            nc.sync.dma_start(w4s_raw[r:P:32, :].bitcast(I32), w4_scales[0, r:16:4, :].bitcast(I32))
 
         expo_t = {}
 
@@ -107,8 +112,8 @@ def tile_list_reefer_yard_alarm_kernel(
             rows = expo[512 * b : 512 * (b + 1), :].rearrange("(p t) m -> p t m", t=4)
             nc.sync.dma_start(expo_t[j][:], rows[:, 2 * u : 2 * u + 2, :])
 
-        got_w = [keep.tile([P, BANK], U32, name=f"got_w{h}", align_bytes=64) for h in range(2)]
-        got_s = [keep.tile([P, BANK], U8, name="got_s0", align_bytes=64)]
+        got_w = [keep.tile([P, BANK], U32, name="got_w0", align_bytes=64)]
+        got_s = [keep.tile([P, BANK], U8, name=f"got_s{h}", align_bytes=64) for h in range(2)]
         list_cols = [slice(BANK // GROUP * h, BANK // GROUP * (h + 1)) for h in range(2)]
 
         w4w = laid.tile([P, 2 * H], U8, name="w4w", align_bytes=64, offset=W4_DEALT_AT)
@@ -122,14 +127,14 @@ def tile_list_reefer_yard_alarm_kernel(
         page1 = laid.tile([P, T2], F32, name="page1", align_bytes=64, offset=0)
         nc.gpsimd.memset(page1[:], 0.0)
         load_w1(1)
+        for h in range(2):
+            nc.vector.tensor_copy(got_s[h][:], tab_sc[:].indirect(offs_t[:, list_cols[h]]))
         nc.vector.tensor_copy(got_w[0][:], tab_w[:].bitcast(U32).indirect(offs_t[:, list_cols[0]]))
-        nc.vector.tensor_copy(got_s[0][:], tab_sc[:].indirect(offs_t[:, list_cols[0]]))
-        nc.vector.tensor_copy(got_w[1][:], tab_w[:].bitcast(U32).indirect(offs_t[:, list_cols[1]]))
         w4s_dealt = w4s_raw[:].rearrange("p (b m t) -> p b t m", b=2, t=4)
-        nc.vector.tensor_copy(w4s_first[:, 0:P], w4s_dealt[:, 0, 0, :])
-        w4s = {0: w4s_first[:, 0:P]}
-        w4s_late = keep.tile([P, 8, P], U8, name="w4s_late", align_bytes=64)
-        nc.vector.tensor_copy(w4s_late[:].rearrange("p (b t) m -> p b t m", b=2), w4s_dealt)
+        w4s = keep.tile([P, 8, P], U8, name="w4s", align_bytes=64)
+        nc.vector.tensor_copy(w4s[:].rearrange("p (b t) m -> p b t m", b=2), w4s_dealt)
+        got_w.append(keep.tile([P, BANK], U32, name="got_w1", tag="got_w1", align_bytes=64))
+        nc.vector.tensor_copy(got_w[1][:], tab_w[:].bitcast(U32).indirect(offs_t[:, list_cols[1]]))
         pages = [page0, page1]
 
         ident = keep.tile([P, P], F32, name="ident")
@@ -145,50 +150,57 @@ def tile_list_reefer_yard_alarm_kernel(
                     nc.tensor.transpose(bank[:, q, :], wgs_t[:, BANK * h + P * q : BANK * h + P * (q + 1)], ident[:])
                 nc.scalar.copy(wgs_col[h].rearrange("p (q g) -> p q g", g=8), bank[:, :, 0:P:GROUP])
 
-        w1_codes = [
-            laid.tile([P, 4 * P], U32, name="w1_codes0", align_bytes=64, offset=W1_CODES_AT),
-            keep.tile([P, 4 * P], U32, name="w1_codes1", align_bytes=64),
-        ]
+        w1_codes = {}
+        codes_at = {0: W1_CODES_AT, 2: 48 * KIB, 4: 52 * KIB - 128}
         w1_scales = [keep.tile([P, 4 * P], U8, name=f"w1_scales{b}", align_bytes=64) for b in range(2)]
 
-        def prepare_w1(k0, k1):
+        def prepare_w1(k0, k1, cast):
             b, t0 = divmod(k0, 4)
             t1 = t0 + k1 - k0
-            rounded = laid.tile([P, k1 - k0, P, 4], BF16, name=f"w1_rounded{k0}", align_bytes=64, offset=W1_ROUNDED_AT[k0])
+            room = laid.tile([P, W1_ROUNDED_BYTES[k0] // 2], BF16, name=f"w1_rounded{k0}", align_bytes=64, offset=W1_ROUNDED_AT[k0])
+            rounded = room[:, 0 : 4 * P * (k1 - k0)].rearrange("p (t m j) -> p t m j", m=P, j=4)
             src = w1_raw[b][:].rearrange("p j (m t) -> p m t j", t=4)
-            nc.scalar.copy(rounded[:].rearrange("p t m j -> p m t j"), src[:, :, t0:t1, :])
+            cast(rounded.rearrange("p t m j -> p m t j"), src[:, :, t0:t1, :])
+            w1_codes[k0] = laid.tile([P, P * (k1 - k0)], U32, name=f"w1_codes{k0}", align_bytes=64, offset=codes_at[k0])
             nc.vector.quantize_mx(
-                out=w1_codes[b][:, P * t0 : P * t1].bitcast(FP8X4),
+                out=w1_codes[k0][:].bitcast(FP8X4),
                 scales=w1_scales[b][:, P * t0 : P * t1],
-                in_=rounded[:].rearrange("p t m j -> p (t m j)"),
+                in_=room[:, 0 : 4 * P * (k1 - k0)],
             )
 
         val = {}
-        val_on = {0: "z_codes1", 1: "plane1_gate", 7: "z_codes0"}
+        val_on = {1: "plane1_gate", 2: "plane2_gate", 7: "z_codes0"}
+        turns_b = [0, 1] + [2, 0] * 7 + list(range(1, 1 + len(PIECES)))
 
-        def trust(k, h):
+        def bank_b(width, name):
+            return psum.tile([P, width], F32, name=name, tag=f"bank_b{turns_b.pop(0) % BANKS_B}", bufs=1)
+
+        def trust(k, h, into=None):
             b, t = divmod(k, 4)
-            if h == 0 and k in val_on:
+            if into is not None:
+                pass
+            elif h == 0 and k in val_on:
                 val[k] = shared([P, S], f"val{k}", val_on[k])
             elif h == 0:
                 val[k] = ring.tile([P, S], F32, name=f"val{k}", tag="val", bufs=4, align_bytes=64)
-            acc = psum.tile([P, BANK], F32, name="acc_b", tag="banks_b", bufs=BANKS_B)
+            acc = bank_b(BANK, "acc_b")
             nc.tensor.matmul_mx(
                 out=acc[:],
                 lhsT=w4w[:, 2 * P * k : 2 * P * (k + 1)].bitcast(FP4X4),
-                lhsT_scale=w4s[k],
+                lhsT_scale=w4s[:, k, :],
                 rhs=got_w[h][:].bitcast(FP8X4),
                 rhs_scale=got_s[h][:],
                 start=True,
                 stop=True,
             )
-            nc.scalar.activation(val[k][:, halves[h]], acc[:], ACT.Sigmoid, bias=bg_t[:, b, t : t + 1])
+            sigmoid = val[k][:, halves[h]] if into is None else into
+            nc.scalar.activation(sigmoid, acc[:], ACT.Sigmoid, bias=bg_t[:, b, t : t + 1])
 
         def deviation(k, h):
             acc = psum.tile([P, BANK], F32, name="acc_a", tag="banks_a")
             nc.tensor.matmul_mx(
                 out=acc[:],
-                lhsT=w1_codes[0][:, P * k : P * (k + 1)].bitcast(FP8X4),
+                lhsT=w1_codes[k - k % 2][:, P * (k % 2) : P * (k % 2 + 1)].bitcast(FP8X4),
                 lhsT_scale=w1_scales[0][:, P * k : P * (k + 1)],
                 rhs=got_w[h][:].bitcast(FP8X4),
                 rhs_scale=got_s[h][:],
@@ -206,7 +218,7 @@ def tile_list_reefer_yard_alarm_kernel(
                 out=acc[:].rearrange("p t m -> p (t m)"),
                 lhsT=got_w[h][:, P * q : P * (q + 1)].bitcast(FP8X4),
                 lhsT_scale=got_s[h][:, P * q : P * (q + 1)],
-                rhs=w1_codes[1][:].bitcast(FP8X4),
+                rhs=w1_codes[4][:].bitcast(FP8X4),
                 rhs_scale=w1_scales[1][:],
                 start=True,
                 stop=True,
@@ -245,7 +257,7 @@ def tile_list_reefer_yard_alarm_kernel(
                 nc.scalar.copy(copied[:, halves[h]], factor(k, h)[:])
             gate = val[k]
             if k == 1:
-                val[k] = shared([P, S], "val1_done", "w1_second")
+                val[k] = shared([P, S], "val1_done", "plane1")
             nc.gpsimd.tensor_tensor(val[k][:], gate[:], copied, MULT)
 
         def gated_on_gpsimd(k):
@@ -290,23 +302,27 @@ def tile_list_reefer_yard_alarm_kernel(
 
         all_cols = slice(0, T2)
 
-        trust(0, 0)
-        prepare_w1(0, 2)
-        got_s.append(laid.tile([P, BANK], U8, name="got_s1", align_bytes=64, offset=GOT_LATE_AT))
-        nc.vector.tensor_copy(got_s[1][:], tab_sc[:].indirect(offs_t[:, list_cols[1]]))
-        prepare_w1(2, 4)
-        for k in range(8):
-            w4s[k] = w4s_late[:, k, :]
+        sigmoid0 = [
+            laid.tile([P, BANK], F32, name="sigmoid0_first", align_bytes=64, offset=56 * KIB),
+            laid.tile([P, BANK], F32, name="sigmoid0_second", align_bytes=64, offset=50 * KIB),
+        ]
+        trust(0, 0, sigmoid0[0][:])
+        trust(0, 1, sigmoid0[1][:])
+        prepare_w1(0, 2, nc.vector.tensor_copy)
         load_expo(0)
-        trust(0, 1)
+        val0 = [laid.tile([P, BANK], F32, name="val0_first", align_bytes=64, offset=48 * KIB)]
+        nc.vector.tensor_tensor(val0[0][:], sigmoid0[0][:], wgs_t[:, halves[0]], MULT)
+        val0.append(laid.tile([P, BANK], F32, name="val0_second", align_bytes=64, offset=54 * KIB + 64))
+        nc.gpsimd.tensor_tensor(val0[1][:], sigmoid0[1][:], wgs_t[:, halves[1]], MULT)
         for h in range(2):
-            nc.gpsimd.tensor_tensor(val[0][:, halves[h]], val[0][:, halves[h]], wgs_t[:, halves[h]], MULT)
-            times_factor_on_vector(0, h)
-            nc.vector.tensor_copy(page0[:].indirect(offs2_t[:, list_cols[h]]), val[0][:, halves[h]])
-        load_expo(1)
+            done = val0[0] if h == 0 else laid.tile([P, BANK], F32, name="val0_done", align_bytes=64, offset=50 * KIB - 64)
+            nc.vector.tensor_tensor(done[:], val0[h][:], deviation(0, h)[:], MULT)
+            nc.vector.tensor_copy(page0[:].indirect(offs2_t[:, list_cols[h]]), done[:])
 
         weighed_gate(1)
-        prepare_w1(4, 8)
+        prepare_w1(2, 4, nc.scalar.copy)
+        prepare_w1(4, 8, nc.scalar.copy)
+        load_expo(1)
         times_factor_on_gpsimd(1)
         weighed_gate(2)
         times_factor_on_gpsimd(2)
@@ -361,7 +377,10 @@ def tile_list_reefer_yard_alarm_kernel(
         times_factor_on_vector(7, 1)
         place(7)
 
-        z_codes = [keep.tile([P, T2], U32, name=f"z_codes{b}", tag=f"z_codes{b}", align_bytes=64) for b in range(2)]
+        z_codes = [
+            keep.tile([P, T2], U32, name="z_codes0", tag="z_codes0", align_bytes=64),
+            laid.tile([P, T2], U32, name="z_codes1", align_bytes=64, offset=LAID_AT["z_codes1"]),
+        ]
         z_scales = [
             keep.tile([P, T2], U8, name=f"z_scales{b}", tag=("table", "z_scales1")[b], align_bytes=64) for b in range(2)
         ]
@@ -388,8 +407,11 @@ def tile_list_reefer_yard_alarm_kernel(
             weave = nc.scalar.copy if i in SCALAR_WEAVES else nc.vector.tensor_copy
             weave(woven1[:], both_pairs(1, cols))
             z.append(quantise(1, cols, woven1[:]))
-            bank_sets = [("banks_a", BANKS_A), ("banks_b", BANKS_B), ("banks_a", BANKS_A)]
-            accs = [psum.tile([P, width], F32, name="acc_o", tag=tag, bufs=bufs) for tag, bufs in bank_sets]
+            accs = [
+                psum.tile([P, width], F32, name="acc_o0", tag="banks_a"),
+                bank_b(width, "acc_o1"),
+                psum.tile([P, width], F32, name="acc_o2", tag="banks_a"),
+            ]
             for b in range(2):
                 for nb in range(N // P):
                     nc.tensor.matmul_mx(

@@ -159,8 +159,8 @@ def tile_list_reefer_yard_alarm_kernel(
             t1 = t0 + k1 - k0
             room = laid.tile([P, W1_ROUNDED_BYTES[k0] // 2], BF16, name=f"w1_rounded{k0}", align_bytes=64, offset=W1_ROUNDED_AT[k0])
             rounded = room[:, 0 : 4 * P * (k1 - k0)].rearrange("p (t m j) -> p t m j", m=P, j=4)
-            src = w1_raw[b][:].rearrange("p j (m t) -> p m t j", t=4)
-            cast(rounded.rearrange("p t m j -> p m t j"), src[:, :, t0:t1, :])
+            src = w1_raw[b][:].rearrange("p j (m t) -> p m j t", t=4)
+            cast(rounded.rearrange("p t m j -> p m j t"), src[:, :, :, t0:t1])
             w1_codes[k0] = laid.tile([P, P * (k1 - k0)], U32, name=f"w1_codes{k0}", align_bytes=64, offset=codes_at[k0])
             nc.vector.quantize_mx(
                 out=w1_codes[k0][:].bitcast(FP8X4),
@@ -298,7 +298,7 @@ def tile_list_reefer_yard_alarm_kernel(
                 load_expo(j + 2)
 
         def both_pairs(b, cols):
-            return words[b][:].rearrange("p (u m) -> p m u", u=2)[:, cols, :]
+            return words[b][:].rearrange("p (u m) -> p u m", u=2)[:, :, cols].rearrange("p u (c i) -> p c u i", i=4)
 
         all_cols = slice(0, T2)
 
@@ -372,7 +372,7 @@ def tile_list_reefer_yard_alarm_kernel(
         woven0 = ring.tile([P, T2, 2], F32, name="woven0", tag="lev", align_bytes=64)
         for c in range(T2 // BANK):
             cols = slice(BANK * c, BANK * (c + 1))
-            nc.scalar.copy(woven0[:, cols, :], both_pairs(0, cols))
+            nc.scalar.copy(woven0[:, cols, :].rearrange("p (c i) u -> p c u i", i=4), both_pairs(0, cols))
         level(6, all_cols)
         times_factor_on_vector(7, 1)
         place(7)
@@ -405,7 +405,7 @@ def tile_list_reefer_yard_alarm_kernel(
             expose(nc.vector, 3, cols)
             woven1 = ring.tile([P, width, 2], F32, name="woven1", tag="stage", bufs=3, align_bytes=64)
             weave = nc.scalar.copy if i in SCALAR_WEAVES else nc.vector.tensor_copy
-            weave(woven1[:], both_pairs(1, cols))
+            weave(woven1[:].rearrange("p (c i) u -> p c u i", i=4), both_pairs(1, cols))
             z.append(quantise(1, cols, woven1[:]))
             accs = [
                 psum.tile([P, width], F32, name="acc_o0", tag="banks_a"),

@@ -22,17 +22,19 @@ BANK = 512
 GROUP = 16
 BANKS_A, BANKS_B = 5, 3
 KIB = 1024
+FIRST_PART = 1536
+EARLY_BANKS = 3
 WIDE = 1024
 
 LAID_AT = {
     "wgs": 8 * KIB,
     "w1_second": 12 * KIB,
     "w1_first": 23 * KIB,
-    "plane1": 12 * KIB,
+    "plane1": 42 * KIB + 64,
     "plane2_gate": 16 * KIB,
-    "plane2": 42 * KIB,
+    "plane2": 50 * KIB - 64,
     "plane3": 54 * KIB - 64,
-    "plane1_gate": 58 * KIB - 64,
+    "plane1_gate": 58 * KIB + 192,
     "z_codes1": 54 * KIB,
 }
 W4_DEALT_AT = 20 * KIB
@@ -40,7 +42,7 @@ W4_SCALES_RAW_AT = 22 * KIB
 W1_CODES_AT = 39 * KIB
 GOT_LATE_AT = 41 * KIB
 W4_RAW_AT, W4_RAW_BYTES = 8 * KIB - 64, 64 + 4 * KIB + 64
-W1_ROUNDED_AT = {0: 44 * KIB - 64, 2: 42 * KIB, 4: 44 * KIB}
+W1_ROUNDED_AT = {0: 44 * KIB - 64, 2: 56 * KIB + 64, 4: 42 * KIB}
 W1_ROUNDED_BYTES = {0: 64 + 4 * KIB + 64, 2: 2 * KIB, 4: 4 * KIB}
 WARM_AT = 22 * KIB - 64
 W4_FIRST_AT = 41 * KIB - 64
@@ -64,6 +66,12 @@ def tile_list_reefer_yard_alarm_kernel(
             if tag in LAID_AT:
                 return laid.tile(shape, F32, name=name, tag=tag, align_bytes=64, offset=LAID_AT[tag])
             return keep.tile(shape, F32, name=name, tag=tag, align_bytes=64)
+
+        turns_a = []
+
+        def next_bank_a():
+            turns_a.append(len(turns_a) % BANKS_A)
+            return f"bank_a{turns_a[-1]}"
 
         offs_t = keep.tile([P, S // GROUP], U16, name="offs_t")
         offs2_t = keep.tile([P, S // GROUP], U16, name="offs2_t")
@@ -140,18 +148,24 @@ def tile_list_reefer_yard_alarm_kernel(
         ident = keep.tile([P, P], F32, name="ident")
         make_identity(nc, ident[:])
         lev0 = ring.tile([P, 2, T2], F32, name="lev0", tag="lev", align_bytes=64)
-        wgs_late = keep.tile([P, 32], F32, name="wgs_late")
-        wgs_col = [lev0[:, 1, 0:32], wgs_late[:]]
+        wgs_late = keep.tile([P, 8 - EARLY_BANKS, 8], F32, name="wgs_late")
+        wgs_early = lev0[:, 1, 0 : 8 * EARLY_BANKS].rearrange("p (e g) -> p e g", g=8)
+        wgs_first = lev0[:, 0, 0:8]
 
         def turn_wgs():
             for h in range(2):
-                bank = psum.tile([P, 4, P], F32, name="wgs_bank", tag="banks_a")
+                bank = psum.tile([P, 4, P], F32, name="wgs_bank", tag=next_bank_a(), bufs=1)
                 for q in range(4):
                     nc.tensor.transpose(bank[:, q, :], wgs_t[:, BANK * h + P * q : BANK * h + P * (q + 1)], ident[:])
-                nc.scalar.copy(wgs_col[h].rearrange("p (q g) -> p q g", g=8), bank[:, :, 0:P:GROUP])
+                if h == 0:
+                    nc.scalar.copy(wgs_first, bank[:, 0, 0:P:GROUP])
+                    nc.scalar.copy(wgs_early[:, 1:, :], bank[:, 1:EARLY_BANKS, 0:P:GROUP])
+                    nc.scalar.copy(wgs_late[:, 0 : 4 - EARLY_BANKS, :], bank[:, EARLY_BANKS:4, 0:P:GROUP])
+                else:
+                    nc.scalar.copy(wgs_late[:, 4 - EARLY_BANKS :, :], bank[:, :, 0:P:GROUP])
 
         w1_codes = {}
-        codes_at = {0: W1_CODES_AT, 2: 48 * KIB, 4: 52 * KIB - 128}
+        codes_at = {0: W1_CODES_AT, 2: 48 * KIB + 64, 4: 46 * KIB + 64}
         w1_scales = [keep.tile([P, 4 * P], U8, name=f"w1_scales{b}", align_bytes=64) for b in range(2)]
 
         def prepare_w1(k0, k1, cast):
@@ -182,7 +196,7 @@ def tile_list_reefer_yard_alarm_kernel(
             elif h == 0 and k in val_on:
                 val[k] = shared([P, S], f"val{k}", val_on[k])
             elif h == 0:
-                val[k] = ring.tile([P, S], F32, name=f"val{k}", tag="val", bufs=4, align_bytes=64)
+                val[k] = keep.tile([P, S], F32, name=f"val{k}", align_bytes=64)
             acc = bank_b(BANK, "acc_b")
             nc.tensor.matmul_mx(
                 out=acc[:],
@@ -197,7 +211,7 @@ def tile_list_reefer_yard_alarm_kernel(
             nc.scalar.activation(sigmoid, acc[:], ACT.Sigmoid, bias=bg_t[:, b, t : t + 1])
 
         def deviation(k, h):
-            acc = psum.tile([P, BANK], F32, name="acc_a", tag="banks_a")
+            acc = psum.tile([P, BANK], F32, name="acc_a", tag=next_bank_a(), bufs=1)
             nc.tensor.matmul_mx(
                 out=acc[:],
                 lhsT=w1_codes[k - k % 2][:, P * (k % 2) : P * (k % 2 + 1)].bitcast(FP8X4),
@@ -213,7 +227,7 @@ def tile_list_reefer_yard_alarm_kernel(
 
         def weigh_transposed(e):
             h, q = divmod(e, 4)
-            acc = psum.tile([P, 4, P], F32, name="acc_t", tag="banks_a")
+            acc = psum.tile([P, 4, P], F32, name="acc_t", tag=next_bank_a(), bufs=1)
             nc.tensor.matmul_mx(
                 out=acc[:].rearrange("p t m -> p (t m)"),
                 lhsT=got_w[h][:, P * q : P * (q + 1)].bitcast(FP8X4),
@@ -225,11 +239,13 @@ def tile_list_reefer_yard_alarm_kernel(
             )
             for g in range(8):
                 run = slice(GROUP * g, GROUP * (g + 1))
-                weight = wgs_col[h][:, 8 * q + g : 8 * q + g + 1]
+                weight = wgs_early[:, e, g : g + 1] if e < EARLY_BANKS else wgs_late[:, e - EARLY_BANKS, g : g + 1]
+                if e == 0:
+                    weight = wgs_first[:, g : g + 1]
                 nc.scalar.activation(weighed[e][:, :, run], acc[:, :, run], ACT.Copy, scale=weight)
 
         def turned_back(k, h):
-            acc = psum.tile([P, BANK], F32, name="acc_r", tag="banks_a")
+            acc = psum.tile([P, BANK], F32, name="acc_r", tag=next_bank_a(), bufs=1)
             for q in range(4):
                 nc.tensor.transpose(acc[:, P * q : P * (q + 1)], weighed[4 * h + q][:, k - 4, :], ident[:])
             return acc
@@ -249,16 +265,22 @@ def tile_list_reefer_yard_alarm_kernel(
             nc.vector.tensor_tensor(val[k][:, halves[h]], val[k][:, halves[h]], factor(k, h)[:], MULT)
 
         def times_factor_on_gpsimd(k):
-            if k < 3:
-                copied = ring.tile([P, S], F32, name="copied", tag="stage", bufs=3, align_bytes=64)[:]
+            if k < 3 or k == 6:
+                copied = ring.tile([P, 2, BANK], F32, name="copied", tag="stage", bufs=3, align_bytes=64)[:]
             else:
-                copied = words[0][:, S * (k - 3) : S * (k - 2)]
+                at = {3: 0, 5: 2 * S, 7: 3 * S}.get(k)
+                if k == 4:
+                    copied = words[0][:].rearrange("p (h m) -> p h m", h=2)[:, :, T2 - BANK : T2]
+                else:
+                    copied = words[0][:, at : at + S].rearrange("p (h m) -> p h m", h=2)
             for h in range(2):
-                nc.scalar.copy(copied[:, halves[h]], factor(k, h)[:])
+                nc.scalar.copy(copied[:, h, :], factor(k, h)[:])
             gate = val[k]
             if k == 1:
                 val[k] = shared([P, S], "val1_done", "plane1")
-            nc.gpsimd.tensor_tensor(val[k][:], gate[:], copied, MULT)
+            nc.gpsimd.tensor_tensor(
+                val[k][:].rearrange("p (h m) -> p h m", h=2), gate[:].rearrange("p (h m) -> p h m", h=2), copied, MULT
+            )
 
         def gated_on_gpsimd(k):
             trust(k, 0)
@@ -293,7 +315,8 @@ def tile_list_reefer_yard_alarm_kernel(
             )
 
         def expose_half(j, half):
-            expose(nc.gpsimd, j, slice(T2 // 2 * half, T2 // 2 * (half + 1)))
+            cut = FIRST_PART if j == 0 else T2 // 2
+            expose(nc.gpsimd, j, (slice(0, cut), slice(cut, T2))[half])
             if half == 1:
                 load_expo(j + 2)
 
@@ -303,25 +326,27 @@ def tile_list_reefer_yard_alarm_kernel(
         all_cols = slice(0, T2)
 
         sigmoid0 = [
-            laid.tile([P, BANK], F32, name="sigmoid0_first", align_bytes=64, offset=56 * KIB),
+            laid.tile([P, BANK + 64], F32, name="sigmoid0_first", align_bytes=64, offset=56 * KIB),
             laid.tile([P, BANK], F32, name="sigmoid0_second", align_bytes=64, offset=50 * KIB),
         ]
-        trust(0, 0, sigmoid0[0][:])
+        trust(0, 0, sigmoid0[0][:, 0:BANK])
         trust(0, 1, sigmoid0[1][:])
         prepare_w1(0, 2, nc.vector.tensor_copy)
         load_expo(0)
         val0 = [laid.tile([P, BANK], F32, name="val0_first", align_bytes=64, offset=48 * KIB)]
-        nc.vector.tensor_tensor(val0[0][:], sigmoid0[0][:], wgs_t[:, halves[0]], MULT)
+        nc.vector.tensor_tensor(val0[0][:], sigmoid0[0][:, 0:BANK], wgs_t[:, halves[0]], MULT)
         val0.append(laid.tile([P, BANK], F32, name="val0_second", align_bytes=64, offset=54 * KIB + 64))
         nc.gpsimd.tensor_tensor(val0[1][:], sigmoid0[1][:], wgs_t[:, halves[1]], MULT)
-        for h in range(2):
-            done = val0[0] if h == 0 else laid.tile([P, BANK], F32, name="val0_done", align_bytes=64, offset=50 * KIB - 64)
-            nc.vector.tensor_tensor(done[:], val0[h][:], deviation(0, h)[:], MULT)
-            nc.vector.tensor_copy(page0[:].indirect(offs2_t[:, list_cols[h]]), done[:])
+        nc.vector.tensor_tensor(val0[0][:], val0[0][:], deviation(0, 0)[:], MULT)
+        nc.vector.tensor_copy(page0[:].indirect(offs2_t[:, list_cols[0]]), val0[0][:])
+        second_factor = deviation(0, 1)
 
         weighed_gate(1)
         prepare_w1(2, 4, nc.scalar.copy)
         prepare_w1(4, 8, nc.scalar.copy)
+        done = laid.tile([P, BANK], F32, name="val0_done", align_bytes=64, offset=40 * KIB + 64)
+        nc.vector.tensor_tensor(done[:], val0[1][:], second_factor[:], MULT)
+        nc.vector.tensor_copy(page0[:].indirect(offs2_t[:, list_cols[1]]), done[:])
         load_expo(1)
         times_factor_on_gpsimd(1)
         weighed_gate(2)
@@ -330,13 +355,15 @@ def tile_list_reefer_yard_alarm_kernel(
         turn_wgs()
         weighed_gate(3)
         times_factor_on_gpsimd(3)
+        weigh_transposed(0)
         level(0, all_cols)
         place(2)
-        for e in range(4):
+        for e in range(1, EARLY_BANKS):
             weigh_transposed(e)
-        level(1, all_cols)
+        level(1, slice(0, FIRST_PART))
+        level(1, slice(FIRST_PART, T2))
         expose_half(0, 0)
-        for e in range(4, 8):
+        for e in range(EARLY_BANKS, 8):
             weigh_transposed(e)
         place(3)
 
@@ -358,12 +385,12 @@ def tile_list_reefer_yard_alarm_kernel(
         expose_half(1, 0)
         place(5)
         gated_on_gpsimd(6)
-        expose_half(1, 1)
         trust(7, 0)
         trust(7, 1)
+        nc.scalar.copy(words[0][:, 3 * S : 3 * S + BANK], factor(7, 0)[:])
+        nc.gpsimd.tensor_tensor(val[7][:, halves[0]], val[7][:, halves[0]], words[0][:, 3 * S : 3 * S + BANK], MULT)
+        expose_half(1, 1)
         level(4, all_cols)
-        nc.scalar.copy(words[1][:, halves[0]], factor(7, 0)[:])
-        nc.gpsimd.tensor_tensor(val[7][:, halves[0]], val[7][:, halves[0]], words[1][:, halves[0]], MULT)
         place(6)
         for half in range(2):
             cols = slice(T2 // 2 * half, T2 // 2 * (half + 1))
@@ -408,9 +435,9 @@ def tile_list_reefer_yard_alarm_kernel(
             weave(woven1[:].rearrange("p (c i) u -> p c u i", i=4), both_pairs(1, cols))
             z.append(quantise(1, cols, woven1[:]))
             accs = [
-                psum.tile([P, width], F32, name="acc_o0", tag="banks_a"),
+                psum.tile([P, width], F32, name="acc_o0", tag=next_bank_a(), bufs=1),
                 bank_b(width, "acc_o1"),
-                psum.tile([P, width], F32, name="acc_o2", tag="banks_a"),
+                psum.tile([P, width], F32, name="acc_o2", tag=next_bank_a(), bufs=1),
             ]
             for b in range(2):
                 for nb in range(N // P):

@@ -22,31 +22,42 @@ BANK = 512
 GROUP = 16
 BANKS_A, BANKS_B = 5, 3
 KIB = 1024
+EDGE = 64
+WIDE = 1024
 FIRST_PART = 1536
 EARLY_BANKS = 3
-WIDE = 1024
+SHARE7 = 768
 
 LAID_AT = {
+    "page1": 0,
+    "w4w_raw": 8 * KIB - EDGE,
     "wgs": 8 * KIB,
     "w1_second": 12 * KIB,
-    "w1_first": 23 * KIB,
-    "plane1": 42 * KIB + 64,
     "plane2_gate": 16 * KIB,
-    "plane2": 50 * KIB - 64,
-    "plane3": 54 * KIB - 64,
-    "plane1_gate": 58 * KIB + 192,
+    "w4w": 20 * KIB,
+    "warm_in": 22 * KIB - EDGE,
+    "w1_first": 23 * KIB,
+    "w1_codes0": 39 * KIB,
+    "w1_rounded4": 42 * KIB,
+    "w1_codes2": 42 * KIB,
+    "plane3": 42 * KIB,
+    "val0_done": 43 * KIB,
+    "w1_rounded0": 44 * KIB - EDGE,
+    "w1_codes4": 46 * KIB + EDGE,
+    "val0_first": 48 * KIB,
+    "plane2": 50 * KIB - EDGE,
+    "sigmoid0_second": 50 * KIB,
     "z_codes1": 54 * KIB,
+    "val0_second": 54 * KIB + EDGE,
+    "plane1": 54 * KIB + 2 * EDGE,
+    "sigmoid0_first": 56 * KIB,
+    "w1_rounded2": 56 * KIB + EDGE,
+    "plane1_gate": 58 * KIB + 3 * EDGE,
 }
-W4_DEALT_AT = 20 * KIB
-W4_SCALES_RAW_AT = 22 * KIB
-W1_CODES_AT = 39 * KIB
-GOT_LATE_AT = 41 * KIB
-W4_RAW_AT, W4_RAW_BYTES = 8 * KIB - 64, 64 + 4 * KIB + 64
-W1_ROUNDED_AT = {0: 44 * KIB - 64, 2: 56 * KIB + 64, 4: 42 * KIB}
-W1_ROUNDED_BYTES = {0: 64 + 4 * KIB + 64, 2: 2 * KIB, 4: 4 * KIB}
-WARM_AT = 22 * KIB - 64
-W4_FIRST_AT = 41 * KIB - 64
-SPAN = 64 + KIB + 64
+W4W_RAW_BYTES = EDGE + 4 * KIB + EDGE
+WARM_IN_BYTES = EDGE + KIB + EDGE
+W1_ROUNDED_BYTES = {0: EDGE + 4 * KIB + EDGE, 2: 2 * KIB, 4: 4 * KIB}
+SIGMOID0_FIRST_BYTES = 2 * KIB + 4 * EDGE
 
 PIECES = [(0, 256), (256, 512), (768, 512), (1280, 512), (1792, 256)]
 SCALAR_WEAVES = (1, 2)
@@ -62,6 +73,9 @@ def tile_list_reefer_yard_alarm_kernel(
         ring = ctx.enter_context(tc.tile_pool(name="ring", bufs=2))
         psum = ctx.enter_context(tc.psum_pool(name="psum", bufs=BANKS_A))
 
+        def laid_tile(shape, dtype, name):
+            return laid.tile(shape, dtype, name=name, align_bytes=64, offset=LAID_AT[name])
+
         def shared(shape, name, tag):
             if tag in LAID_AT:
                 return laid.tile(shape, F32, name=name, tag=tag, align_bytes=64, offset=LAID_AT[tag])
@@ -75,9 +89,9 @@ def tile_list_reefer_yard_alarm_kernel(
 
         offs_t = keep.tile([P, S // GROUP], U16, name="offs_t")
         offs2_t = keep.tile([P, S // GROUP], U16, name="offs2_t")
-        warm_in = laid.tile([P, SPAN // 4], F32, name="warm_in", align_bytes=64, offset=WARM_AT)
+        warm_in = laid_tile([P, WARM_IN_BYTES // 4], F32, "warm_in")
         tab_sc = keep.tile([P, T], U8, name="tab_sc", tag="z_scales1", align_bytes=64)
-        w4w_raw = laid.tile([P, W4_RAW_BYTES], U8, name="w4w_raw", align_bytes=64, offset=W4_RAW_AT)
+        w4w_raw = laid_tile([P, W4W_RAW_BYTES], U8, "w4w_raw")
         bg_t = keep.tile([P, 2, 4], F32, name="bg_t")
         amb_t = keep.tile([P, 2, 4], F32, name="amb_t")
         warm_out = keep.tile([P, 8], F32, name="warm_out")
@@ -124,7 +138,7 @@ def tile_list_reefer_yard_alarm_kernel(
         got_s = [keep.tile([P, BANK], U8, name=f"got_s{h}", align_bytes=64) for h in range(2)]
         list_cols = [slice(BANK // GROUP * h, BANK // GROUP * (h + 1)) for h in range(2)]
 
-        w4w = laid.tile([P, 2 * H], U8, name="w4w", align_bytes=64, offset=W4_DEALT_AT)
+        w4w = laid_tile([P, 2 * H], U8, "w4w")
         nc.vector.tensor_copy(
             w4w[:].bitcast(U16).rearrange("p (b t m) -> p b t m", b=2, t=4),
             w4w_raw[:, 0 : 2 * H].bitcast(U16).rearrange("p (b m t) -> p b t m", b=2, t=4),
@@ -132,7 +146,7 @@ def tile_list_reefer_yard_alarm_kernel(
         wgs_t = shared([P, S], "wgs_t", "wgs")
         for half in halves:
             nc.sync.dma_start(wgs_t[:, half], wgs[:, half])
-        page1 = laid.tile([P, T2], F32, name="page1", align_bytes=64, offset=0)
+        page1 = laid_tile([P, T2], F32, "page1")
         nc.gpsimd.memset(page1[:], 0.0)
         load_w1(1)
         for h in range(2):
@@ -151,6 +165,8 @@ def tile_list_reefer_yard_alarm_kernel(
         wgs_late = keep.tile([P, 8 - EARLY_BANKS, 8], F32, name="wgs_late")
         wgs_early = lev0[:, 1, 0 : 8 * EARLY_BANKS].rearrange("p (e g) -> p e g", g=8)
         wgs_first = lev0[:, 0, 0:8]
+        wgs_blocks = [wgs_first] + [wgs_early[:, e, :] for e in range(1, EARLY_BANKS)]
+        wgs_blocks.extend(wgs_late[:, e, :] for e in range(8 - EARLY_BANKS))
 
         def turn_wgs():
             for h in range(2):
@@ -165,21 +181,26 @@ def tile_list_reefer_yard_alarm_kernel(
                     nc.scalar.copy(wgs_late[:, 4 - EARLY_BANKS :, :], bank[:, :, 0:P:GROUP])
 
         w1_codes = {}
-        codes_at = {0: W1_CODES_AT, 2: 48 * KIB + 64, 4: 46 * KIB + 64}
+        w1_rounded = {}
         w1_scales = [keep.tile([P, 4 * P], U8, name=f"w1_scales{b}", align_bytes=64) for b in range(2)]
 
-        def prepare_w1(k0, k1, cast):
+        def round_w1(k0, k1, cast):
             b, t0 = divmod(k0, 4)
             t1 = t0 + k1 - k0
-            room = laid.tile([P, W1_ROUNDED_BYTES[k0] // 2], BF16, name=f"w1_rounded{k0}", align_bytes=64, offset=W1_ROUNDED_AT[k0])
-            rounded = room[:, 0 : 4 * P * (k1 - k0)].rearrange("p (t m j) -> p t m j", m=P, j=4)
+            room = laid_tile([P, W1_ROUNDED_BYTES[k0] // 2], BF16, f"w1_rounded{k0}")
+            w1_rounded[k0] = room[:, 0 : 4 * P * (k1 - k0)]
+            rounded = w1_rounded[k0].rearrange("p (t m j) -> p t m j", m=P, j=4)
             src = w1_raw[b][:].rearrange("p j (m t) -> p m j t", t=4)
             cast(rounded.rearrange("p t m j -> p m j t"), src[:, :, :, t0:t1])
-            w1_codes[k0] = laid.tile([P, P * (k1 - k0)], U32, name=f"w1_codes{k0}", align_bytes=64, offset=codes_at[k0])
+
+        def quantise_w1(k0, k1):
+            b, t0 = divmod(k0, 4)
+            t1 = t0 + k1 - k0
+            w1_codes[k0] = laid_tile([P, P * (k1 - k0)], U32, f"w1_codes{k0}")
             nc.vector.quantize_mx(
                 out=w1_codes[k0][:].bitcast(FP8X4),
                 scales=w1_scales[b][:, P * t0 : P * t1],
-                in_=room[:, 0 : 4 * P * (k1 - k0)],
+                in_=w1_rounded[k0],
             )
 
         val = {}
@@ -189,14 +210,8 @@ def tile_list_reefer_yard_alarm_kernel(
         def bank_b(width, name):
             return psum.tile([P, width], F32, name=name, tag=f"bank_b{turns_b.pop(0) % BANKS_B}", bufs=1)
 
-        def trust(k, h, into=None):
+        def trust(k, h, sigmoid):
             b, t = divmod(k, 4)
-            if into is not None:
-                pass
-            elif h == 0 and k in val_on:
-                val[k] = shared([P, S], f"val{k}", val_on[k])
-            elif h == 0:
-                val[k] = keep.tile([P, S], F32, name=f"val{k}", align_bytes=64)
             acc = bank_b(BANK, "acc_b")
             nc.tensor.matmul_mx(
                 out=acc[:],
@@ -207,8 +222,12 @@ def tile_list_reefer_yard_alarm_kernel(
                 start=True,
                 stop=True,
             )
-            sigmoid = val[k][:, halves[h]] if into is None else into
             nc.scalar.activation(sigmoid, acc[:], ACT.Sigmoid, bias=bg_t[:, b, t : t + 1])
+
+        def gate(k):
+            val[k] = shared([P, S], f"val{k}", val_on.get(k, f"val{k}"))
+            for h in range(2):
+                trust(k, h, val[k][:, halves[h]])
 
         def deviation(k, h):
             acc = psum.tile([P, BANK], F32, name="acc_a", tag=next_bank_a(), bufs=1)
@@ -239,9 +258,7 @@ def tile_list_reefer_yard_alarm_kernel(
             )
             for g in range(8):
                 run = slice(GROUP * g, GROUP * (g + 1))
-                weight = wgs_early[:, e, g : g + 1] if e < EARLY_BANKS else wgs_late[:, e - EARLY_BANKS, g : g + 1]
-                if e == 0:
-                    weight = wgs_first[:, g : g + 1]
+                weight = wgs_blocks[e][:, g : g + 1]
                 nc.scalar.activation(weighed[e][:, :, run], acc[:, :, run], ACT.Copy, scale=weight)
 
         def turned_back(k, h):
@@ -254,43 +271,39 @@ def tile_list_reefer_yard_alarm_kernel(
             return deviation(k, h) if k < 4 else turned_back(k, h)
 
         def weighed_gate(k):
-            trust(k, 0)
-            trust(k, 1)
+            gate(k)
             sigmoids = val[k]
             if k > 1:
                 val[k] = shared([P, S], f"val{k}_weighed", f"plane{k}")
             nc.gpsimd.tensor_tensor(val[k][:], sigmoids[:], wgs_t[:], MULT)
 
-        def times_factor_on_vector(k, h):
-            nc.vector.tensor_tensor(val[k][:, halves[h]], val[k][:, halves[h]], factor(k, h)[:], MULT)
-
         def times_factor_on_gpsimd(k):
-            if k < 3 or k == 6:
-                copied = ring.tile([P, 2, BANK], F32, name="copied", tag="stage", bufs=3, align_bytes=64)[:]
+            if k in copied_on_words:
+                copied = copied_on_words[k]
             else:
-                at = {3: 0, 5: 2 * S, 7: 3 * S}.get(k)
-                if k == 4:
-                    copied = words[0][:].rearrange("p (h m) -> p h m", h=2)[:, :, T2 - BANK : T2]
-                else:
-                    copied = words[0][:, at : at + S].rearrange("p (h m) -> p h m", h=2)
+                copied = ring.tile([P, 2, BANK], F32, name="copied", tag="stage", bufs=3, align_bytes=64)[:]
             for h in range(2):
                 nc.scalar.copy(copied[:, h, :], factor(k, h)[:])
-            gate = val[k]
+            gated = val[k]
             if k == 1:
                 val[k] = shared([P, S], "val1_done", "plane1")
             nc.gpsimd.tensor_tensor(
-                val[k][:].rearrange("p (h m) -> p h m", h=2), gate[:].rearrange("p (h m) -> p h m", h=2), copied, MULT
+                val[k][:].rearrange("p (h m) -> p h m", h=2), gated[:].rearrange("p (h m) -> p h m", h=2), copied, MULT
             )
 
         def gated_on_gpsimd(k):
-            trust(k, 0)
-            trust(k, 1)
+            gate(k)
             times_factor_on_gpsimd(k)
 
         def place(k):
             nc.vector.tensor_copy(pages[k % 2][:].indirect(offs2_t[:]), val[k][:])
 
         words = [keep.tile([P, 2 * T2], F32, name=f"words{b}", tag=f"words{b}") for b in range(2)]
+        copied_on_words = {
+            3: words[0][:, 0:S].rearrange("p (h m) -> p h m", h=2),
+            4: words[0][:].rearrange("p (h m) -> p h m", h=2)[:, :, T2 - BANK : T2],
+            5: words[0][:, T2 : T2 + S].rearrange("p (h m) -> p h m", h=2),
+        }
         late_lev = keep.tile([P, 3 * T2], F32, name="late_lev")
         lev = {
             0: lev0[:],
@@ -314,10 +327,10 @@ def tile_list_reefer_yard_alarm_kernel(
                 MULT,
             )
 
-        def expose_half(j, half):
+        def expose_part(j, part):
             cut = FIRST_PART if j == 0 else T2 // 2
-            expose(nc.gpsimd, j, (slice(0, cut), slice(cut, T2))[half])
-            if half == 1:
+            expose(nc.gpsimd, j, (slice(0, cut), slice(cut, T2))[part])
+            if part == 1:
                 load_expo(j + 2)
 
         def both_pairs(b, cols):
@@ -326,28 +339,31 @@ def tile_list_reefer_yard_alarm_kernel(
         all_cols = slice(0, T2)
 
         sigmoid0 = [
-            laid.tile([P, BANK + 64], F32, name="sigmoid0_first", align_bytes=64, offset=56 * KIB),
-            laid.tile([P, BANK], F32, name="sigmoid0_second", align_bytes=64, offset=50 * KIB),
+            laid_tile([P, SIGMOID0_FIRST_BYTES // 4], F32, "sigmoid0_first"),
+            laid_tile([P, BANK], F32, "sigmoid0_second"),
         ]
         trust(0, 0, sigmoid0[0][:, 0:BANK])
         trust(0, 1, sigmoid0[1][:])
-        prepare_w1(0, 2, nc.vector.tensor_copy)
+        round_w1(0, 2, nc.vector.tensor_copy)
+        quantise_w1(0, 2)
         load_expo(0)
-        val0 = [laid.tile([P, BANK], F32, name="val0_first", align_bytes=64, offset=48 * KIB)]
+        val0 = [laid_tile([P, BANK], F32, "val0_first")]
         nc.vector.tensor_tensor(val0[0][:], sigmoid0[0][:, 0:BANK], wgs_t[:, halves[0]], MULT)
-        val0.append(laid.tile([P, BANK], F32, name="val0_second", align_bytes=64, offset=54 * KIB + 64))
+        val0.append(laid_tile([P, BANK], F32, "val0_second"))
         nc.gpsimd.tensor_tensor(val0[1][:], sigmoid0[1][:], wgs_t[:, halves[1]], MULT)
         nc.vector.tensor_tensor(val0[0][:], val0[0][:], deviation(0, 0)[:], MULT)
         nc.vector.tensor_copy(page0[:].indirect(offs2_t[:, list_cols[0]]), val0[0][:])
         second_factor = deviation(0, 1)
-
         weighed_gate(1)
-        prepare_w1(2, 4, nc.scalar.copy)
-        prepare_w1(4, 8, nc.scalar.copy)
-        done = laid.tile([P, BANK], F32, name="val0_done", align_bytes=64, offset=40 * KIB + 64)
+        round_w1(2, 4, nc.scalar.copy)
+        round_w1(4, 8, nc.scalar.copy)
+        quantise_w1(4, 8)
+        done = laid_tile([P, BANK], F32, "val0_done")
         nc.vector.tensor_tensor(done[:], val0[1][:], second_factor[:], MULT)
+        quantise_w1(2, 4)
         nc.vector.tensor_copy(page0[:].indirect(offs2_t[:, list_cols[1]]), done[:])
         load_expo(1)
+
         times_factor_on_gpsimd(1)
         weighed_gate(2)
         times_factor_on_gpsimd(2)
@@ -362,7 +378,7 @@ def tile_list_reefer_yard_alarm_kernel(
             weigh_transposed(e)
         level(1, slice(0, FIRST_PART))
         level(1, slice(FIRST_PART, T2))
-        expose_half(0, 0)
+        expose_part(0, 0)
         for e in range(EARLY_BANKS, 8):
             weigh_transposed(e)
         place(3)
@@ -377,19 +393,22 @@ def tile_list_reefer_yard_alarm_kernel(
             )
 
         gated_on_gpsimd(4)
-        expose_half(0, 1)
+        expose_part(0, 1)
         level(2, all_cols)
         place(4)
         gated_on_gpsimd(5)
         level(3, all_cols)
-        expose_half(1, 0)
+        expose_part(1, 0)
         place(5)
         gated_on_gpsimd(6)
-        trust(7, 0)
-        trust(7, 1)
-        nc.scalar.copy(words[0][:, 3 * S : 3 * S + BANK], factor(7, 0)[:])
-        nc.gpsimd.tensor_tensor(val[7][:, halves[0]], val[7][:, halves[0]], words[0][:, 3 * S : 3 * S + BANK], MULT)
-        expose_half(1, 1)
+        gate(7)
+        copied7 = words[0][:, T2 + S : T2 + S + SHARE7]
+        nc.scalar.copy(copied7[:, halves[0]], factor(7, 0)[:])
+        second7 = factor(7, 1)
+        nc.scalar.copy(copied7[:, BANK:SHARE7], second7[:, 0 : SHARE7 - BANK])
+        nc.vector.tensor_tensor(val[7][:, SHARE7:S], val[7][:, SHARE7:S], second7[:, SHARE7 - BANK : BANK], MULT)
+        nc.gpsimd.tensor_tensor(val[7][:, 0:SHARE7], val[7][:, 0:SHARE7], copied7, MULT)
+        expose_part(1, 1)
         level(4, all_cols)
         place(6)
         for half in range(2):
@@ -401,7 +420,6 @@ def tile_list_reefer_yard_alarm_kernel(
             cols = slice(BANK * c, BANK * (c + 1))
             nc.scalar.copy(woven0[:, cols, :].rearrange("p (c i) u -> p c u i", i=4), both_pairs(0, cols))
         level(6, all_cols)
-        times_factor_on_vector(7, 1)
         place(7)
 
         z_codes = [

@@ -20,47 +20,54 @@ MULT = mybir.AluOpType.mult
 P = 128
 BANK = 512
 GROUP = 16
-BANKS_A, BANKS_B = 5, 3
 KIB = 1024
-EDGE = 64
-WIDE = 1024
-FIRST_PART = 1536
-EARLY_BANKS = 3
-SHARE7 = 768
+RING_BANKS = 4
+HALVES = [slice(0, BANK), slice(BANK, 2 * BANK)]
 
-LAID_AT = {
-    "page1": 0,
-    "w4w_raw": 8 * KIB - EDGE,
-    "wgs": 8 * KIB,
-    "w1_second": 12 * KIB,
-    "plane2_gate": 16 * KIB,
-    "w4w": 20 * KIB,
-    "warm_in": 22 * KIB - EDGE,
-    "w1_first": 23 * KIB,
-    "w1_codes0": 39 * KIB,
-    "w1_rounded4": 42 * KIB,
-    "w1_codes2": 42 * KIB,
-    "plane3": 42 * KIB,
-    "val0_done": 43 * KIB,
-    "w1_rounded0": 44 * KIB - EDGE,
-    "w1_codes4": 46 * KIB + EDGE,
-    "val0_first": 48 * KIB,
-    "plane2": 50 * KIB - EDGE,
-    "sigmoid0_second": 50 * KIB,
-    "z_codes1": 54 * KIB,
-    "val0_second": 54 * KIB + EDGE,
-    "plane1": 54 * KIB + 2 * EDGE,
-    "sigmoid0_first": 56 * KIB,
-    "w1_rounded2": 56 * KIB + EDGE,
-    "plane1_gate": 58 * KIB + 3 * EDGE,
+AT = {
+    "w1_raw00": 4,
+    "rounded01": 8,
+    "room23": 26,
+    "val1": 12,
+    "val4": 0,
+    "val7": 0,
+    "w1_raw01": 0,
+    "sigmoid0_second": 16,
+    "val2_room": 18,
+    "val5": 18,
+    "sigmoid2_first": 10,
+    "codes47": 154,
+    "codes23": 156,
+    "w1_raw1": 154,
+    "levels": 26,
+    "table": 50,
+    "expo0": 50,
+    "expo1": 58,
+    "expo2": 66,
+    "expo3": 74,
+    "expo4": 50,
+    "expo5": 58,
+    "expo67": 66,
+    "z_scales0": 58,
+    "words0": 82,
+    "words1": 98,
+    "woven0": 114,
+    "weighed": 130,
+    "z_codes0": 130,
+    "z_codes1": 138,
+    "val3": 146,
+    "val6": 146,
+    "copied0": 150,
+    "copied1": 155,
+    "copied2": 150,
+    "woven1": 146,
+    "results_early": 82,
+    "results_late": 12,
 }
-W4W_RAW_BYTES = EDGE + 4 * KIB + EDGE
-WARM_IN_BYTES = EDGE + KIB + EDGE
-W1_ROUNDED_BYTES = {0: EDGE + 4 * KIB + EDGE, 2: 2 * KIB, 4: 4 * KIB}
-SIGMOID0_FIRST_BYTES = 2 * KIB + 4 * EDGE
 
 PIECES = [(0, 256), (256, 512), (768, 512), (1280, 512), (1792, 256)]
-SCALAR_WEAVES = (1, 2)
+SCALAR_WEAVES = 3
+FIRST_PART = 1536
 
 
 def tile_list_reefer_yard_alarm_kernel(
@@ -69,321 +76,286 @@ def tile_list_reefer_yard_alarm_kernel(
     nc = tc.nc
     with ExitStack() as ctx:
         keep = ctx.enter_context(tc.tile_pool(name="keep", bufs=1))
-        laid = ctx.enter_context(tc.tile_pool(name="laid", bufs=1))
-        ring = ctx.enter_context(tc.tile_pool(name="ring", bufs=2))
-        psum = ctx.enter_context(tc.psum_pool(name="psum", bufs=BANKS_A))
+        laid_pool = ctx.enter_context(tc.tile_pool(name="laid", bufs=1))
+        psum = ctx.enter_context(tc.psum_pool(name="psum", bufs=1))
 
-        def laid_tile(shape, dtype, name):
-            return laid.tile(shape, dtype, name=name, align_bytes=64, offset=LAID_AT[name])
+        def laid(shape, dtype, place, name=None, plus=0):
+            return laid_pool.tile(shape, dtype, name=name or place, align_bytes=64, offset=AT[place] * KIB + plus)
 
-        def shared(shape, name, tag):
-            if tag in LAID_AT:
-                return laid.tile(shape, F32, name=name, tag=tag, align_bytes=64, offset=LAID_AT[tag])
-            return keep.tile(shape, F32, name=name, tag=tag, align_bytes=64)
+        turns = []
 
-        turns_a = []
-
-        def next_bank_a():
-            turns_a.append(len(turns_a) % BANKS_A)
-            return f"bank_a{turns_a[-1]}"
+        def ring_bank(shape, name):
+            turns.append(len(turns) % RING_BANKS)
+            return psum.tile(shape, F32, name=name, tag=f"bank{turns[-1]}")
 
         offs_t = keep.tile([P, S // GROUP], U16, name="offs_t")
         offs2_t = keep.tile([P, S // GROUP], U16, name="offs2_t")
-        warm_in = laid_tile([P, WARM_IN_BYTES // 4], F32, "warm_in")
         tab_sc = keep.tile([P, T], U8, name="tab_sc", tag="z_scales1", align_bytes=64)
-        w4w_raw = laid_tile([P, W4W_RAW_BYTES], U8, "w4w_raw")
+        w4s_raw = keep.tile([P, H], U8, name="w4s_raw", align_bytes=64)
+        warm_out = keep.tile([P, 8], F32, name="warm_out")
+        pages = [keep.tile([P, T2], F32, name=f"page{u}") for u in range(2)]
         bg_t = keep.tile([P, 2, 4], F32, name="bg_t")
         amb_t = keep.tile([P, 2, 4], F32, name="amb_t")
-        warm_out = keep.tile([P, 8], F32, name="warm_out")
-        page0 = keep.tile([P, T2], F32, name="page0")
-
-        zeros = keep.tile([P, H // 4], I32, name="zeros", tag="table", align_bytes=64)
-        w4s_raw = keep.tile([P, H], U8, name="w4s_raw", tag="got_w1", align_bytes=64)
-        nc.vector.memset(zeros[:], 0)
-        nc.vector.memset(warm_in[:, 0:8], 0.0)
         nc.vector.memset(tab_sc[:].bitcast(I32), 0)
-        nc.vector.tensor_copy(w4s_raw[:].bitcast(I32), zeros[:])
-        nc.vector.memset(page0[:], 0.0)
+        nc.vector.memset(w4s_raw[:].bitcast(I32), 0)
+        ident = keep.tile([P, P], F32, name="ident")
+        make_identity(nc, ident[:])
+        for page in pages:
+            nc.gpsimd.memset(page[:], 0.0)
 
-        w1_raw = {}
+        def load_w1(place, c0, c1):
+            raw = laid([P, 4, c1 - c0], F32, place)
+            nc.sync.dma_start(raw[:], w1[:, c0:c1].rearrange("(p j) c -> p j c", j=4))
+            return raw
 
-        def load_w1(b):
-            w1_raw[b] = shared([P, 4, 512], f"w1_raw{b}", ("w1_first", "w1_second")[b])
-            nc.sync.dma_start(w1_raw[b][:], w1[:, 512 * b : 512 * (b + 1)].rearrange("(p j) c -> p j c", j=4))
+        w4w_raw = [keep.tile([P, H], U8, name=f"w4w_raw{b}", align_bytes=64) for b in range(2)]
 
+        def load_w4_words(b):
+            nc.sync.dma_start(w4w_raw[b][:].bitcast(I32), w4_words[0][:, H * b : H * (b + 1)].bitcast(I32))
+
+        w1_raw00 = load_w1("w1_raw00", 0, 256)
         nc.sync.dma_start(offs_t[:], offs)
         nc.sync.dma_start(offs2_t[:], offs2)
-        nc.sync.dma_start(w4w_raw[:, 0 : 2 * H].bitcast(I32), w4_words[0].bitcast(I32))
         for r in range(4):
             nc.sync.dma_start(tab_sc[r:P:32, :].bitcast(I32), tab_scales[0, r:16:4, :].bitcast(I32))
-        tab_w = keep.tile([P, T], I32, name="tab_w", tag="table", align_bytes=64)
+        tab_w = laid([P, T], I32, "table")
         nc.sync.dma_start(tab_w[:], tab_words[0].rearrange("p t i -> p (t i)").bitcast(I32))
+        load_w4_words(0)
         for r in range(4):
             nc.sync.dma_start(w4s_raw[r:P:32, :].bitcast(I32), w4_scales[0, r:16:4, :].bitcast(I32))
-        nc.scalar.activation(warm_out[:], warm_in[:, 0:8], ACT.Sigmoid)
-        nc.gpsimd.dma_start(bg_t[:], bg.rearrange("(b p t) -> p b t", b=2, t=4))
-        nc.gpsimd.dma_start(amb_t[:], amb.rearrange("(b p t) -> p b t", b=2, t=4))
-        load_w1(0)
-        halves = [slice(BANK * h, BANK * (h + 1)) for h in range(2)]
+        w1_raw01 = load_w1("w1_raw01", 256, 512)
+        nc.sync.dma_start(bg_t[:], bg.rearrange("(b p t) -> p b t", b=2, t=4))
+        wgs_t = keep.tile([P, S], F32, name="wgs_t")
+        for half in HALVES:
+            nc.sync.dma_start(wgs_t[:, half], wgs[:, half])
+        w1_raw1 = load_w1("w1_raw1", 512, 1024)
+        load_w4_words(1)
+        nc.sync.dma_start(amb_t[:], amb.rearrange("(b p t) -> p b t", b=2, t=4))
+        nc.scalar.activation(warm_out[:], w1_raw00[:, 0, 0:8], ACT.Sigmoid)
+
+        def round_w1(rounded, raw, m0, t0, t1):
+            src = raw[:].rearrange("p j (m t) -> p m j t", t=4)
+            dst = rounded.rearrange("p (t m j) -> p m j t", m=P, j=4)
+            nc.scalar.copy(dst[:, m0 : m0 + src.shape[1], :, :], src[:, :, :, t0:t1])
+
+        room23 = laid([P, 2 * BANK], F32, "room23")
+        rounded = {0: laid([P, 8 * P], BF16, "rounded01")[:], 2: room23[:, 0:BANK].bitcast(BF16)}
+        round_w1(rounded[0], w1_raw00, 0, 0, 2)
+        round_w1(rounded[2], w1_raw00, 0, 2, 4)
+
+        got_w = [keep.tile([P, BANK], U32, name=f"got_w{h}", align_bytes=64) for h in range(2)]
+        got_s = [keep.tile([P, BANK], U8, name=f"got_s{h}", align_bytes=64) for h in range(2)]
+        list_cols = [slice(BANK // GROUP * h, BANK // GROUP * (h + 1)) for h in range(2)]
+        for h in range(2):
+            nc.vector.tensor_copy(got_s[h][:], tab_sc[:].indirect(offs_t[:, list_cols[h]]))
+        for h in range(2):
+            nc.vector.tensor_copy(got_w[h][:], tab_w[:].bitcast(U32).indirect(offs_t[:, list_cols[h]]))
+
+        w4w = [keep.tile([P, H], U8, name=f"w4w{b}", align_bytes=64) for b in range(2)]
+        w4s = [keep.tile([P, 4, P], U8, name=f"w4s{b}", align_bytes=64) for b in range(2)]
+
+        def deal_w4_words(b):
+            nc.scalar.copy(
+                w4w[b][:].bitcast(U16).rearrange("p (t m) -> p t m", t=4),
+                w4w_raw[b][:].bitcast(U16).rearrange("p (m t) -> p t m", t=4),
+            )
+
+        deal_w4_words(0)
+        for b in range(2):
+            nc.gpsimd.tensor_copy(w4s[b][:], w4s_raw[:, BANK * b : BANK * (b + 1)].rearrange("p (m t) -> p t m", t=4))
 
         expo_t = {}
 
-        def load_expo(j):
-            b, u = divmod(j, 2)
-            expo_t[j] = shared([P, 2, T2], f"expo{j}", ("table", "w1_first")[u])
+        def load_expo(k):
+            b, t = divmod(k, 4)
             rows = expo[512 * b : 512 * (b + 1), :].rearrange("(p t) m -> p t m", t=4)
-            nc.sync.dma_start(expo_t[j][:], rows[:, 2 * u : 2 * u + 2, :])
+            if k < 6:
+                expo_t[k] = laid([P, T2], F32, f"expo{k}")[:]
+                nc.sync.dma_start(expo_t[k], rows[:, t, :])
+            else:
+                expo_t[k] = []
+                for m0, width in PIECES:
+                    expo_t[k].append(laid([P, 2, width], F32, "expo67", name=f"expo67_{m0}", plus=8 * m0))
+                    nc.sync.dma_start(expo_t[k][-1][:], rows[:, 2:4, m0 : m0 + width])
 
-        got_w = [keep.tile([P, BANK], U32, name="got_w0", align_bytes=64)]
-        got_s = [keep.tile([P, BANK], U8, name=f"got_s{h}", align_bytes=64) for h in range(2)]
-        list_cols = [slice(BANK // GROUP * h, BANK // GROUP * (h + 1)) for h in range(2)]
-
-        w4w = laid_tile([P, 2 * H], U8, "w4w")
-        nc.vector.tensor_copy(
-            w4w[:].bitcast(U16).rearrange("p (b t m) -> p b t m", b=2, t=4),
-            w4w_raw[:, 0 : 2 * H].bitcast(U16).rearrange("p (b m t) -> p b t m", b=2, t=4),
-        )
-        wgs_t = shared([P, S], "wgs_t", "wgs")
-        for half in halves:
-            nc.sync.dma_start(wgs_t[:, half], wgs[:, half])
-        page1 = laid_tile([P, T2], F32, "page1")
-        nc.gpsimd.memset(page1[:], 0.0)
-        load_w1(1)
-        for h in range(2):
-            nc.vector.tensor_copy(got_s[h][:], tab_sc[:].indirect(offs_t[:, list_cols[h]]))
-        nc.vector.tensor_copy(got_w[0][:], tab_w[:].bitcast(U32).indirect(offs_t[:, list_cols[0]]))
-        w4s_dealt = w4s_raw[:].rearrange("p (b m t) -> p b t m", b=2, t=4)
-        w4s = keep.tile([P, 8, P], U8, name="w4s", align_bytes=64)
-        nc.vector.tensor_copy(w4s[:].rearrange("p (b t) m -> p b t m", b=2), w4s_dealt)
-        got_w.append(keep.tile([P, BANK], U32, name="got_w1", tag="got_w1", align_bytes=64))
-        nc.vector.tensor_copy(got_w[1][:], tab_w[:].bitcast(U32).indirect(offs_t[:, list_cols[1]]))
-        pages = [page0, page1]
-
-        ident = keep.tile([P, P], F32, name="ident")
-        make_identity(nc, ident[:])
-        lev0 = ring.tile([P, 2, T2], F32, name="lev0", tag="lev", align_bytes=64)
-        wgs_late = keep.tile([P, 8 - EARLY_BANKS, 8], F32, name="wgs_late")
-        wgs_early = lev0[:, 1, 0 : 8 * EARLY_BANKS].rearrange("p (e g) -> p e g", g=8)
-        wgs_first = lev0[:, 0, 0:8]
-        wgs_blocks = [wgs_first] + [wgs_early[:, e, :] for e in range(1, EARLY_BANKS)]
-        wgs_blocks.extend(wgs_late[:, e, :] for e in range(8 - EARLY_BANKS))
-
-        def turn_wgs():
-            for h in range(2):
-                bank = psum.tile([P, 4, P], F32, name="wgs_bank", tag=next_bank_a(), bufs=1)
-                for q in range(4):
-                    nc.tensor.transpose(bank[:, q, :], wgs_t[:, BANK * h + P * q : BANK * h + P * (q + 1)], ident[:])
-                if h == 0:
-                    nc.scalar.copy(wgs_first, bank[:, 0, 0:P:GROUP])
-                    nc.scalar.copy(wgs_early[:, 1:, :], bank[:, 1:EARLY_BANKS, 0:P:GROUP])
-                    nc.scalar.copy(wgs_late[:, 0 : 4 - EARLY_BANKS, :], bank[:, EARLY_BANKS:4, 0:P:GROUP])
-                else:
-                    nc.scalar.copy(wgs_late[:, 4 - EARLY_BANKS :, :], bank[:, :, 0:P:GROUP])
-
-        w1_codes = {}
-        w1_rounded = {}
+        expo01 = laid([P, 2, T2], F32, "expo0")
+        nc.sync.dma_start(expo01[:], expo[0:512, :].rearrange("(p t) m -> p t m", t=4)[:, 0:2, :])
+        expo_t[0], expo_t[1] = expo01[:, 0, :], expo01[:, 1, :]
+        for k in (2, 3):
+            load_expo(k)
         w1_scales = [keep.tile([P, 4 * P], U8, name=f"w1_scales{b}", align_bytes=64) for b in range(2)]
+        w1_codes = {0: keep.tile([P, 2 * P], U32, name="w1_codes0", align_bytes=64)}
 
-        def round_w1(k0, k1, cast):
-            b, t0 = divmod(k0, 4)
-            t1 = t0 + k1 - k0
-            room = laid_tile([P, W1_ROUNDED_BYTES[k0] // 2], BF16, f"w1_rounded{k0}")
-            w1_rounded[k0] = room[:, 0 : 4 * P * (k1 - k0)]
-            rounded = w1_rounded[k0].rearrange("p (t m j) -> p t m j", m=P, j=4)
-            src = w1_raw[b][:].rearrange("p j (m t) -> p m j t", t=4)
-            cast(rounded.rearrange("p t m j -> p m j t"), src[:, :, :, t0:t1])
+        def quantise(codes, scales, values):
+            nc.vector.quantize_mx(out=codes.bitcast(FP8X4), scales=scales, in_=values)
 
-        def quantise_w1(k0, k1):
-            b, t0 = divmod(k0, 4)
-            t1 = t0 + k1 - k0
-            w1_codes[k0] = laid_tile([P, P * (k1 - k0)], U32, f"w1_codes{k0}")
-            nc.vector.quantize_mx(
-                out=w1_codes[k0][:].bitcast(FP8X4),
-                scales=w1_scales[b][:, P * t0 : P * t1],
-                in_=w1_rounded[k0],
-            )
-
-        val = {}
-        val_on = {1: "plane1_gate", 2: "plane2_gate", 7: "z_codes0"}
-        turns_b = [0, 1] + [2, 0] * 7 + list(range(1, 1 + len(PIECES)))
-
-        def bank_b(width, name):
-            return psum.tile([P, width], F32, name=name, tag=f"bank_b{turns_b.pop(0) % BANKS_B}", bufs=1)
+        def product(acc, lhs, lhs_scale, rhs, rhs_scale, start=True, stop=True):
+            nc.tensor.matmul_mx(out=acc, lhsT=lhs, lhsT_scale=lhs_scale, rhs=rhs, rhs_scale=rhs_scale, start=start, stop=stop)
 
         def trust(k, h, sigmoid):
             b, t = divmod(k, 4)
-            acc = bank_b(BANK, "acc_b")
-            nc.tensor.matmul_mx(
-                out=acc[:],
-                lhsT=w4w[:, 2 * P * k : 2 * P * (k + 1)].bitcast(FP4X4),
-                lhsT_scale=w4s[:, k, :],
-                rhs=got_w[h][:].bitcast(FP8X4),
-                rhs_scale=got_s[h][:],
-                start=True,
-                stop=True,
-            )
+            acc = ring_bank([P, BANK], "acc_b")
+            lhs = w4w[b][:, 2 * P * t : 2 * P * (t + 1)].bitcast(FP4X4)
+            product(acc[:], lhs, w4s[b][:, t, :], got_w[h][:].bitcast(FP8X4), got_s[h][:])
             nc.scalar.activation(sigmoid, acc[:], ACT.Sigmoid, bias=bg_t[:, b, t : t + 1])
 
-        def gate(k):
-            val[k] = shared([P, S], f"val{k}", val_on.get(k, f"val{k}"))
-            for h in range(2):
-                trust(k, h, val[k][:, halves[h]])
-
-        def deviation(k, h):
-            acc = psum.tile([P, BANK], F32, name="acc_a", tag=next_bank_a(), bufs=1)
-            nc.tensor.matmul_mx(
-                out=acc[:],
-                lhsT=w1_codes[k - k % 2][:, P * (k % 2) : P * (k % 2 + 1)].bitcast(FP8X4),
-                lhsT_scale=w1_scales[0][:, P * k : P * (k + 1)],
-                rhs=got_w[h][:].bitcast(FP8X4),
-                rhs_scale=got_s[h][:],
-                start=True,
-                stop=True,
-            )
+        def deviation(k, h, acc):
+            lhs = w1_codes[k - k % 2][:, P * (k % 2) : P * (k % 2 + 1)].bitcast(FP8X4)
+            product(acc[:], lhs, w1_scales[0][:, P * k : P * (k + 1)], got_w[h][:].bitcast(FP8X4), got_s[h][:])
             return acc
 
-        weighed = [keep.tile([P, 4, P], F32, name=f"weighed{e}", tag=f"weighed{e}") for e in range(S // P)]
-
-        def weigh_transposed(e):
-            h, q = divmod(e, 4)
-            acc = psum.tile([P, 4, P], F32, name="acc_t", tag=next_bank_a(), bufs=1)
-            nc.tensor.matmul_mx(
-                out=acc[:].rearrange("p t m -> p (t m)"),
-                lhsT=got_w[h][:, P * q : P * (q + 1)].bitcast(FP8X4),
-                lhsT_scale=got_s[h][:, P * q : P * (q + 1)],
-                rhs=w1_codes[4][:].bitcast(FP8X4),
-                rhs_scale=w1_scales[1][:],
-                start=True,
-                stop=True,
-            )
-            for g in range(8):
-                run = slice(GROUP * g, GROUP * (g + 1))
-                weight = wgs_blocks[e][:, g : g + 1]
-                nc.scalar.activation(weighed[e][:, :, run], acc[:, :, run], ACT.Copy, scale=weight)
-
-        def turned_back(k, h):
-            acc = psum.tile([P, BANK], F32, name="acc_r", tag=next_bank_a(), bufs=1)
-            for q in range(4):
-                nc.tensor.transpose(acc[:, P * q : P * (q + 1)], weighed[4 * h + q][:, k - 4, :], ident[:])
-            return acc
-
-        def factor(k, h):
-            return deviation(k, h) if k < 4 else turned_back(k, h)
-
-        def weighed_gate(k):
-            gate(k)
-            sigmoids = val[k]
-            if k > 1:
-                val[k] = shared([P, S], f"val{k}_weighed", f"plane{k}")
-            nc.gpsimd.tensor_tensor(val[k][:], sigmoids[:], wgs_t[:], MULT)
-
-        def times_factor_on_gpsimd(k):
-            if k in copied_on_words:
-                copied = copied_on_words[k]
-            else:
-                copied = ring.tile([P, 2, BANK], F32, name="copied", tag="stage", bufs=3, align_bytes=64)[:]
-            for h in range(2):
-                nc.scalar.copy(copied[:, h, :], factor(k, h)[:])
-            gated = val[k]
-            if k == 1:
-                val[k] = shared([P, S], "val1_done", "plane1")
-            nc.gpsimd.tensor_tensor(
-                val[k][:].rearrange("p (h m) -> p h m", h=2), gated[:].rearrange("p (h m) -> p h m", h=2), copied, MULT
-            )
-
-        def gated_on_gpsimd(k):
-            gate(k)
-            times_factor_on_gpsimd(k)
+        val = {}
 
         def place(k):
-            nc.vector.tensor_copy(pages[k % 2][:].indirect(offs2_t[:]), val[k][:])
+            nc.vector.tensor_copy(pages[k % 2][:].indirect(offs2_t[:]), val[k])
 
-        words = [keep.tile([P, 2 * T2], F32, name=f"words{b}", tag=f"words{b}") for b in range(2)]
-        copied_on_words = {
-            3: words[0][:, 0:S].rearrange("p (h m) -> p h m", h=2),
-            4: words[0][:].rearrange("p (h m) -> p h m", h=2)[:, :, T2 - BANK : T2],
-            5: words[0][:, T2 : T2 + S].rearrange("p (h m) -> p h m", h=2),
-        }
-        late_lev = keep.tile([P, 3 * T2], F32, name="late_lev")
-        lev = {
-            0: lev0[:],
-            2: late_lev[:, T2 : 3 * T2].rearrange("p (t m) -> p t m", t=2),
-            3: late_lev[:, 0 : 2 * T2].rearrange("p (t m) -> p t m", t=2),
-        }
+        def gate(k, halves=(0, 1)):
+            if k not in val:
+                val[k] = laid([P, S], F32, f"val{k}")[:]
+            for h in halves:
+                trust(k, h, val[k][:, HALVES[h]])
 
-        def level(k, cols):
+        wgs_turned = keep.tile([P, S // P, 8], F32, name="wgs_turned")
+
+        def turn_wgs():
+            for h in range(2):
+                bank = ring_bank([P, 4, P], "wgs_bank")
+                for q in range(4):
+                    nc.tensor.transpose(bank[:, q, :], wgs_t[:, BANK * h + P * q : BANK * h + P * (q + 1)], ident[:])
+                nc.scalar.copy(wgs_turned[:, 4 * h : 4 * h + 4, :], bank[:, :, 0:P:GROUP])
+
+        round_w1(rounded[0], w1_raw01, P // 2, 0, 2)
+        val0_first = keep.tile([P, BANK], F32, name="val0_first")
+        sigmoid0_first = room23[:, BANK - 16 : 2 * BANK - 16]
+        trust(0, 0, sigmoid0_first)
+        sigmoid0_second = laid([P, BANK], F32, "sigmoid0_second")
+        trust(0, 1, sigmoid0_second[:])
+        quantise(w1_codes[0][:], w1_scales[0][:, 0 : 2 * P], rounded[0])
+        first_factor = deviation(0, 0, psum.tile([P, BANK], F32, name="acc_v0", tag="bank4"))
+        nc.vector.tensor_tensor(val0_first[:], sigmoid0_first, wgs_t[:, HALVES[0]], MULT)
+        nc.vector.tensor_tensor(val0_first[:], val0_first[:], first_factor[:], MULT)
+        nc.vector.tensor_copy(pages[0][:].indirect(offs2_t[:, list_cols[0]]), val0_first[:])
+
+        val0_second = room23[:, BANK : 2 * BANK]
+        nc.gpsimd.tensor_tensor(val0_second, sigmoid0_second[:], wgs_t[:, HALVES[1]], MULT)
+        copied = laid([P, BANK], F32, "copied0")
+        nc.scalar.copy(copied[:], deviation(0, 1, ring_bank([P, BANK], "acc_a"))[:])
+        nc.gpsimd.tensor_tensor(val0_second, val0_second, copied[:], MULT)
+        nc.vector.tensor_copy(pages[0][:].indirect(offs2_t[:, list_cols[1]]), val0_second)
+
+        val[1] = laid([P, S], F32, "val1")[:]
+        for h in range(2):
+            trust(1, h, val[1][:, HALVES[h]])
+        nc.gpsimd.tensor_tensor(val[1], val[1], wgs_t[:], MULT)
+        second_factor = deviation(1, 1, psum.tile([P, BANK], F32, name="acc_v1", tag="bank5"))
+        nc.vector.tensor_tensor(val[1][:, HALVES[1]], val[1][:, HALVES[1]], second_factor[:], MULT)
+
+        sigmoid2 = [laid([P, BANK], F32, "sigmoid2_first"), keep.tile([P, BANK], F32, name="sigmoid2_second")]
+        for h in range(2):
+            trust(2, h, sigmoid2[h][:])
+        round_w1(rounded[2], w1_raw01, P // 2, 2, 4)
+        val2_room = laid([P, 3 * BANK], F32, "val2_room")
+        val[2] = val2_room[:, 0:S]
+        rounded47 = val2_room[:, BANK : 3 * BANK].bitcast(BF16)
+        round_w1(rounded47, w1_raw1, 0, 0, 4)
+        nc.gpsimd.tensor_tensor(val[2][:, HALVES[0]], sigmoid2[0][:], wgs_t[:, HALVES[0]], MULT)
+        copied = laid([P, BANK], F32, "copied1")
+        nc.scalar.copy(copied[:], deviation(1, 0, ring_bank([P, BANK], "acc_a"))[:])
+        nc.gpsimd.tensor_tensor(val[1][:, HALVES[0]], val[1][:, HALVES[0]], copied[:], MULT)
+        gate(3)
+        turn_wgs()
+        deal_w4_words(1)
+        gate(4)
+        w1_codes[2] = laid([P, 2 * P], U32, "codes23")
+        quantise(w1_codes[2][:], w1_scales[0][:, 2 * P : 4 * P], rounded[2])
+        codes47 = laid([P, 4 * P], U32, "codes47")
+        quantise(codes47[:], w1_scales[1][:], rounded47)
+        place(1)
+        copied2 = laid([P, S], F32, "copied2")
+        for h in range(2):
+            nc.scalar.copy(copied2[:, HALVES[h]], deviation(2, h, ring_bank([P, BANK], "acc_a"))[:])
+        nc.gpsimd.tensor_tensor(val[2][:, HALVES[1]], sigmoid2[1][:], wgs_t[:, HALVES[1]], MULT)
+        nc.gpsimd.tensor_tensor(val[2], val[2], copied2[:], MULT)
+
+        levels = laid([P, 3 * T2], F32, "levels")
+        words = [laid([P, 2 * T2], F32, f"words{b}") for b in range(2)]
+
+        def level_of(k):
+            slot = 2 if k == 7 else k % 3
+            return levels[:, T2 * slot : T2 * (slot + 1)]
+
+        def level(k, cols=slice(0, T2)):
             b, t = divmod(k, 4)
-            j, u = divmod(k, 2)
-            if j not in lev:
-                lev[j] = ring.tile([P, 2, T2], F32, name=f"lev{j}", tag="lev", align_bytes=64)[:]
-            nc.scalar.activation(lev[j][:, u, cols], pages[u][:, cols], ACT.Identity, bias=amb_t[:, b, t : t + 1])
+            nc.scalar.activation(level_of(k)[:, cols], pages[k % 2][:, cols], ACT.Identity, bias=amb_t[:, b, t : t + 1])
 
-        def expose(eng, j, cols):
+        def pair_words(j, cols):
             at = T2 * (j % 2)
-            eng.tensor_tensor(
-                words[j // 2][:, at + cols.start : at + cols.stop].bitcast(BF16).rearrange("p (c i t) -> p c t i", i=4, t=2),
-                lev[j][:, :, cols].rearrange("p t (c i) -> p c t i", i=4),
-                expo_t[j][:, :, cols].rearrange("p t (c i) -> p c t i", i=4),
+            return words[j // 2][:, at + cols.start : at + cols.stop].bitcast(BF16)
+
+        def expose(k, cols=slice(0, T2)):
+            dst = pair_words(k // 2, cols).rearrange("p (m t) -> p m t", t=2)[:, :, k % 2]
+            nc.gpsimd.tensor_tensor(dst, level_of(k)[:, cols], expo_t[k][:, cols], MULT)
+
+        def expose_pair(engine, j, pair_levels, pair_expo, cols):
+            engine.tensor_tensor(
+                pair_words(j, cols).rearrange("p (c i t) -> p c t i", i=4, t=2),
+                pair_levels[:, :, cols].rearrange("p t (c i) -> p c t i", i=4),
+                pair_expo.rearrange("p t (c i) -> p c t i", i=4),
                 MULT,
             )
-
-        def expose_part(j, part):
-            cut = FIRST_PART if j == 0 else T2 // 2
-            expose(nc.gpsimd, j, (slice(0, cut), slice(cut, T2))[part])
-            if part == 1:
-                load_expo(j + 2)
 
         def both_pairs(b, cols):
             return words[b][:].rearrange("p (u m) -> p u m", u=2)[:, :, cols].rearrange("p u (c i) -> p c u i", i=4)
 
-        all_cols = slice(0, T2)
+        weighed = [laid([P, 4, P], F32, "weighed", name=f"weighed{e}", plus=2 * KIB * e) for e in range(S // P)]
 
-        sigmoid0 = [
-            laid_tile([P, SIGMOID0_FIRST_BYTES // 4], F32, "sigmoid0_first"),
-            laid_tile([P, BANK], F32, "sigmoid0_second"),
-        ]
-        trust(0, 0, sigmoid0[0][:, 0:BANK])
-        trust(0, 1, sigmoid0[1][:])
-        round_w1(0, 2, nc.vector.tensor_copy)
-        quantise_w1(0, 2)
-        load_expo(0)
-        val0 = [laid_tile([P, BANK], F32, "val0_first")]
-        nc.vector.tensor_tensor(val0[0][:], sigmoid0[0][:, 0:BANK], wgs_t[:, halves[0]], MULT)
-        val0.append(laid_tile([P, BANK], F32, "val0_second"))
-        nc.gpsimd.tensor_tensor(val0[1][:], sigmoid0[1][:], wgs_t[:, halves[1]], MULT)
-        nc.vector.tensor_tensor(val0[0][:], val0[0][:], deviation(0, 0)[:], MULT)
-        nc.vector.tensor_copy(page0[:].indirect(offs2_t[:, list_cols[0]]), val0[0][:])
-        second_factor = deviation(0, 1)
-        weighed_gate(1)
-        round_w1(2, 4, nc.scalar.copy)
-        round_w1(4, 8, nc.scalar.copy)
-        quantise_w1(4, 8)
-        done = laid_tile([P, BANK], F32, "val0_done")
-        nc.vector.tensor_tensor(done[:], val0[1][:], second_factor[:], MULT)
-        quantise_w1(2, 4)
-        nc.vector.tensor_copy(page0[:].indirect(offs2_t[:, list_cols[1]]), done[:])
-        load_expo(1)
+        def weigh_transposed(e):
+            h, q = divmod(e, 4)
+            acc = ring_bank([P, 4, P], "acc_t")
+            lhs = got_w[h][:, P * q : P * (q + 1)].bitcast(FP8X4)
+            lhs_scale = got_s[h][:, P * q : P * (q + 1)]
+            product(acc[:].rearrange("p t m -> p (t m)"), lhs, lhs_scale, codes47[:].bitcast(FP8X4), w1_scales[1][:])
+            for g in range(8):
+                run = slice(GROUP * g, GROUP * (g + 1))
+                nc.scalar.activation(weighed[e][:, :, run], acc[:, :, run], ACT.Copy, scale=wgs_turned[:, e, g : g + 1])
 
-        times_factor_on_gpsimd(1)
-        weighed_gate(2)
-        times_factor_on_gpsimd(2)
-        place(1)
-        turn_wgs()
-        weighed_gate(3)
-        times_factor_on_gpsimd(3)
-        weigh_transposed(0)
-        level(0, all_cols)
-        place(2)
-        for e in range(1, EARLY_BANKS):
+        def turned_back(k, h, acc):
+            for q in range(4):
+                nc.tensor.transpose(acc[:, P * q : P * (q + 1)], weighed[4 * h + q][:, k - 4, :], ident[:])
+            return acc
+
+        copied_on = {
+            3: words[0][:, 0:S],
+            4: words[0][:, FIRST_PART : FIRST_PART + S],
+            5: words[1][:, 0:S],
+            6: words[0][:, T2 + S : 2 * T2],
+            7: words[1][:, S:T2],
+        }
+
+        def copy_factor(k, halves=(0, 1)):
+            factor = deviation if k < 4 else turned_back
+            for h in halves:
+                nc.scalar.copy(copied_on[k][:, HALVES[h]], factor(k, h, ring_bank([P, BANK], "acc_a"))[:])
+
+        def times_factor(k):
+            nc.gpsimd.tensor_tensor(val[k], val[k], copied_on[k], MULT)
+
+        copy_factor(3)
+        level(0)
+        nc.gpsimd.tensor_tensor(val[3], val[3], wgs_t[:], MULT)
+        times_factor(3)
+        for e in range(4):
             weigh_transposed(e)
-        level(1, slice(0, FIRST_PART))
-        level(1, slice(FIRST_PART, T2))
-        expose_part(0, 0)
-        for e in range(EARLY_BANKS, 8):
+        place(2)
+        level(1)
+        first_part = slice(0, FIRST_PART)
+        expose(0, first_part)
+        copy_factor(4, (0,))
+        for e in range(4, 8):
             weigh_transposed(e)
         place(3)
 
-        w8w = laid.tile([P, 2, N], I32, name="w8w", tag="w1_second", align_bytes=64, offset=LAID_AT["w1_second"])
+        w8w = keep.tile([P, 2, N], I32, name="w8w", align_bytes=64)
         nc.sync.dma_start(w8w[:], w8_words.rearrange("a p c i -> p a (c i)").bitcast(I32))
         w8s = w1_scales[0]
         for quad in range(4):
@@ -392,91 +364,105 @@ def tile_list_reefer_yard_alarm_kernel(
                 w8_scales[:, 4 * quad : 4 * quad + 4, :].bitcast(I32),
             )
 
-        gated_on_gpsimd(4)
-        expose_part(0, 1)
-        level(2, all_cols)
+        expose(1, first_part)
+        gate(5, (0,))
+        copy_factor(4, (1,))
+        times_factor(4)
+        level(2)
         place(4)
-        gated_on_gpsimd(5)
-        level(3, all_cols)
-        expose_part(1, 0)
+        expose_pair(nc.gpsimd, 0, levels[:].rearrange("p (s m) -> p s m", s=3)[:, 0:2, :], expo01[:, :, FIRST_PART:T2], slice(FIRST_PART, T2))
+        load_expo(4)
+        load_expo(5)
+        gate(5, (1,))
+        copy_factor(5)
+        times_factor(5)
+        gate(6)
+        copy_factor(6)
+        times_factor(6)
+        level(3)
         place(5)
-        gated_on_gpsimd(6)
+        expose(2)
         gate(7)
-        copied7 = words[0][:, T2 + S : T2 + S + SHARE7]
-        nc.scalar.copy(copied7[:, halves[0]], factor(7, 0)[:])
-        second7 = factor(7, 1)
-        nc.scalar.copy(copied7[:, BANK:SHARE7], second7[:, 0 : SHARE7 - BANK])
-        nc.vector.tensor_tensor(val[7][:, SHARE7:S], val[7][:, SHARE7:S], second7[:, SHARE7 - BANK : BANK], MULT)
-        nc.gpsimd.tensor_tensor(val[7][:, 0:SHARE7], val[7][:, 0:SHARE7], copied7, MULT)
-        expose_part(1, 1)
-        level(4, all_cols)
+        copy_factor(7, (0,))
+        last_factor = turned_back(7, 1, psum.tile([P, BANK], F32, name="acc_v7", tag="bank4"))
+        nc.vector.tensor_tensor(val[7][:, HALVES[1]], val[7][:, HALVES[1]], last_factor[:], MULT)
+        level(4)
         place(6)
-        for half in range(2):
-            cols = slice(T2 // 2 * half, T2 // 2 * (half + 1))
-            level(5, cols)
-            expose(nc.gpsimd, 2, cols)
-        woven0 = ring.tile([P, T2, 2], F32, name="woven0", tag="lev", align_bytes=64)
+        expose(3)
+        load_expo(6)
+        nc.gpsimd.tensor_tensor(val[7][:, HALVES[0]], val[7][:, HALVES[0]], copied_on[7][:, HALVES[0]], MULT)
+        level(5)
+        expose(4)
+        woven0 = laid([P, T2, 2], F32, "woven0")
         for c in range(T2 // BANK):
             cols = slice(BANK * c, BANK * (c + 1))
             nc.scalar.copy(woven0[:, cols, :].rearrange("p (c i) u -> p c u i", i=4), both_pairs(0, cols))
-        level(6, all_cols)
+        level(6)
         place(7)
+        expose(5)
 
-        z_codes = [
-            keep.tile([P, T2], U32, name="z_codes0", tag="z_codes0", align_bytes=64),
-            laid.tile([P, T2], U32, name="z_codes1", align_bytes=64, offset=LAID_AT["z_codes1"]),
-        ]
-        z_scales = [
-            keep.tile([P, T2], U8, name=f"z_scales{b}", tag=("table", "z_scales1")[b], align_bytes=64) for b in range(2)
-        ]
+        z_codes1 = laid([P, T2], U32, "z_codes1")
+        z_codes = {}
+        z_scales = [laid([P, T2], U8, "z_scales0"), keep.tile([P, T2], U8, name="z_scales1", tag="z_scales1", align_bytes=64)]
+        cols_of = [slice(m0, m0 + width) for m0, width in PIECES]
+        last_levels = levels[:].rearrange("p (s m) -> p s m", s=3)[:, 0:3:2, :]
+        woven1 = {}
+        accs = {}
+        tail_turns = []
+        results_used = {"results_early": 0, "results_late": 0}
 
-        def quantise(b, cols, woven):
-            codes, scales = z_codes[b][:, cols], z_scales[b][:, cols]
-            nc.vector.quantize_mx(
-                out=codes.bitcast(FP8X4), scales=scales, in_=woven.rearrange("p m u -> p (m u)").bitcast(BF16)
-            )
-            return codes, scales
-
-        spare = keep.tile([P, 2 * T2], F32, name="spare", tag="words0")
-        used = 0
-        for i, (m0, width) in enumerate(PIECES):
-            cols = slice(m0, m0 + width)
-            level(7, cols)
-            if m0 // WIDE != (m0 + width) // WIDE or m0 == 0:
-                wide = slice(WIDE * ((m0 + width) // WIDE), WIDE * ((m0 + width) // WIDE + 1))
-                if wide.stop <= T2:
-                    quantise(0, wide, woven0[:, wide, :])
-            z = [(z_codes[0][:, cols], z_scales[0][:, cols])]
-            expose(nc.vector, 3, cols)
-            woven1 = ring.tile([P, width, 2], F32, name="woven1", tag="stage", bufs=3, align_bytes=64)
-            weave = nc.scalar.copy if i in SCALAR_WEAVES else nc.vector.tensor_copy
-            weave(woven1[:].rearrange("p (c i) u -> p c u i", i=4), both_pairs(1, cols))
-            z.append(quantise(1, cols, woven1[:]))
-            accs = [
-                psum.tile([P, width], F32, name="acc_o0", tag=next_bank_a(), bufs=1),
-                bank_b(width, "acc_o1"),
-                psum.tile([P, width], F32, name="acc_o2", tag=next_bank_a(), bufs=1),
-            ]
-            for b in range(2):
-                for nb in range(N // P):
-                    nc.tensor.matmul_mx(
-                        out=accs[nb][:],
-                        lhsT=w8w[:, b, P * nb : P * (nb + 1)].bitcast(FP8X4),
-                        lhsT_scale=w8s[4 * (b + 1) : P, P * nb : P * (nb + 1)],
-                        rhs=z[b][0].bitcast(FP8X4),
-                        rhs_scale=z[b][1],
-                        start=(b == 0),
-                        stop=(b == 1),
-                    )
+        def quantise_z(b, i):
+            woven = woven0[:, cols_of[i], :] if b == 0 else woven1[i][:]
+            values = woven.rearrange("p m u -> p (m u)").bitcast(BF16)
+            if b == 1:
+                z_codes[b, i] = z_codes1[:, cols_of[i]]
+            elif i < 2:
+                z_codes[b, i] = laid([P, PIECES[i][1]], U32, "z_codes0", name=f"z_codes0_{i}", plus=4 * PIECES[i][0])[:]
+            else:
+                z_codes[b, i] = laid([P, PIECES[i][1]], U32, "expo67", name=f"z_codes0_{i}", plus=8 * PIECES[i - 2][0])[:]
+            quantise(z_codes[b, i], z_scales[b][:, cols_of[i]], values)
             for nb in range(N // P):
-                store = i * (N // P) + nb
-                if store < len(weighed):
-                    res = keep.tile([P, width], F32, name="res", tag=f"weighed{store}")[:]
-                else:
-                    res = spare[:, used : used + width]
-                    used = used + width
-                if i == len(PIECES) - 1 and nb > 0:
-                    nc.vector.tensor_copy(res, accs[nb][:])
-                else:
-                    nc.scalar.copy(res, accs[nb][:])
-                nc.sync.dma_start(out[P * nb : P * (nb + 1), cols], res)
+                if b == 0:
+                    tail_turns.append(len(tail_turns) % 8)
+                    accs[i, nb] = psum.tile([P, PIECES[i][1]], F32, name="acc_o", tag=f"bank{tail_turns[-1]}")
+                lhs = w8w[:, b, P * nb : P * (nb + 1)].bitcast(FP8X4)
+                lhs_scale = w8s[4 * (b + 1) : P, P * nb : P * (nb + 1)]
+                rhs = z_codes[b, i].bitcast(FP8X4)
+                product(accs[i, nb][:], lhs, lhs_scale, rhs, z_scales[b][:, cols_of[i]], start=b == 0, stop=b == 1)
+
+        def expose_last_pair(i):
+            expose_pair(nc.vector, 3, last_levels, expo_t[6][i][:], cols_of[i])
+
+        def weave(i):
+            woven1[i] = laid([P, PIECES[i][1], 2], F32, "woven1", name=f"woven1_{i}", plus=4 * KIB * (i % 3))
+            copy = nc.scalar.copy if i < SCALAR_WEAVES else nc.vector.tensor_copy
+            copy(woven1[i][:].rearrange("p (c i) u -> p c u i", i=4), both_pairs(1, cols_of[i]))
+
+        def store(i, on_vector):
+            width = PIECES[i][1]
+            for nb in range(N // P):
+                room = "results_early" if results_used["results_early"] + 4 * width <= 16 * KIB else "results_late"
+                res = laid([P, width], F32, room, name=f"res{i}_{nb}", plus=results_used[room])
+                results_used[room] = results_used[room] + 4 * width
+                copy = nc.vector.tensor_copy if nb in on_vector else nc.scalar.copy
+                copy(res[:], accs[i, nb][:])
+                nc.sync.dma_start(out[P * nb : P * (nb + 1), cols_of[i]], res[:])
+
+        last = len(PIECES) - 1
+        for i in range(2):
+            level(7, cols_of[i])
+            quantise_z(0, i)
+        for i in range(2):
+            expose_last_pair(i)
+            weave(i)
+        for i in range(2, last + 1):
+            level(7, cols_of[i])
+            quantise_z(1, i - 2)
+            quantise_z(0, i)
+            expose_last_pair(i)
+            store(i - 2, ())
+            weave(i)
+        quantise_z(1, last - 1)
+        quantise_z(1, last)
+        store(last - 1, ())
+        store(last, (1, 2))

@@ -36,37 +36,35 @@ AT = {
     "val2_room": 18,
     "val5": 18,
     "sigmoid2_first": 10,
-    "codes47": 154,
-    "codes23": 156,
-    "w1_raw1": 154,
+    "codes47": 162,
+    "codes23": 164,
+    "w1_raw1": 162,
     "levels": 26,
-    "table": 50,
-    "expo0": 50,
-    "expo1": 58,
-    "expo2": 66,
-    "expo3": 74,
-    "expo4": 50,
-    "expo5": 58,
-    "expo67": 66,
-    "z_scales0": 58,
-    "words0": 82,
-    "words1": 98,
-    "woven0": 114,
-    "weighed": 130,
-    "z_codes0": 130,
-    "z_codes1": 138,
-    "val3": 146,
-    "val6": 146,
-    "copied0": 150,
-    "copied1": 155,
-    "copied2": 150,
-    "woven1": 146,
-    "results_early": 82,
+    "table": 58,
+    "expo01": 58,
+    "expo23": 74,
+    "expo45": 58,
+    "expo67": 74,
+    "z_scales0": 66,
+    "words0": 90,
+    "words1": 106,
+    "woven0": 122,
+    "weighed": 138,
+    "z_codes0": 138,
+    "z_codes1": 146,
+    "val3": 154,
+    "val6": 154,
+    "copied0": 158,
+    "copied1": 163,
+    "copied2": 158,
+    "woven1": 154,
+    "results_early": 90,
     "results_late": 12,
 }
 
 PIECES = [(0, 256), (256, 512), (768, 512), (1280, 512), (1792, 256)]
 SCALAR_WEAVES = 3
+LEVEL_SLOT = (2, 3, 0, 1, 2, 3, 0, 3)
 FIRST_PART = 1536
 
 
@@ -166,23 +164,20 @@ def tile_list_reefer_yard_alarm_kernel(
 
         expo_t = {}
 
-        def load_expo(k):
-            b, t = divmod(k, 4)
-            rows = expo[512 * b : 512 * (b + 1), :].rearrange("(p t) m -> p t m", t=4)
-            if k < 6:
-                expo_t[k] = laid([P, T2], F32, f"expo{k}")[:]
-                nc.sync.dma_start(expo_t[k], rows[:, t, :])
+        def load_expo(j):
+            b, u = divmod(j, 2)
+            rows = expo[512 * b : 512 * (b + 1), :].rearrange("(p t) m -> p t m", t=4)[:, 2 * u : 2 * u + 2, :]
+            if j < 3:
+                expo_t[j] = laid([P, 2, T2], F32, f"expo{2 * j}{2 * j + 1}")
+                nc.sync.dma_start(expo_t[j][:], rows)
             else:
-                expo_t[k] = []
+                expo_t[j] = []
                 for m0, width in PIECES:
-                    expo_t[k].append(laid([P, 2, width], F32, "expo67", name=f"expo67_{m0}", plus=8 * m0))
-                    nc.sync.dma_start(expo_t[k][-1][:], rows[:, 2:4, m0 : m0 + width])
+                    expo_t[j].append(laid([P, 2, width], F32, "expo67", name=f"expo67_{m0}", plus=8 * m0))
+                    nc.sync.dma_start(expo_t[j][-1][:], rows[:, :, m0 : m0 + width])
 
-        expo01 = laid([P, 2, T2], F32, "expo0")
-        nc.sync.dma_start(expo01[:], expo[0:512, :].rearrange("(p t) m -> p t m", t=4)[:, 0:2, :])
-        expo_t[0], expo_t[1] = expo01[:, 0, :], expo01[:, 1, :]
-        for k in (2, 3):
-            load_expo(k)
+        for j in range(2):
+            load_expo(j)
         w1_scales = [keep.tile([P, 4 * P], U8, name=f"w1_scales{b}", align_bytes=64) for b in range(2)]
         w1_codes = {0: keep.tile([P, 2 * P], U32, name="w1_codes0", align_bytes=64)}
 
@@ -277,11 +272,11 @@ def tile_list_reefer_yard_alarm_kernel(
         nc.gpsimd.tensor_tensor(val[2][:, HALVES[1]], sigmoid2[1][:], wgs_t[:, HALVES[1]], MULT)
         nc.gpsimd.tensor_tensor(val[2], val[2], copied2[:], MULT)
 
-        levels = laid([P, 3 * T2], F32, "levels")
+        levels = laid([P, 4 * T2], F32, "levels")
         words = [laid([P, 2 * T2], F32, f"words{b}") for b in range(2)]
 
         def level_of(k):
-            slot = 2 if k == 7 else k % 3
+            slot = LEVEL_SLOT[k]
             return levels[:, T2 * slot : T2 * (slot + 1)]
 
         def level(k, cols=slice(0, T2)):
@@ -292,11 +287,12 @@ def tile_list_reefer_yard_alarm_kernel(
             at = T2 * (j % 2)
             return words[j // 2][:, at + cols.start : at + cols.stop].bitcast(BF16)
 
-        def expose(k, cols=slice(0, T2)):
-            dst = pair_words(k // 2, cols).rearrange("p (m t) -> p m t", t=2)[:, :, k % 2]
-            nc.gpsimd.tensor_tensor(dst, level_of(k)[:, cols], expo_t[k][:, cols], MULT)
+        def expose(j, cols):
+            expose_pair(nc.gpsimd, j, expo_t[j][:, :, cols], cols)
 
-        def expose_pair(engine, j, pair_levels, pair_expo, cols):
+        def expose_pair(engine, j, pair_expo, cols):
+            first, second = LEVEL_SLOT[2 * j], LEVEL_SLOT[2 * j + 1]
+            pair_levels = levels[:].rearrange("p (s m) -> p s m", s=4)[:, first : second + 1 : second - first, :]
             engine.tensor_tensor(
                 pair_words(j, cols).rearrange("p (c i t) -> p c t i", i=4, t=2),
                 pair_levels[:, :, cols].rearrange("p t (c i) -> p c t i", i=4),
@@ -328,8 +324,8 @@ def tile_list_reefer_yard_alarm_kernel(
             3: words[0][:, 0:S],
             4: words[0][:, FIRST_PART : FIRST_PART + S],
             5: words[1][:, 0:S],
-            6: words[0][:, T2 + S : 2 * T2],
-            7: words[1][:, S:T2],
+            6: words[0][:, T2 + BANK : T2 + 3 * BANK],
+            7: words[0][:, T2 + 3 * BANK : 2 * T2],
         }
 
         def copy_factor(k, halves=(0, 1)):
@@ -344,12 +340,13 @@ def tile_list_reefer_yard_alarm_kernel(
         level(0)
         nc.gpsimd.tensor_tensor(val[3], val[3], wgs_t[:], MULT)
         times_factor(3)
-        for e in range(4):
+        for e in range(2):
             weigh_transposed(e)
         place(2)
         level(1)
-        first_part = slice(0, FIRST_PART)
-        expose(0, first_part)
+        expose(0, slice(0, FIRST_PART))
+        for e in range(2, 4):
+            weigh_transposed(e)
         copy_factor(4, (0,))
         for e in range(4, 8):
             weigh_transposed(e)
@@ -364,15 +361,13 @@ def tile_list_reefer_yard_alarm_kernel(
                 w8_scales[:, 4 * quad : 4 * quad + 4, :].bitcast(I32),
             )
 
-        expose(1, first_part)
         gate(5, (0,))
         copy_factor(4, (1,))
         times_factor(4)
         level(2)
         place(4)
-        expose_pair(nc.gpsimd, 0, levels[:].rearrange("p (s m) -> p s m", s=3)[:, 0:2, :], expo01[:, :, FIRST_PART:T2], slice(FIRST_PART, T2))
-        load_expo(4)
-        load_expo(5)
+        expose(0, slice(FIRST_PART, T2))
+        load_expo(2)
         gate(5, (1,))
         copy_factor(5)
         times_factor(5)
@@ -381,31 +376,29 @@ def tile_list_reefer_yard_alarm_kernel(
         times_factor(6)
         level(3)
         place(5)
-        expose(2)
+        expose(1, slice(0, S))
         gate(7)
         copy_factor(7, (0,))
         last_factor = turned_back(7, 1, psum.tile([P, BANK], F32, name="acc_v7", tag="bank4"))
         nc.vector.tensor_tensor(val[7][:, HALVES[1]], val[7][:, HALVES[1]], last_factor[:], MULT)
         level(4)
         place(6)
-        expose(3)
-        load_expo(6)
-        nc.gpsimd.tensor_tensor(val[7][:, HALVES[0]], val[7][:, HALVES[0]], copied_on[7][:, HALVES[0]], MULT)
+        nc.gpsimd.tensor_tensor(val[7][:, HALVES[0]], val[7][:, HALVES[0]], copied_on[7], MULT)
+        expose(1, slice(S, T2))
+        load_expo(3)
         level(5)
-        expose(4)
         woven0 = laid([P, T2, 2], F32, "woven0")
         for c in range(T2 // BANK):
             cols = slice(BANK * c, BANK * (c + 1))
             nc.scalar.copy(woven0[:, cols, :].rearrange("p (c i) u -> p c u i", i=4), both_pairs(0, cols))
         level(6)
         place(7)
-        expose(5)
+        expose(2, slice(0, T2))
 
         z_codes1 = laid([P, T2], U32, "z_codes1")
         z_codes = {}
         z_scales = [laid([P, T2], U8, "z_scales0"), keep.tile([P, T2], U8, name="z_scales1", tag="z_scales1", align_bytes=64)]
         cols_of = [slice(m0, m0 + width) for m0, width in PIECES]
-        last_levels = levels[:].rearrange("p (s m) -> p s m", s=3)[:, 0:3:2, :]
         woven1 = {}
         accs = {}
         tail_turns = []
@@ -431,7 +424,7 @@ def tile_list_reefer_yard_alarm_kernel(
                 product(accs[i, nb][:], lhs, lhs_scale, rhs, z_scales[b][:, cols_of[i]], start=b == 0, stop=b == 1)
 
         def expose_last_pair(i):
-            expose_pair(nc.vector, 3, last_levels, expo_t[6][i][:], cols_of[i])
+            expose_pair(nc.vector, 3, expo_t[3][i][:], cols_of[i])
 
         def weave(i):
             woven1[i] = laid([P, PIECES[i][1], 2], F32, "woven1", name=f"woven1_{i}", plus=4 * KIB * (i % 3))

@@ -60,6 +60,8 @@ AT = {
     "woven1": 154,
     "results_early": 90,
     "results_late": 12,
+    "page1": 170,
+    "ident": 178,
 }
 
 PIECES = [(0, 256), (256, 512), (768, 512), (1280, 512), (1792, 256)]
@@ -91,15 +93,17 @@ def tile_list_reefer_yard_alarm_kernel(
         tab_sc = keep.tile([P, T], U8, name="tab_sc", tag="z_scales1", align_bytes=64)
         w4s_raw = keep.tile([P, H], U8, name="w4s_raw", align_bytes=64)
         warm_out = keep.tile([P, 8], F32, name="warm_out")
-        pages = [keep.tile([P, T2], F32, name=f"page{u}") for u in range(2)]
+        zeros = laid([P, H // 4], I32, "ident", name="zeros", plus=-H // 2)
         bg_t = keep.tile([P, 2, 4], F32, name="bg_t")
         amb_t = keep.tile([P, 2, 4], F32, name="amb_t")
         nc.vector.memset(tab_sc[:].bitcast(I32), 0)
-        nc.vector.memset(w4s_raw[:].bitcast(I32), 0)
-        ident = keep.tile([P, P], F32, name="ident")
+        nc.vector.memset(zeros[:], 0)
+        nc.vector.tensor_copy(w4s_raw[:].bitcast(I32), zeros[:])
+        pages = [keep.tile([P, T2], F32, name="page0"), laid([P, T2], F32, "page1")]
+        nc.vector.memset(pages[0][:], 0.0)
+        ident = laid([P, P], F32, "ident")
         make_identity(nc, ident[:])
-        for page in pages:
-            nc.gpsimd.memset(page[:], 0.0)
+        nc.gpsimd.memset(pages[1][:], 0.0)
 
         def load_w1(place, c0, c1):
             raw = laid([P, 4, c1 - c0], F32, place)

@@ -27,18 +27,18 @@ HALVES = [slice(0, BANK), slice(BANK, 2 * BANK)]
 AT = {
     "w1_raw00": 4,
     "rounded01": 8,
-    "room23": 26,
+    "rounded23": 162,
+    "val0_second": 162,
     "val1": 12,
     "val4": 0,
     "val7": 0,
-    "w1_raw01": 0,
+    "w1_raw01": 14,
     "sigmoid0_second": 16,
     "val2_room": 18,
     "val5": 18,
     "sigmoid2_first": 10,
-    "codes47": 162,
-    "codes23": 164,
-    "w1_raw1": 162,
+    "codes47": 24,
+    "w1_raw1": 24,
     "levels": 26,
     "table": 58,
     "expo01": 58,
@@ -55,7 +55,7 @@ AT = {
     "val3": 154,
     "val6": 154,
     "copied0": 158,
-    "copied1": 163,
+    "copied1": 25,
     "copied2": 158,
     "woven1": 154,
     "results_early": 90,
@@ -64,8 +64,9 @@ AT = {
     "ident": 178,
 }
 
-PIECES = [(0, 256), (256, 512), (768, 512), (1280, 512), (1792, 256)]
+PIECES = [(0, 256), (256, 512), (768, 512), (1280, 256), (1536, 256), (1792, 256)]
 SCALAR_WEAVES = 3
+SCALAR_LAST = 2
 LEVEL_SLOT = (2, 3, 0, 1, 2, 3, 0, 3)
 FIRST_PART = 1536
 
@@ -94,7 +95,7 @@ def tile_list_reefer_yard_alarm_kernel(
         w4s_raw = keep.tile([P, H], U8, name="w4s_raw", align_bytes=64)
         warm_out = keep.tile([P, 8], F32, name="warm_out")
         zeros = laid([P, H // 4], I32, "ident", name="zeros", plus=-H // 2)
-        bg_t = keep.tile([P, 2, 4], F32, name="bg_t")
+        bg_t = [keep.tile([P, 4], F32, name=f"bg_t{b}") for b in range(2)]
         amb_t = keep.tile([P, 2, 4], F32, name="amb_t")
         nc.vector.memset(tab_sc[:].bitcast(I32), 0)
         nc.vector.memset(zeros[:], 0)
@@ -117,7 +118,6 @@ def tile_list_reefer_yard_alarm_kernel(
 
         w1_raw00 = load_w1("w1_raw00", 0, 256)
         nc.sync.dma_start(offs_t[:], offs)
-        nc.sync.dma_start(offs2_t[:], offs2)
         for r in range(4):
             nc.sync.dma_start(tab_sc[r:P:32, :].bitcast(I32), tab_scales[0, r:16:4, :].bitcast(I32))
         tab_w = laid([P, T], I32, "table")
@@ -125,23 +125,24 @@ def tile_list_reefer_yard_alarm_kernel(
         load_w4_words(0)
         for r in range(4):
             nc.sync.dma_start(w4s_raw[r:P:32, :].bitcast(I32), w4_scales[0, r:16:4, :].bitcast(I32))
+        nc.sync.dma_start(bg_t[0][:], bg[0:512].rearrange("(p t) -> p t", t=4))
+        nc.sync.dma_start(offs2_t[:], offs2)
         w1_raw01 = load_w1("w1_raw01", 256, 512)
-        nc.sync.dma_start(bg_t[:], bg.rearrange("(b p t) -> p b t", b=2, t=4))
         wgs_t = keep.tile([P, S], F32, name="wgs_t")
         for half in HALVES:
             nc.sync.dma_start(wgs_t[:, half], wgs[:, half])
         w1_raw1 = load_w1("w1_raw1", 512, 1024)
         load_w4_words(1)
+        nc.sync.dma_start(bg_t[1][:], bg[512:1024].rearrange("(p t) -> p t", t=4))
         nc.sync.dma_start(amb_t[:], amb.rearrange("(b p t) -> p b t", b=2, t=4))
         nc.scalar.activation(warm_out[:], w1_raw00[:, 0, 0:8], ACT.Sigmoid)
 
-        def round_w1(rounded, raw, m0, t0, t1):
+        def round_w1(rounded, raw, m0, t0, t1, cast=nc.scalar.copy):
             src = raw[:].rearrange("p j (m t) -> p m j t", t=4)
             dst = rounded.rearrange("p (t m j) -> p m j t", m=P, j=4)
-            nc.scalar.copy(dst[:, m0 : m0 + src.shape[1], :, :], src[:, :, :, t0:t1])
+            cast(dst[:, m0 : m0 + src.shape[1], :, :], src[:, :, :, t0:t1])
 
-        room23 = laid([P, 2 * BANK], F32, "room23")
-        rounded = {0: laid([P, 8 * P], BF16, "rounded01")[:], 2: room23[:, 0:BANK].bitcast(BF16)}
+        rounded = {0: laid([P, 8 * P], BF16, "rounded01")[:], 2: laid([P, 8 * P], BF16, "rounded23")[:]}
         round_w1(rounded[0], w1_raw00, 0, 0, 2)
         round_w1(rounded[2], w1_raw00, 0, 2, 4)
 
@@ -183,7 +184,7 @@ def tile_list_reefer_yard_alarm_kernel(
         for j in range(2):
             load_expo(j)
         w1_scales = [keep.tile([P, 4 * P], U8, name=f"w1_scales{b}", align_bytes=64) for b in range(2)]
-        w1_codes = {0: keep.tile([P, 2 * P], U32, name="w1_codes0", align_bytes=64)}
+        w1_codes = {k: keep.tile([P, 2 * P], U32, name=f"w1_codes{k}", align_bytes=64) for k in (0, 2)}
 
         def quantise(codes, scales, values):
             nc.vector.quantize_mx(out=codes.bitcast(FP8X4), scales=scales, in_=values)
@@ -196,7 +197,7 @@ def tile_list_reefer_yard_alarm_kernel(
             acc = ring_bank([P, BANK], "acc_b")
             lhs = w4w[b][:, 2 * P * t : 2 * P * (t + 1)].bitcast(FP4X4)
             product(acc[:], lhs, w4s[b][:, t, :], got_w[h][:].bitcast(FP8X4), got_s[h][:])
-            nc.scalar.activation(sigmoid, acc[:], ACT.Sigmoid, bias=bg_t[:, b, t : t + 1])
+            nc.scalar.activation(sigmoid, acc[:], ACT.Sigmoid, bias=bg_t[b][:, t : t + 1])
 
         def deviation(k, h, acc):
             lhs = w1_codes[k - k % 2][:, P * (k % 2) : P * (k % 2 + 1)].bitcast(FP8X4)
@@ -223,19 +224,20 @@ def tile_list_reefer_yard_alarm_kernel(
                     nc.tensor.transpose(bank[:, q, :], wgs_t[:, BANK * h + P * q : BANK * h + P * (q + 1)], ident[:])
                 nc.scalar.copy(wgs_turned[:, 4 * h : 4 * h + 4, :], bank[:, :, 0:P:GROUP])
 
-        round_w1(rounded[0], w1_raw01, P // 2, 0, 2)
         val0_first = keep.tile([P, BANK], F32, name="val0_first")
-        sigmoid0_first = room23[:, BANK - 16 : 2 * BANK - 16]
-        trust(0, 0, sigmoid0_first)
+        trust(0, 0, val0_first[:])
+        round_w1(rounded[0], w1_raw01, P // 2, 0, 2, nc.vector.tensor_copy)
+        round_w1(rounded[2], w1_raw01, P // 2, 2, 4)
         sigmoid0_second = laid([P, BANK], F32, "sigmoid0_second")
         trust(0, 1, sigmoid0_second[:])
         quantise(w1_codes[0][:], w1_scales[0][:, 0 : 2 * P], rounded[0])
         first_factor = deviation(0, 0, psum.tile([P, BANK], F32, name="acc_v0", tag="bank4"))
-        nc.vector.tensor_tensor(val0_first[:], sigmoid0_first, wgs_t[:, HALVES[0]], MULT)
+        nc.vector.tensor_tensor(val0_first[:], val0_first[:], wgs_t[:, HALVES[0]], MULT)
+        quantise(w1_codes[2][:], w1_scales[0][:, 2 * P : 4 * P], rounded[2])
         nc.vector.tensor_tensor(val0_first[:], val0_first[:], first_factor[:], MULT)
         nc.vector.tensor_copy(pages[0][:].indirect(offs2_t[:, list_cols[0]]), val0_first[:])
 
-        val0_second = room23[:, BANK : 2 * BANK]
+        val0_second = laid([P, BANK], F32, "val0_second")[:]
         nc.gpsimd.tensor_tensor(val0_second, sigmoid0_second[:], wgs_t[:, HALVES[1]], MULT)
         copied = laid([P, BANK], F32, "copied0")
         nc.scalar.copy(copied[:], deviation(0, 1, ring_bank([P, BANK], "acc_a"))[:])
@@ -252,7 +254,6 @@ def tile_list_reefer_yard_alarm_kernel(
         sigmoid2 = [laid([P, BANK], F32, "sigmoid2_first"), keep.tile([P, BANK], F32, name="sigmoid2_second")]
         for h in range(2):
             trust(2, h, sigmoid2[h][:])
-        round_w1(rounded[2], w1_raw01, P // 2, 2, 4)
         val2_room = laid([P, 3 * BANK], F32, "val2_room")
         val[2] = val2_room[:, 0:S]
         rounded47 = val2_room[:, BANK : 3 * BANK].bitcast(BF16)
@@ -261,18 +262,13 @@ def tile_list_reefer_yard_alarm_kernel(
         copied = laid([P, BANK], F32, "copied1")
         nc.scalar.copy(copied[:], deviation(1, 0, ring_bank([P, BANK], "acc_a"))[:])
         nc.gpsimd.tensor_tensor(val[1][:, HALVES[0]], val[1][:, HALVES[0]], copied[:], MULT)
-        gate(3)
-        turn_wgs()
-        deal_w4_words(1)
-        gate(4)
-        w1_codes[2] = laid([P, 2 * P], U32, "codes23")
-        quantise(w1_codes[2][:], w1_scales[0][:, 2 * P : 4 * P], rounded[2])
-        codes47 = laid([P, 4 * P], U32, "codes47")
-        quantise(codes47[:], w1_scales[1][:], rounded47)
-        place(1)
         copied2 = laid([P, S], F32, "copied2")
         for h in range(2):
             nc.scalar.copy(copied2[:, HALVES[h]], deviation(2, h, ring_bank([P, BANK], "acc_a"))[:])
+        gate(3)
+        codes47 = laid([P, 4 * P], U32, "codes47")
+        quantise(codes47[:], w1_scales[1][:], rounded47)
+        place(1)
         nc.gpsimd.tensor_tensor(val[2][:, HALVES[1]], sigmoid2[1][:], wgs_t[:, HALVES[1]], MULT)
         nc.gpsimd.tensor_tensor(val[2], val[2], copied2[:], MULT)
 
@@ -341,6 +337,9 @@ def tile_list_reefer_yard_alarm_kernel(
             nc.gpsimd.tensor_tensor(val[k], val[k], copied_on[k], MULT)
 
         copy_factor(3)
+        turn_wgs()
+        deal_w4_words(1)
+        gate(4)
         level(0)
         nc.gpsimd.tensor_tensor(val[3], val[3], wgs_t[:], MULT)
         times_factor(3)
@@ -452,14 +451,25 @@ def tile_list_reefer_yard_alarm_kernel(
         for i in range(2):
             expose_last_pair(i)
             weave(i)
-        for i in range(2, last + 1):
+        for i in range(2, last):
             level(7, cols_of[i])
             quantise_z(1, i - 2)
+            if i > SCALAR_LAST + 1:
+                weave(i - 1)
             quantise_z(0, i)
             expose_last_pair(i)
             store(i - 2, ())
-            weave(i)
+            if i <= SCALAR_LAST:
+                weave(i)
+        level(7, cols_of[last])
+        quantise_z(1, last - 2)
+        weave(last - 1)
+        i = last
+        expose_last_pair(i)
+        store(last - 2, ())
         quantise_z(1, last - 1)
+        weave(last)
+        quantise_z(0, last)
         quantise_z(1, last)
         store(last - 1, ())
         store(last, (1, 2))

@@ -28,15 +28,17 @@ AT = {
     "w1_raw00": 4,
     "rounded01": 8,
     "rounded23": 162,
-    "val0_second": 162,
-    "val1": 12,
+    "val1_first": 162,
+    "val1_second": 13,
+    "sigmoid1_first": 14,
+    "val0_second": 16,
+    "val2": 4,
+    "rounded47": 18,
+    "val2_done": 18,
     "val4": 0,
     "val7": 0,
     "w1_raw01": 14,
-    "sigmoid0_second": 16,
-    "val2_room": 18,
     "val5": 18,
-    "sigmoid2_first": 10,
     "codes47": 24,
     "w1_raw1": 24,
     "levels": 26,
@@ -54,8 +56,9 @@ AT = {
     "z_codes1": 146,
     "val3": 154,
     "val6": 154,
-    "copied0": 158,
-    "copied1": 25,
+    "copied1_first": 158,
+    "copied0_second": 160,
+    "copied1_second": 25,
     "copied2": 158,
     "woven1": 154,
     "results_early": 90,
@@ -118,15 +121,15 @@ def tile_list_reefer_yard_alarm_kernel(
 
         w1_raw00 = load_w1("w1_raw00", 0, 256)
         nc.sync.dma_start(offs_t[:], offs)
+        nc.sync.dma_start(offs2_t[:], offs2)
         for r in range(4):
             nc.sync.dma_start(tab_sc[r:P:32, :].bitcast(I32), tab_scales[0, r:16:4, :].bitcast(I32))
         tab_w = laid([P, T], I32, "table")
         nc.sync.dma_start(tab_w[:], tab_words[0].rearrange("p t i -> p (t i)").bitcast(I32))
-        load_w4_words(0)
         for r in range(4):
             nc.sync.dma_start(w4s_raw[r:P:32, :].bitcast(I32), w4_scales[0, r:16:4, :].bitcast(I32))
+        load_w4_words(0)
         nc.sync.dma_start(bg_t[0][:], bg[0:512].rearrange("(p t) -> p t", t=4))
-        nc.sync.dma_start(offs2_t[:], offs2)
         w1_raw01 = load_w1("w1_raw01", 256, 512)
         wgs_t = keep.tile([P, S], F32, name="wgs_t")
         for half in HALVES:
@@ -228,8 +231,8 @@ def tile_list_reefer_yard_alarm_kernel(
         trust(0, 0, val0_first[:])
         round_w1(rounded[0], w1_raw01, P // 2, 0, 2, nc.vector.tensor_copy)
         round_w1(rounded[2], w1_raw01, P // 2, 2, 4)
-        sigmoid0_second = laid([P, BANK], F32, "sigmoid0_second")
-        trust(0, 1, sigmoid0_second[:])
+        sigmoid1_first = laid([P, BANK], F32, "sigmoid1_first")
+        trust(1, 0, sigmoid1_first[:])
         quantise(w1_codes[0][:], w1_scales[0][:, 0 : 2 * P], rounded[0])
         first_factor = deviation(0, 0, psum.tile([P, BANK], F32, name="acc_v0", tag="bank4"))
         nc.vector.tensor_tensor(val0_first[:], val0_first[:], wgs_t[:, HALVES[0]], MULT)
@@ -237,40 +240,44 @@ def tile_list_reefer_yard_alarm_kernel(
         nc.vector.tensor_tensor(val0_first[:], val0_first[:], first_factor[:], MULT)
         nc.vector.tensor_copy(pages[0][:].indirect(offs2_t[:, list_cols[0]]), val0_first[:])
 
+        def weigh(dst, src, h):
+            nc.gpsimd.tensor_tensor(dst, src, wgs_t[:, HALVES[h]], MULT)
+
+        def finish_half(k, h, values, place_of_copy):
+            copied = laid([P, BANK], F32, place_of_copy)
+            nc.scalar.copy(copied[:], deviation(k, h, ring_bank([P, BANK], "acc_a"))[:])
+            nc.gpsimd.tensor_tensor(values, values, copied[:], MULT)
+
+        def place_half(k, h, values):
+            nc.vector.tensor_copy(pages[k][:].indirect(offs2_t[:, list_cols[h]]), values)
+
+        val1_first = laid([P, BANK], F32, "val1_first")[:]
+        weigh(val1_first, sigmoid1_first[:], 0)
+        finish_half(1, 0, val1_first, "copied1_first")
+        place_half(1, 0, val1_first)
         val0_second = laid([P, BANK], F32, "val0_second")[:]
-        nc.gpsimd.tensor_tensor(val0_second, sigmoid0_second[:], wgs_t[:, HALVES[1]], MULT)
-        copied = laid([P, BANK], F32, "copied0")
-        nc.scalar.copy(copied[:], deviation(0, 1, ring_bank([P, BANK], "acc_a"))[:])
-        nc.gpsimd.tensor_tensor(val0_second, val0_second, copied[:], MULT)
-        nc.vector.tensor_copy(pages[0][:].indirect(offs2_t[:, list_cols[1]]), val0_second)
-
-        val[1] = laid([P, S], F32, "val1")[:]
-        for h in range(2):
-            trust(1, h, val[1][:, HALVES[h]])
-        nc.gpsimd.tensor_tensor(val[1], val[1], wgs_t[:], MULT)
-        second_factor = deviation(1, 1, psum.tile([P, BANK], F32, name="acc_v1", tag="bank5"))
-        nc.vector.tensor_tensor(val[1][:, HALVES[1]], val[1][:, HALVES[1]], second_factor[:], MULT)
-
-        sigmoid2 = [laid([P, BANK], F32, "sigmoid2_first"), keep.tile([P, BANK], F32, name="sigmoid2_second")]
-        for h in range(2):
-            trust(2, h, sigmoid2[h][:])
-        val2_room = laid([P, 3 * BANK], F32, "val2_room")
-        val[2] = val2_room[:, 0:S]
-        rounded47 = val2_room[:, BANK : 3 * BANK].bitcast(BF16)
-        round_w1(rounded47, w1_raw1, 0, 0, 4)
-        nc.gpsimd.tensor_tensor(val[2][:, HALVES[0]], sigmoid2[0][:], wgs_t[:, HALVES[0]], MULT)
-        copied = laid([P, BANK], F32, "copied1")
-        nc.scalar.copy(copied[:], deviation(1, 0, ring_bank([P, BANK], "acc_a"))[:])
-        nc.gpsimd.tensor_tensor(val[1][:, HALVES[0]], val[1][:, HALVES[0]], copied[:], MULT)
+        trust(0, 1, val0_second)
+        weigh(val0_second, val0_second, 1)
+        finish_half(0, 1, val0_second, "copied0_second")
+        place_half(0, 1, val0_second)
+        val1_second = laid([P, BANK], F32, "val1_second")[:]
+        trust(1, 1, val1_second)
+        weigh(val1_second, val1_second, 1)
+        gate(2)
+        nc.gpsimd.tensor_tensor(val[2], val[2], wgs_t[:], MULT)
+        rounded47 = laid([P, 16 * P], BF16, "rounded47")
+        round_w1(rounded47[:], w1_raw1, 0, 0, 4)
+        finish_half(1, 1, val1_second, "copied1_second")
         copied2 = laid([P, S], F32, "copied2")
         for h in range(2):
             nc.scalar.copy(copied2[:, HALVES[h]], deviation(2, h, ring_bank([P, BANK], "acc_a"))[:])
         gate(3)
         codes47 = laid([P, 4 * P], U32, "codes47")
-        quantise(codes47[:], w1_scales[1][:], rounded47)
-        place(1)
-        nc.gpsimd.tensor_tensor(val[2][:, HALVES[1]], sigmoid2[1][:], wgs_t[:, HALVES[1]], MULT)
-        nc.gpsimd.tensor_tensor(val[2], val[2], copied2[:], MULT)
+        quantise(codes47[:], w1_scales[1][:], rounded47[:])
+        place_half(1, 1, val1_second)
+        weighed2 = val[2]
+        val[2] = laid([P, S], F32, "val2_done")[:]
+        nc.gpsimd.tensor_tensor(val[2], weighed2, copied2[:], MULT)
 
         levels = laid([P, 4 * T2], F32, "levels")
         words = [laid([P, 2 * T2], F32, f"words{b}") for b in range(2)]
@@ -343,15 +350,11 @@ def tile_list_reefer_yard_alarm_kernel(
         level(0)
         nc.gpsimd.tensor_tensor(val[3], val[3], wgs_t[:], MULT)
         times_factor(3)
-        for e in range(2):
-            weigh_transposed(e)
+        weigh_transposed(0)
         place(2)
         level(1)
         expose(0, slice(0, FIRST_PART))
-        for e in range(2, 4):
-            weigh_transposed(e)
-        copy_factor(4, (0,))
-        for e in range(4, 8):
+        for e in range(1, 8):
             weigh_transposed(e)
         place(3)
 
@@ -364,14 +367,13 @@ def tile_list_reefer_yard_alarm_kernel(
                 w8_scales[:, 4 * quad : 4 * quad + 4, :].bitcast(I32),
             )
 
-        gate(5, (0,))
-        copy_factor(4, (1,))
+        copy_factor(4)
         times_factor(4)
         level(2)
         place(4)
         expose(0, slice(FIRST_PART, T2))
         load_expo(2)
-        gate(5, (1,))
+        gate(5)
         copy_factor(5)
         times_factor(5)
         gate(6)
@@ -471,5 +473,5 @@ def tile_list_reefer_yard_alarm_kernel(
         weave(last)
         quantise_z(0, last)
         quantise_z(1, last)
-        store(last - 1, ())
+        store(last - 1, (1, 2))
         store(last, (1, 2))

@@ -329,10 +329,10 @@ def tile_list_reefer_yard_alarm_kernel(
 
         copied_on = {
             3: words[0][:, 0:S],
-            4: words[0][:, FIRST_PART : FIRST_PART + S],
+            4: words[0][:, FIRST_PART : FIRST_PART + BANK],
             5: words[1][:, 0:S],
-            6: words[0][:, T2 + BANK : T2 + 3 * BANK],
-            7: words[0][:, T2 + 3 * BANK : 2 * T2],
+            6: words[0][:, T2 : T2 + S],
+            7: words[1][:, S:T2],
         }
 
         def copy_factor(k, halves=(0, 1)):
@@ -346,15 +346,18 @@ def tile_list_reefer_yard_alarm_kernel(
         copy_factor(3)
         turn_wgs()
         deal_w4_words(1)
-        gate(4)
         level(0)
+        gate(4)
         nc.gpsimd.tensor_tensor(val[3], val[3], wgs_t[:], MULT)
         times_factor(3)
         weigh_transposed(0)
         place(2)
         level(1)
         expose(0, slice(0, FIRST_PART))
-        for e in range(1, 8):
+        for e in range(1, 4):
+            weigh_transposed(e)
+        copy_factor(4, (0,))
+        for e in range(4, 8):
             weigh_transposed(e)
         place(3)
 
@@ -367,8 +370,9 @@ def tile_list_reefer_yard_alarm_kernel(
                 w8_scales[:, 4 * quad : 4 * quad + 4, :].bitcast(I32),
             )
 
-        copy_factor(4)
-        times_factor(4)
+        nc.gpsimd.tensor_tensor(val[4][:, HALVES[0]], val[4][:, HALVES[0]], copied_on[4], MULT)
+        second_factor = turned_back(4, 1, psum.tile([P, BANK], F32, name="acc_v4", tag="bank4"))
+        nc.vector.tensor_tensor(val[4][:, HALVES[1]], val[4][:, HALVES[1]], second_factor[:], MULT)
         level(2)
         place(4)
         expose(0, slice(FIRST_PART, T2))
@@ -381,16 +385,13 @@ def tile_list_reefer_yard_alarm_kernel(
         times_factor(6)
         level(3)
         place(5)
-        expose(1, slice(0, S))
+        expose(1, slice(0, T2))
+        load_expo(3)
         gate(7)
-        copy_factor(7, (0,))
-        last_factor = turned_back(7, 1, psum.tile([P, BANK], F32, name="acc_v7", tag="bank4"))
-        nc.vector.tensor_tensor(val[7][:, HALVES[1]], val[7][:, HALVES[1]], last_factor[:], MULT)
+        copy_factor(7)
         level(4)
         place(6)
-        nc.gpsimd.tensor_tensor(val[7][:, HALVES[0]], val[7][:, HALVES[0]], copied_on[7], MULT)
-        expose(1, slice(S, T2))
-        load_expo(3)
+        times_factor(7)
         level(5)
         woven0 = laid([P, T2, 2], F32, "woven0")
         for c in range(T2 // BANK):

@@ -25,7 +25,6 @@ RING_BANKS = 4
 HALVES = [slice(0, BANK), slice(BANK, 2 * BANK)]
 
 AT = {
-    "w1_raw00": 4,
     "rounded01": 8,
     "rounded23": 162,
     "val1_first": 162,
@@ -37,7 +36,7 @@ AT = {
     "val2_done": 18,
     "val4": 0,
     "val7": 0,
-    "w1_raw01": 14,
+    "w1_raw0": 10,
     "val5": 18,
     "codes47": 24,
     "w1_raw1": 24,
@@ -103,6 +102,7 @@ def tile_list_reefer_yard_alarm_kernel(
         nc.vector.memset(tab_sc[:].bitcast(I32), 0)
         nc.vector.memset(zeros[:], 0)
         nc.vector.tensor_copy(w4s_raw[:].bitcast(I32), zeros[:])
+        nc.scalar.activation(warm_out[:], zeros[:, 0:8].bitcast(F32), ACT.Sigmoid)
         pages = [keep.tile([P, T2], F32, name="page0"), laid([P, T2], F32, "page1")]
         nc.vector.memset(pages[0][:], 0.0)
         ident = laid([P, P], F32, "ident")
@@ -119,18 +119,17 @@ def tile_list_reefer_yard_alarm_kernel(
         def load_w4_words(b):
             nc.sync.dma_start(w4w_raw[b][:].bitcast(I32), w4_words[0][:, H * b : H * (b + 1)].bitcast(I32))
 
-        w1_raw00 = load_w1("w1_raw00", 0, 256)
         nc.sync.dma_start(offs_t[:], offs)
         nc.sync.dma_start(offs2_t[:], offs2)
+        load_w4_words(0)
         for r in range(4):
             nc.sync.dma_start(tab_sc[r:P:32, :].bitcast(I32), tab_scales[0, r:16:4, :].bitcast(I32))
         tab_w = laid([P, T], I32, "table")
         nc.sync.dma_start(tab_w[:], tab_words[0].rearrange("p t i -> p (t i)").bitcast(I32))
         for r in range(4):
             nc.sync.dma_start(w4s_raw[r:P:32, :].bitcast(I32), w4_scales[0, r:16:4, :].bitcast(I32))
-        load_w4_words(0)
         nc.sync.dma_start(bg_t[0][:], bg[0:512].rearrange("(p t) -> p t", t=4))
-        w1_raw01 = load_w1("w1_raw01", 256, 512)
+        w1_raw0 = load_w1("w1_raw0", 0, 512)
         wgs_t = keep.tile([P, S], F32, name="wgs_t")
         for half in HALVES:
             nc.sync.dma_start(wgs_t[:, half], wgs[:, half])
@@ -138,7 +137,6 @@ def tile_list_reefer_yard_alarm_kernel(
         load_w4_words(1)
         nc.sync.dma_start(bg_t[1][:], bg[512:1024].rearrange("(p t) -> p t", t=4))
         nc.sync.dma_start(amb_t[:], amb.rearrange("(b p t) -> p b t", b=2, t=4))
-        nc.scalar.activation(warm_out[:], w1_raw00[:, 0, 0:8], ACT.Sigmoid)
 
         def round_w1(rounded, raw, m0, t0, t1, cast=nc.scalar.copy):
             src = raw[:].rearrange("p j (m t) -> p m j t", t=4)
@@ -146,8 +144,6 @@ def tile_list_reefer_yard_alarm_kernel(
             cast(dst[:, m0 : m0 + src.shape[1], :, :], src[:, :, :, t0:t1])
 
         rounded = {0: laid([P, 8 * P], BF16, "rounded01")[:], 2: laid([P, 8 * P], BF16, "rounded23")[:]}
-        round_w1(rounded[0], w1_raw00, 0, 0, 2)
-        round_w1(rounded[2], w1_raw00, 0, 2, 4)
 
         got_w = [keep.tile([P, BANK], U32, name=f"got_w{h}", align_bytes=64) for h in range(2)]
         got_s = [keep.tile([P, BANK], U8, name=f"got_s{h}", align_bytes=64) for h in range(2)]
@@ -229,8 +225,8 @@ def tile_list_reefer_yard_alarm_kernel(
 
         val0_first = keep.tile([P, BANK], F32, name="val0_first")
         trust(0, 0, val0_first[:])
-        round_w1(rounded[0], w1_raw01, P // 2, 0, 2, nc.vector.tensor_copy)
-        round_w1(rounded[2], w1_raw01, P // 2, 2, 4)
+        round_w1(rounded[0], w1_raw0, 0, 0, 2, nc.vector.tensor_copy)
+        round_w1(rounded[2], w1_raw0, 0, 2, 4)
         sigmoid1_first = laid([P, BANK], F32, "sigmoid1_first")
         trust(1, 0, sigmoid1_first[:])
         quantise(w1_codes[0][:], w1_scales[0][:, 0 : 2 * P], rounded[0])

@@ -66,9 +66,9 @@ AT = {
     "ident": 178,
 }
 
-PIECES = [(0, 256), (256, 512), (768, 512), (1280, 256), (1536, 256), (1792, 256)]
-SCALAR_WEAVES = 3
-SCALAR_LAST = 2
+PIECE = 256
+PIECES = T2 // PIECE
+SCALAR_WEAVES = 5
 LEVEL_SLOT = (2, 3, 0, 1, 2, 3, 0, 3)
 FIRST_PART = 1536
 
@@ -120,19 +120,19 @@ def tile_list_reefer_yard_alarm_kernel(
             nc.sync.dma_start(w4w_raw[b][:].bitcast(I32), w4_words[0][:, H * b : H * (b + 1)].bitcast(I32))
 
         nc.sync.dma_start(offs_t[:], offs)
-        nc.sync.dma_start(offs2_t[:], offs2)
         load_w4_words(0)
+        nc.sync.dma_start(bg_t[0][:], bg[0:512].rearrange("(p t) -> p t", t=4))
         for r in range(4):
             nc.sync.dma_start(tab_sc[r:P:32, :].bitcast(I32), tab_scales[0, r:16:4, :].bitcast(I32))
         tab_w = laid([P, T], I32, "table")
         nc.sync.dma_start(tab_w[:], tab_words[0].rearrange("p t i -> p (t i)").bitcast(I32))
         for r in range(4):
             nc.sync.dma_start(w4s_raw[r:P:32, :].bitcast(I32), w4_scales[0, r:16:4, :].bitcast(I32))
-        nc.sync.dma_start(bg_t[0][:], bg[0:512].rearrange("(p t) -> p t", t=4))
         w1_raw0 = load_w1("w1_raw0", 0, 512)
         wgs_t = keep.tile([P, S], F32, name="wgs_t")
         for half in HALVES:
             nc.sync.dma_start(wgs_t[:, half], wgs[:, half])
+        nc.sync.dma_start(offs2_t[:], offs2)
         w1_raw1 = load_w1("w1_raw1", 512, 1024)
         load_w4_words(1)
         nc.sync.dma_start(bg_t[1][:], bg[512:1024].rearrange("(p t) -> p t", t=4))
@@ -176,9 +176,9 @@ def tile_list_reefer_yard_alarm_kernel(
                 nc.sync.dma_start(expo_t[j][:], rows)
             else:
                 expo_t[j] = []
-                for m0, width in PIECES:
-                    expo_t[j].append(laid([P, 2, width], F32, "expo67", name=f"expo67_{m0}", plus=8 * m0))
-                    nc.sync.dma_start(expo_t[j][-1][:], rows[:, :, m0 : m0 + width])
+                for m0 in range(0, T2, PIECE):
+                    expo_t[j].append(laid([P, 2, PIECE], F32, "expo67", name=f"expo67_{m0}", plus=8 * m0))
+                    nc.sync.dma_start(expo_t[j][-1][:], rows[:, :, m0 : m0 + PIECE])
 
         for j in range(2):
             load_expo(j)
@@ -398,77 +398,65 @@ def tile_list_reefer_yard_alarm_kernel(
         expose(2, slice(0, T2))
 
         z_codes1 = laid([P, T2], U32, "z_codes1")
-        z_codes = {}
         z_scales = [laid([P, T2], U8, "z_scales0"), keep.tile([P, T2], U8, name="z_scales1", tag="z_scales1", align_bytes=64)]
-        cols_of = [slice(m0, m0 + width) for m0, width in PIECES]
         woven1 = {}
         accs = {}
         tail_turns = []
-        results_used = {"results_early": 0, "results_late": 0}
 
-        def quantise_z(b, i):
-            woven = woven0[:, cols_of[i], :] if b == 0 else woven1[i][:]
-            values = woven.rearrange("p m u -> p (m u)").bitcast(BF16)
-            if b == 1:
-                z_codes[b, i] = z_codes1[:, cols_of[i]]
-            elif i < 2:
-                z_codes[b, i] = laid([P, PIECES[i][1]], U32, "z_codes0", name=f"z_codes0_{i}", plus=4 * PIECES[i][0])[:]
-            else:
-                z_codes[b, i] = laid([P, PIECES[i][1]], U32, "expo67", name=f"z_codes0_{i}", plus=8 * PIECES[i - 2][0])[:]
-            quantise(z_codes[b, i], z_scales[b][:, cols_of[i]], values)
+        def cols_of(i):
+            return slice(PIECE * i, PIECE * (i + 1))
+
+        def multiply(b, i, codes):
             for nb in range(N // P):
                 if b == 0:
                     tail_turns.append(len(tail_turns) % 8)
-                    accs[i, nb] = psum.tile([P, PIECES[i][1]], F32, name="acc_o", tag=f"bank{tail_turns[-1]}")
+                    accs[i, nb] = psum.tile([P, PIECE], F32, name="acc_o", tag=f"bank{tail_turns[-1]}")
                 lhs = w8w[:, b, P * nb : P * (nb + 1)].bitcast(FP8X4)
                 lhs_scale = w8s[4 * (b + 1) : P, P * nb : P * (nb + 1)]
-                rhs = z_codes[b, i].bitcast(FP8X4)
-                product(accs[i, nb][:], lhs, lhs_scale, rhs, z_scales[b][:, cols_of[i]], start=b == 0, stop=b == 1)
+                product(accs[i, nb][:], lhs, lhs_scale, codes.bitcast(FP8X4), z_scales[b][:, cols_of(i)], b == 0, b == 1)
 
-        def expose_last_pair(i):
-            expose_pair(nc.vector, 3, expo_t[3][i][:], cols_of[i])
+        def first_pass(i):
+            if i < 2:
+                codes = laid([P, PIECE], U32, "z_codes0", name=f"z_codes0_{i}", plus=4 * PIECE * i)
+            else:
+                codes = laid([P, PIECE], U32, "expo67", name=f"z_codes0_{i}", plus=8 * PIECE * (i - 2))
+            values = woven0[:, cols_of(i), :].rearrange("p m u -> p (m u)").bitcast(BF16)
+            quantise(codes[:], z_scales[0][:, cols_of(i)], values)
+            multiply(0, i, codes[:])
 
-        def weave(i):
-            woven1[i] = laid([P, PIECES[i][1], 2], F32, "woven1", name=f"woven1_{i}", plus=4 * KIB * (i % 3))
-            copy = nc.scalar.copy if i < SCALAR_WEAVES else nc.vector.tensor_copy
-            copy(woven1[i][:].rearrange("p (c i) u -> p c u i", i=4), both_pairs(1, cols_of[i]))
+        def second_pass(i):
+            values = woven1[i][:].rearrange("p m u -> p (m u)").bitcast(BF16)
+            quantise(z_codes1[:, cols_of(i)], z_scales[1][:, cols_of(i)], values)
+            multiply(1, i, z_codes1[:, cols_of(i)])
+
+        def weave(i, copy):
+            woven1[i] = laid([P, PIECE, 2], F32, "woven1", name=f"woven1_{i}", plus=8 * PIECE * (i % 4))
+            copy(woven1[i][:].rearrange("p (c i) u -> p c u i", i=4), both_pairs(1, cols_of(i)))
 
         def store(i, on_vector):
-            width = PIECES[i][1]
+            room, slot = ("results_early", i) if i < 5 else ("results_late", i - 5)
             for nb in range(N // P):
-                room = "results_early" if results_used["results_early"] + 4 * width <= 16 * KIB else "results_late"
-                res = laid([P, width], F32, room, name=f"res{i}_{nb}", plus=results_used[room])
-                results_used[room] = results_used[room] + 4 * width
+                res = laid([P, PIECE], F32, room, name=f"res{i}_{nb}", plus=4 * PIECE * (3 * slot + nb))
                 copy = nc.vector.tensor_copy if nb in on_vector else nc.scalar.copy
                 copy(res[:], accs[i, nb][:])
-                nc.sync.dma_start(out[P * nb : P * (nb + 1), cols_of[i]], res[:])
+                nc.sync.dma_start(out[P * nb : P * (nb + 1), cols_of(i)], res[:])
 
-        last = len(PIECES) - 1
-        for i in range(2):
-            level(7, cols_of[i])
-            quantise_z(0, i)
-        for i in range(2):
-            expose_last_pair(i)
-            weave(i)
-        for i in range(2, last):
-            level(7, cols_of[i])
-            quantise_z(1, i - 2)
-            if i > SCALAR_LAST + 1:
-                weave(i - 1)
-            quantise_z(0, i)
-            expose_last_pair(i)
-            store(i - 2, ())
-            if i <= SCALAR_LAST:
-                weave(i)
-        level(7, cols_of[last])
-        quantise_z(1, last - 2)
-        weave(last - 1)
-        i = last
-        expose_last_pair(i)
-        store(last - 2, ())
-        quantise_z(1, last - 1)
-        weave(last)
-        quantise_z(0, last)
-        quantise_z(1, last)
-        store(last - 1, (1, 2))
-        store(last, (1, 2))
+        for i in range(PIECES):
+            level(7, cols_of(i))
+            if i >= 2:
+                second_pass(i - 2)
+            if i - 1 >= SCALAR_WEAVES:
+                weave(i - 1, nc.vector.tensor_copy)
+            if i < PIECES - 1:
+                first_pass(i)
+            expose_pair(nc.vector, 3, expo_t[3][i][:], cols_of(i))
+            if i >= 2:
+                store(i - 2, ())
+            if i < SCALAR_WEAVES:
+                weave(i, nc.scalar.copy)
+        second_pass(PIECES - 2)
+        weave(PIECES - 1, nc.vector.tensor_copy)
+        first_pass(PIECES - 1)
+        second_pass(PIECES - 1)
+        for i in range(PIECES - 2, PIECES):
+            store(i, (1, 2))

from contextlib import ExitStack

import concourse.mybir as mybir
from concourse.masks import make_identity

K, T, S, H, T2, N = 512, 2048, 1024, 1024, 2048, 384
FLOPS = 2 * K * H * S * 2 + 2 * H * N * T2

F32 = mybir.dt.float32
BF16 = mybir.dt.bfloat16
I32 = mybir.dt.int32
U32 = mybir.dt.uint32
U16 = mybir.dt.uint16
U8 = mybir.dt.uint8
FP8X4 = mybir.dt.float8_e4m3fn_x4
FP4X4 = mybir.dt.float4_e2m1fn_x4
ACT = mybir.ActivationFunctionType
MULT = mybir.AluOpType.mult

P = 128
BANK = 512
GROUP = 16
KIB = 1024
RING_BANKS = 4
HALVES = [slice(0, BANK), slice(BANK, 2 * BANK)]

AT = {
    "rounded01": 8,
    "rounded23": 162,
    "val1_first": 162,
    "val1_second": 13,
    "sigmoid1_first": 14,
    "val0_second": 16,
    "val2": 4,
    "rounded47": 18,
    "val2_done": 18,
    "val4": 0,
    "val7": 0,
    "w1_raw0": 10,
    "val5": 18,
    "codes47": 24,
    "w1_raw1": 24,
    "levels": 26,
    "table": 58,
    "expo01": 58,
    "expo23": 74,
    "expo45": 58,
    "expo67": 74,
    "z_scales0": 66,
    "words0": 90,
    "words1": 106,
    "woven0": 122,
    "weighed": 138,
    "z_codes0": 138,
    "z_codes1": 146,
    "val3": 154,
    "val6": 154,
    "copied1_first": 158,
    "copied0_second": 160,
    "copied1_second": 25,
    "copied2": 158,
    "woven1": 154,
    "results_early": 90,
    "results_late": 12,
    "page1": 170,
    "ident": 178,
}

PIECE = 256
PIECES = T2 // PIECE
SCALAR_WEAVES = 5
LEVEL_SLOT = (2, 3, 0, 1, 2, 3, 0, 3)
FIRST_PART = 1536


def tile_list_reefer_yard_alarm_kernel(
    tc, tab_words, tab_scales, offs, w1, w4_words, w4_scales, bg, wgs, offs2, amb, expo, w8_words, w8_scales, out
):
    nc = tc.nc
    with ExitStack() as ctx:
        keep = ctx.enter_context(tc.tile_pool(name="keep", bufs=1))
        laid_pool = ctx.enter_context(tc.tile_pool(name="laid", bufs=1))
        psum = ctx.enter_context(tc.psum_pool(name="psum", bufs=1))

        def laid(shape, dtype, place, name=None, plus=0):
            return laid_pool.tile(shape, dtype, name=name or place, align_bytes=64, offset=AT[place] * KIB + plus)

        turns = []

        def ring_bank(shape, name):
            turns.append(len(turns) % RING_BANKS)
            return psum.tile(shape, F32, name=name, tag=f"bank{turns[-1]}")

        offs_t = keep.tile([P, S // GROUP], U16, name="offs_t")
        offs2_t = keep.tile([P, S // GROUP], U16, name="offs2_t")
        tab_sc = keep.tile([P, T], U8, name="tab_sc", tag="z_scales1", align_bytes=64)
        w4s_raw = keep.tile([P, H], U8, name="w4s_raw", align_bytes=64)
        warm_out = keep.tile([P, 8], F32, name="warm_out")
        zeros = laid([P, H // 4], I32, "ident", name="zeros", plus=-H // 2)
        bg_t = [keep.tile([P, 4], F32, name=f"bg_t{b}") for b in range(2)]
        amb_t = keep.tile([P, 2, 4], F32, name="amb_t")
        nc.vector.memset(tab_sc[:].bitcast(I32), 0)
        nc.vector.memset(zeros[:], 0)
        nc.vector.tensor_copy(w4s_raw[:].bitcast(I32), zeros[:])
        nc.scalar.activation(warm_out[:], zeros[:, 0:8].bitcast(F32), ACT.Sigmoid)
        pages = [keep.tile([P, T2], F32, name="page0"), laid([P, T2], F32, "page1")]
        nc.vector.memset(pages[0][:], 0.0)
        ident = laid([P, P], F32, "ident")
        make_identity(nc, ident[:])
        nc.gpsimd.memset(pages[1][:], 0.0)

        def load_w1(place, c0, c1):
            raw = laid([P, 4, c1 - c0], F32, place)
            nc.sync.dma_start(raw[:], w1[:, c0:c1].rearrange("(p j) c -> p j c", j=4))
            return raw

        w4w_raw = [keep.tile([P, H], U8, name=f"w4w_raw{b}", align_bytes=64) for b in range(2)]

        def load_w4_words(b):
            nc.sync.dma_start(w4w_raw[b][:].bitcast(I32), w4_words[0][:, H * b : H * (b + 1)].bitcast(I32))

        nc.sync.dma_start(offs_t[:], offs)
        load_w4_words(0)
        nc.sync.dma_start(bg_t[0][:], bg[0:512].rearrange("(p t) -> p t", t=4))
        for r in range(4):
            nc.sync.dma_start(tab_sc[r:P:32, :].bitcast(I32), tab_scales[0, r:16:4, :].bitcast(I32))
        tab_w = laid([P, T], I32, "table")
        nc.sync.dma_start(tab_w[:], tab_words[0].rearrange("p t i -> p (t i)").bitcast(I32))
        for r in range(4):
            nc.sync.dma_start(w4s_raw[r:P:32, :].bitcast(I32), w4_scales[0, r:16:4, :].bitcast(I32))
        w1_raw0 = load_w1("w1_raw0", 0, 512)
        wgs_t = keep.tile([P, S], F32, name="wgs_t")
        for half in HALVES:
            nc.sync.dma_start(wgs_t[:, half], wgs[:, half])
        nc.sync.dma_start(offs2_t[:], offs2)
        w1_raw1 = load_w1("w1_raw1", 512, 1024)
        load_w4_words(1)
        nc.sync.dma_start(bg_t[1][:], bg[512:1024].rearrange("(p t) -> p t", t=4))
        nc.sync.dma_start(amb_t[:], amb.rearrange("(b p t) -> p b t", b=2, t=4))

        def round_w1(rounded, raw, m0, t0, t1, cast=nc.scalar.copy):
            src = raw[:].rearrange("p j (m t) -> p m j t", t=4)
            dst = rounded.rearrange("p (t m j) -> p m j t", m=P, j=4)
            cast(dst[:, m0 : m0 + src.shape[1], :, :], src[:, :, :, t0:t1])

        rounded = {0: laid([P, 8 * P], BF16, "rounded01")[:], 2: laid([P, 8 * P], BF16, "rounded23")[:]}

        got_w = [keep.tile([P, BANK], U32, name=f"got_w{h}", align_bytes=64) for h in range(2)]
        got_s = [keep.tile([P, BANK], U8, name=f"got_s{h}", align_bytes=64) for h in range(2)]
        list_cols = [slice(BANK // GROUP * h, BANK // GROUP * (h + 1)) for h in range(2)]
        for h in range(2):
            nc.vector.tensor_copy(got_s[h][:], tab_sc[:].indirect(offs_t[:, list_cols[h]]))
        for h in range(2):
            nc.vector.tensor_copy(got_w[h][:], tab_w[:].bitcast(U32).indirect(offs_t[:, list_cols[h]]))

        w4w = [keep.tile([P, H], U8, name=f"w4w{b}", align_bytes=64) for b in range(2)]
        w4s = [keep.tile([P, 4, P], U8, name=f"w4s{b}", align_bytes=64) for b in range(2)]

        def deal_w4_words(b):
            nc.scalar.copy(
                w4w[b][:].bitcast(U16).rearrange("p (t m) -> p t m", t=4),
                w4w_raw[b][:].bitcast(U16).rearrange("p (m t) -> p t m", t=4),
            )

        deal_w4_words(0)
        for b in range(2):
            nc.gpsimd.tensor_copy(w4s[b][:], w4s_raw[:, BANK * b : BANK * (b + 1)].rearrange("p (m t) -> p t m", t=4))

        expo_t = {}

        def load_expo(j):
            b, u = divmod(j, 2)
            rows = expo[512 * b : 512 * (b + 1), :].rearrange("(p t) m -> p t m", t=4)[:, 2 * u : 2 * u + 2, :]
            if j < 3:
                expo_t[j] = laid([P, 2, T2], F32, f"expo{2 * j}{2 * j + 1}")
                nc.sync.dma_start(expo_t[j][:], rows)
            else:
                expo_t[j] = []
                for m0 in range(0, T2, PIECE):
                    expo_t[j].append(laid([P, 2, PIECE], F32, "expo67", name=f"expo67_{m0}", plus=8 * m0))
                    nc.sync.dma_start(expo_t[j][-1][:], rows[:, :, m0 : m0 + PIECE])

        for j in range(2):
            load_expo(j)
        w1_scales = [keep.tile([P, 4 * P], U8, name=f"w1_scales{b}", align_bytes=64) for b in range(2)]
        w1_codes = {k: keep.tile([P, 2 * P], U32, name=f"w1_codes{k}", align_bytes=64) for k in (0, 2)}

        def quantise(codes, scales, values):
            nc.vector.quantize_mx(out=codes.bitcast(FP8X4), scales=scales, in_=values)

        def product(acc, lhs, lhs_scale, rhs, rhs_scale, start=True, stop=True):
            nc.tensor.matmul_mx(out=acc, lhsT=lhs, lhsT_scale=lhs_scale, rhs=rhs, rhs_scale=rhs_scale, start=start, stop=stop)

        def trust(k, h, sigmoid):
            b, t = divmod(k, 4)
            acc = ring_bank([P, BANK], "acc_b")
            lhs = w4w[b][:, 2 * P * t : 2 * P * (t + 1)].bitcast(FP4X4)
            product(acc[:], lhs, w4s[b][:, t, :], got_w[h][:].bitcast(FP8X4), got_s[h][:])
            nc.scalar.activation(sigmoid, acc[:], ACT.Sigmoid, bias=bg_t[b][:, t : t + 1])

        def deviation(k, h, acc):
            lhs = w1_codes[k - k % 2][:, P * (k % 2) : P * (k % 2 + 1)].bitcast(FP8X4)
            product(acc[:], lhs, w1_scales[0][:, P * k : P * (k + 1)], got_w[h][:].bitcast(FP8X4), got_s[h][:])
            return acc

        val = {}

        def place(k):
            nc.vector.tensor_copy(pages[k % 2][:].indirect(offs2_t[:]), val[k])

        def gate(k, halves=(0, 1)):
            if k not in val:
                val[k] = laid([P, S], F32, f"val{k}")[:]
            for h in halves:
                trust(k, h, val[k][:, HALVES[h]])

        wgs_turned = keep.tile([P, S // P, 8], F32, name="wgs_turned")

        def turn_wgs():
            for h in range(2):
                bank = ring_bank([P, 4, P], "wgs_bank")
                for q in range(4):
                    nc.tensor.transpose(bank[:, q, :], wgs_t[:, BANK * h + P * q : BANK * h + P * (q + 1)], ident[:])
                nc.scalar.copy(wgs_turned[:, 4 * h : 4 * h + 4, :], bank[:, :, 0:P:GROUP])

        val0_first = keep.tile([P, BANK], F32, name="val0_first")
        trust(0, 0, val0_first[:])
        round_w1(rounded[0], w1_raw0, 0, 0, 2, nc.vector.tensor_copy)
        round_w1(rounded[2], w1_raw0, 0, 2, 4)
        sigmoid1_first = laid([P, BANK], F32, "sigmoid1_first")
        trust(1, 0, sigmoid1_first[:])
        quantise(w1_codes[0][:], w1_scales[0][:, 0 : 2 * P], rounded[0])
        first_factor = deviation(0, 0, psum.tile([P, BANK], F32, name="acc_v0", tag="bank4"))
        nc.vector.tensor_tensor(val0_first[:], val0_first[:], wgs_t[:, HALVES[0]], MULT)
        quantise(w1_codes[2][:], w1_scales[0][:, 2 * P : 4 * P], rounded[2])
        nc.vector.tensor_tensor(val0_first[:], val0_first[:], first_factor[:], MULT)
        nc.vector.tensor_copy(pages[0][:].indirect(offs2_t[:, list_cols[0]]), val0_first[:])

        def weigh(dst, src, h):
            nc.gpsimd.tensor_tensor(dst, src, wgs_t[:, HALVES[h]], MULT)

        def finish_half(k, h, values, place_of_copy):
            copied = laid([P, BANK], F32, place_of_copy)
            nc.scalar.copy(copied[:], deviation(k, h, ring_bank([P, BANK], "acc_a"))[:])
            nc.gpsimd.tensor_tensor(values, values, copied[:], MULT)

        def place_half(k, h, values):
            nc.vector.tensor_copy(pages[k][:].indirect(offs2_t[:, list_cols[h]]), values)

        val1_first = laid([P, BANK], F32, "val1_first")[:]
        weigh(val1_first, sigmoid1_first[:], 0)
        finish_half(1, 0, val1_first, "copied1_first")
        place_half(1, 0, val1_first)
        val0_second = laid([P, BANK], F32, "val0_second")[:]
        trust(0, 1, val0_second)
        weigh(val0_second, val0_second, 1)
        finish_half(0, 1, val0_second, "copied0_second")
        place_half(0, 1, val0_second)
        val1_second = laid([P, BANK], F32, "val1_second")[:]
        trust(1, 1, val1_second)
        weigh(val1_second, val1_second, 1)
        gate(2)
        nc.gpsimd.tensor_tensor(val[2], val[2], wgs_t[:], MULT)
        rounded47 = laid([P, 16 * P], BF16, "rounded47")
        round_w1(rounded47[:], w1_raw1, 0, 0, 4)
        finish_half(1, 1, val1_second, "copied1_second")
        copied2 = laid([P, S], F32, "copied2")
        for h in range(2):
            nc.scalar.copy(copied2[:, HALVES[h]], deviation(2, h, ring_bank([P, BANK], "acc_a"))[:])
        gate(3)
        codes47 = laid([P, 4 * P], U32, "codes47")
        quantise(codes47[:], w1_scales[1][:], rounded47[:])
        place_half(1, 1, val1_second)
        weighed2 = val[2]
        val[2] = laid([P, S], F32, "val2_done")[:]
        nc.gpsimd.tensor_tensor(val[2], weighed2, copied2[:], MULT)

        levels = laid([P, 4 * T2], F32, "levels")
        words = [laid([P, 2 * T2], F32, f"words{b}") for b in range(2)]

        def level_of(k):
            slot = LEVEL_SLOT[k]
            return levels[:, T2 * slot : T2 * (slot + 1)]

        def level(k, cols=slice(0, T2)):
            b, t = divmod(k, 4)
            nc.scalar.activation(level_of(k)[:, cols], pages[k % 2][:, cols], ACT.Identity, bias=amb_t[:, b, t : t + 1])

        def pair_words(j, cols):
            at = T2 * (j % 2)
            return words[j // 2][:, at + cols.start : at + cols.stop].bitcast(BF16)

        def expose(j, cols):
            expose_pair(nc.gpsimd, j, expo_t[j][:, :, cols], cols)

        def expose_pair(engine, j, pair_expo, cols):
            first, second = LEVEL_SLOT[2 * j], LEVEL_SLOT[2 * j + 1]
            pair_levels = levels[:].rearrange("p (s m) -> p s m", s=4)[:, first : second + 1 : second - first, :]
            engine.tensor_tensor(
                pair_words(j, cols).rearrange("p (c i t) -> p c t i", i=4, t=2),
                pair_levels[:, :, cols].rearrange("p t (c i) -> p c t i", i=4),
                pair_expo.rearrange("p t (c i) -> p c t i", i=4),
                MULT,
            )

        def both_pairs(b, cols):
            return words[b][:].rearrange("p (u m) -> p u m", u=2)[:, :, cols].rearrange("p u (c i) -> p c u i", i=4)

        weighed = [laid([P, 4, P], F32, "weighed", name=f"weighed{e}", plus=2 * KIB * e) for e in range(S // P)]

        def weigh_transposed(e):
            h, q = divmod(e, 4)
            acc = ring_bank([P, 4, P], "acc_t")
            lhs = got_w[h][:, P * q : P * (q + 1)].bitcast(FP8X4)
            lhs_scale = got_s[h][:, P * q : P * (q + 1)]
            product(acc[:].rearrange("p t m -> p (t m)"), lhs, lhs_scale, codes47[:].bitcast(FP8X4), w1_scales[1][:])
            for g in range(8):
                run = slice(GROUP * g, GROUP * (g + 1))
                nc.scalar.activation(weighed[e][:, :, run], acc[:, :, run], ACT.Copy, scale=wgs_turned[:, e, g : g + 1])

        def turned_back(k, h, acc):
            for q in range(4):
                nc.tensor.transpose(acc[:, P * q : P * (q + 1)], weighed[4 * h + q][:, k - 4, :], ident[:])
            return acc

        copied_on = {
            3: words[0][:, 0:S],
            4: words[0][:, FIRST_PART : FIRST_PART + BANK],
            5: words[1][:, 0:S],
            6: words[0][:, T2 : T2 + S],
            7: words[1][:, S:T2],
        }

        def copy_factor(k, halves=(0, 1)):
            factor = deviation if k < 4 else turned_back
            for h in halves:
                nc.scalar.copy(copied_on[k][:, HALVES[h]], factor(k, h, ring_bank([P, BANK], "acc_a"))[:])

        def times_factor(k):
            nc.gpsimd.tensor_tensor(val[k], val[k], copied_on[k], MULT)

        copy_factor(3)
        turn_wgs()
        deal_w4_words(1)
        level(0)
        gate(4)
        nc.gpsimd.tensor_tensor(val[3], val[3], wgs_t[:], MULT)
        times_factor(3)
        weigh_transposed(0)
        place(2)
        level(1)
        expose(0, slice(0, FIRST_PART))
        for e in range(1, 4):
            weigh_transposed(e)
        copy_factor(4, (0,))
        for e in range(4, 8):
            weigh_transposed(e)
        place(3)

        w8w = keep.tile([P, 2, N], I32, name="w8w", align_bytes=64)
        nc.sync.dma_start(w8w[:], w8_words.rearrange("a p c i -> p a (c i)").bitcast(I32))
        w8s = w1_scales[0]
        for quad in range(4):
            nc.sync.dma_start(
                w8s[32 * quad + 4 : 32 * quad + 12, 0:N].bitcast(I32),
                w8_scales[:, 4 * quad : 4 * quad + 4, :].bitcast(I32),
            )

        nc.gpsimd.tensor_tensor(val[4][:, HALVES[0]], val[4][:, HALVES[0]], copied_on[4], MULT)
        second_factor = turned_back(4, 1, psum.tile([P, BANK], F32, name="acc_v4", tag="bank4"))
        nc.vector.tensor_tensor(val[4][:, HALVES[1]], val[4][:, HALVES[1]], second_factor[:], MULT)
        level(2)
        place(4)
        expose(0, slice(FIRST_PART, T2))
        load_expo(2)
        gate(5)
        copy_factor(5)
        times_factor(5)
        gate(6)
        copy_factor(6)
        times_factor(6)
        level(3)
        place(5)
        expose(1, slice(0, T2))
        load_expo(3)
        gate(7)
        copy_factor(7)
        level(4)
        place(6)
        times_factor(7)
        level(5)
        woven0 = laid([P, T2, 2], F32, "woven0")
        for c in range(T2 // BANK):
            cols = slice(BANK * c, BANK * (c + 1))
            nc.scalar.copy(woven0[:, cols, :].rearrange("p (c i) u -> p c u i", i=4), both_pairs(0, cols))
        level(6)
        place(7)
        expose(2, slice(0, T2))

        z_codes1 = laid([P, T2], U32, "z_codes1")
        z_scales = [laid([P, T2], U8, "z_scales0"), keep.tile([P, T2], U8, name="z_scales1", tag="z_scales1", align_bytes=64)]
        woven1 = {}
        accs = {}
        tail_turns = []

        def cols_of(i):
            return slice(PIECE * i, PIECE * (i + 1))

        def multiply(b, i, codes):
            for nb in range(N // P):
                if b == 0:
                    tail_turns.append(len(tail_turns) % 8)
                    accs[i, nb] = psum.tile([P, PIECE], F32, name="acc_o", tag=f"bank{tail_turns[-1]}")
                lhs = w8w[:, b, P * nb : P * (nb + 1)].bitcast(FP8X4)
                lhs_scale = w8s[4 * (b + 1) : P, P * nb : P * (nb + 1)]
                product(accs[i, nb][:], lhs, lhs_scale, codes.bitcast(FP8X4), z_scales[b][:, cols_of(i)], b == 0, b == 1)

        def first_pass(i):
            if i < 2:
                codes = laid([P, PIECE], U32, "z_codes0", name=f"z_codes0_{i}", plus=4 * PIECE * i)
            else:
                codes = laid([P, PIECE], U32, "expo67", name=f"z_codes0_{i}", plus=8 * PIECE * (i - 2))
            values = woven0[:, cols_of(i), :].rearrange("p m u -> p (m u)").bitcast(BF16)
            quantise(codes[:], z_scales[0][:, cols_of(i)], values)
            multiply(0, i, codes[:])

        def second_pass(i):
            values = woven1[i][:].rearrange("p m u -> p (m u)").bitcast(BF16)
            quantise(z_codes1[:, cols_of(i)], z_scales[1][:, cols_of(i)], values)
            multiply(1, i, z_codes1[:, cols_of(i)])

        def weave(i, copy):
            woven1[i] = laid([P, PIECE, 2], F32, "woven1", name=f"woven1_{i}", plus=8 * PIECE * (i % 4))
            copy(woven1[i][:].rearrange("p (c i) u -> p c u i", i=4), both_pairs(1, cols_of(i)))

        def store(i, on_vector):
            room, slot = ("results_early", i) if i < 5 else ("results_late", i - 5)
            for nb in range(N // P):
                res = laid([P, PIECE], F32, room, name=f"res{i}_{nb}", plus=4 * PIECE * (3 * slot + nb))
                copy = nc.vector.tensor_copy if nb in on_vector else nc.scalar.copy
                copy(res[:], accs[i, nb][:])
                nc.sync.dma_start(out[P * nb : P * (nb + 1), cols_of(i)], res[:])

        for i in range(PIECES):
            level(7, cols_of(i))
            if i >= 2:
                second_pass(i - 2)
            if i - 1 >= SCALAR_WEAVES:
                weave(i - 1, nc.vector.tensor_copy)
            if i < PIECES - 1:
                first_pass(i)
            expose_pair(nc.vector, 3, expo_t[3][i][:], cols_of(i))
            if i >= 2:
                store(i - 2, ())
            if i < SCALAR_WEAVES:
                weave(i, nc.scalar.copy)
        second_pass(PIECES - 2)
        weave(PIECES - 1, nc.vector.tensor_copy)
        first_pass(PIECES - 1)
        second_pass(PIECES - 1)
        for i in range(PIECES - 2, PIECES):
            store(i, (1, 2))
